import numpy as np, ml_dtypes
CORES = [6,15,38,47]
N = 4
import mx_ref
BF = ml_dtypes.bfloat16
def gentries(a):
    return np.ascontiguousarray(a.reshape(8, 16, -1).transpose(0, 2, 1)).reshape(8, -1)
def gtable(e):
    e = np.asarray(e); return np.ascontiguousarray(e.reshape(8, -1, 16).transpose(0, 2, 1)).reshape(128, -1).astype(np.int32)
def gcols(t, e):
    v = np.concatenate([t.reshape(8, 16, -1, 4), np.zeros((8, 16, 1, 4), BF)], axis=2)
    return np.ascontiguousarray(np.stack([v[g][:, e[g]] for g in range(8)])).reshape(128, -1)
def tile(rs):
    return np.stack(rs, axis=2).reshape(128, -1).astype(BF)
def cut(t, i, w=512):
    return t[:, w * i:w * i + w]
def pick(q, e):
    c = np.concatenate([q[0].reshape(128, -1, 4), np.zeros((128, 1, 4), np.uint8)], axis=1); s = np.concatenate([q[1], np.ones((16, 1), np.uint8)], axis=1)
    return (np.ascontiguousarray(c[:, e].reshape(128, -1)), np.ascontiguousarray(s[:, e]))
def join(*qs):
    return (np.concatenate([q[0] for q in qs], axis=1), np.concatenate([q[1] for q in qs], axis=1))
def put(q, e, v):
    c, s = q[0].reshape(128, -1, 4).copy(), q[1].copy(); c[:, e] = v[0].reshape(128, -1, 4); s[:, e] = v[1]
    return (c.reshape(128, -1), s)
def pk(c, s):
    return (np.ascontiguousarray(c), mx_ref.live(s))
def emit(q):
    return q[0], q[1]
def packed(v, rng):
    q = [mx_ref.quantize(np.ascontiguousarray(v[r])) for r in range(N)]
    return np.stack([a for a, b in q]), np.stack([mx_ref.plane(b, rng) for a, b in q])
def values_of_codes():
    e, c = np.zeros((128, 128, 4), np.float32), np.zeros((128, 2, 4), np.uint8)
    e[np.arange(128), np.arange(128), 0] = 1
    c[:127, :, 0] = np.arange(256).reshape(2, 128).T[:127]
    return mx_ref.matmul(mx_ref.quantize(e.reshape(128, 512).astype(BF)), (c.reshape(128, 8), np.full((16, 2), 127, np.uint8))).T.reshape(-1).astype(np.float64)
CODE_VALUE, SCALE_VALUE = values_of_codes(), 2.0 ** (np.arange(256) - 127.0)
def decode(q):
    return (CODE_VALUE[q[0]].reshape(16, 8, -1, 4) * SCALE_VALUE[q[1]][:, None, :, None] + 0.0).reshape(128, -1).astype(np.float32)
def f(rng, *shape):
    return mx_ref.flush((rng.standard_normal(shape, dtype=np.float32) * np.exp2(rng.integers(-2, 3, shape[:-1] + (1,)))).astype(BF))
def wide(rng, *shape, cols=0):
    v = rng.standard_normal(shape, dtype=np.float32) * np.exp2(rng.integers(-12, 13, shape)).astype(np.float32)
    if cols: v *= np.repeat(np.exp2(rng.integers(-cols, cols + 1, shape[:-2] + (1, shape[-1] // 4))) * (rng.random(shape[:-2] + (1, shape[-1] // 4)) > 0.0625), 4, axis=-1).astype(np.float32)
    return mx_ref.flush(v.astype(BF))
C, V, L, K, R = 384, 3, 5, 96, 3
def order(s, names):
    by = np.argsort(np.argsort(-s, axis=1, kind="stable"), axis=1)
    place = np.where(by == 0, 0, C)
    for t in range(L):
        first = np.min(np.take_along_axis(place, names.reshape(8, -1), axis=1).reshape(8, C, V), axis=2)
        new = (place == C) & (first < C)
        key = np.where(new, first * C + by, C * C)
        n = np.sum(place < C, axis=1)
        place = np.where(new, n[:, None] + np.argsort(np.argsort(key, axis=1, kind="stable"), axis=1), place)
    return np.argsort(place, axis=1, kind="stable")
def big(v):
    v = v.astype(np.float32)
    v[np.abs(v) < np.float32(2.0 ** -16)] = 0
    return v.astype(BF)
def numbers_of(rng):
    return {"x": big(f(rng, N, 128, 4 * C)), "u": np.array(f(rng, N, 128, 512)), "v": np.array(f(rng, N, 128, 512))}
def names_of(rng):
    return rng.integers(0, C, (N, 8, C, V))
def stored(l):
    return {"nb": np.stack([gtable(e.reshape(8, -1)) for e in l])}
def weights(rng, w):
    c, p = packed(w, rng)
    return {"wc": c, "ws": p}
def still(rng):
    w = np.zeros((N, 128, 4, 128, 4), np.float32)
    i = np.arange(128)
    for b in range(4): w[:, i, b, i, b] = 32
    return weights(rng, w.reshape(N, 128, 2048).astype(BF))
def signs(rng):
    return np.stack([rng.permutation(8) % 2 * 2.0 - 1.0 for r in range(N)])
def setup_inputs(rng):
    return {**numbers_of(rng), **stored(names_of(rng)), **weights(rng, f(rng, N, 128, 2048))}
def setup_inputs_ties(rng):
    d = numbers_of(rng)
    e = rng.permutation(N)
    x = d["x"].reshape(N, 8, 16, C, 4)
    for r in range(N):
        k = np.zeros(C, int) if r == e[0] else rng.permutation(C) % 3
        a = x[r][:, :8, :3].copy()
        a[:, :, 2] = 0
        x[r][:, :8] = a[:, :, k]
    x[e[1]] = 0
    u = d["u"].reshape(N, 8, 16, 128, 4)
    u[:, :, 8:, ::16] = 0
    w = np.array(f(rng, N, 128, 2048)).reshape(N, 8, 16, 4, 8, 16, 4)
    w[:, :, 8:, :, :, :8] = 0
    return {"x": x.reshape(N, 128, 4 * C), "u": u.reshape(N, 128, 512), "v": d["v"], **stored(names_of(rng)), **weights(rng, w.reshape(N, 128, 2048))}
def setup_inputs_near(rng):
    d, l = numbers_of(rng), names_of(rng)
    x = d["x"].astype(np.float32).reshape(N, 8, 16, C, 4)
    s = np.arange(C) // 2
    g = ((s[:, None] >> np.arange(8)) & 1) * np.exp2(np.arange(8) - 23.0)
    x[:, :, 0] = 0
    x[:, :, 0, :, 0] = 1
    x[:, :, 8] = g[:, :4]
    x[:, :, 9] = g[:, 4:]
    x[:, :, 10:] = rng.integers(4, 8, (N, 8, 6, C, 4)) * rng.choice([-1.0, 1.0], (N, 8, 6, C, 4)) * 2.0 ** -20
    u = d["u"].reshape(N, 128, 128, 4)
    k = np.where(rng.permutation(N) < N // 2, 2.0 ** -30, 1.0)
    a = k[:, None] * signs(rng)
    a[np.ix_(np.flatnonzero(k < 1), rng.permutation(8)[:2])] = 0
    a = a.astype(np.float32).astype(BF)
    k = k.astype(np.float32).astype(BF)
    u[:, :, ::16] = 0
    for h in range(0, 128, 16):
        u[:, h, h, 0] = a[:, h // 16]
        u[:, h + 8:h + 10, h] = k[:, None, None]
    l[:, :, :C // 4, 0] = C - 2
    l[:, :, 1::2] = l[:, :, ::2]
    return {"x": x.reshape(N, 128, 4 * C).astype(BF), "u": u.reshape(N, 128, 512), "v": d["v"], **stored(l), **still(rng)}
def setup_inputs_huge(rng):
    d = numbers_of(rng)
    x = 2.0 ** 30 * (0.6 + 0.4 * rng.random((N, 128, C, 4)))
    c = np.stack([rng.permutation(C) % 2 * 2.0 - 1.0 for r in range(N)])
    c[rng.permutation(N) < N // 2] = 1
    x *= c[:, None, :, None]
    u = d["u"].reshape(N, 128, 128, 4)
    a = 2.0 ** 30 * (1 - 0.25 * rng.random((N, 128, 8, 4))) * signs(rng)[:, None, :, None]
    u[:, :, ::16] = a.astype(np.float32).astype(BF)
    return {"x": x.astype(np.float32).reshape(N, 128, 4 * C).astype(BF), "u": u.reshape(N, 128, 512), "v": d["v"], **stored(names_of(rng)), **still(rng)}
def setup_inputs_graphs(rng):
    d, l = numbers_of(rng), names_of(rng)
    o = rng.permutation(N)
    x = d["x"].reshape(N, 8, 16, C, 4)
    u = d["u"].reshape(N, 128, 128, 4)
    u[:, ::16, ::16, 0] = np.eye(8, dtype=np.float32).astype(BF)
    for r in range(N):
        for g in range(8):
            e = rng.permutation(C)
            x[r, g, 0, e[0], 0] = 16384
            if o[r] % 4 == 0: l[r, g] = np.arange(C)[:, None]
            if o[r] % 4 == 1: l[r, g] = e[0]
            if o[r] % 4 == 2: l[r, g, e] = np.roll(e, 1)[:, None]
            if o[r] % 4 == 3:
                m = L if g % 2 else 2
                l[r, g] = e[m - 1 + rng.integers(0, 2, (C, V))]
                l[r, g, e[m - 1:m + 1]] = e[m - 2]
                for j in range(1, m - 1): l[r, g, e[j]] = e[j - 1]
    return {"x": x.reshape(N, 128, 4 * C), "u": u.reshape(N, 128, 512), "v": d["v"], **stored(l), **weights(rng, f(rng, N, 128, 2048))}
def setup_inputs_spread(rng):
    d = setup_inputs(rng)
    d["x"] = big(wide(rng, N, 128, 4 * C, cols=6))
    return d
def check_inputs(d):
    b = []
    for k in ("x", "u", "v"):
        a = np.abs(d[k].astype(np.float32))
        if not (np.isfinite(a).all() and ((a == 0) | (a >= 2.0 ** -30) & (a <= 2.0 ** 30)).all()): b.append("a value of " + k)
    if ((d["nb"] < 0) | (d["nb"] >= C)).any(): b.append("an entry of nb")
    if (d["wc"] % 128 == 127).any(): b.append("wc: a code that is no number")
    for r in range(N):
        a = np.abs(decode(pk(d["wc"][r], d["ws"][r])))
        if not ((a == 0) | (a >= 2.0 ** -30) & (a <= 2.0 ** 30)).all(): b.append("a number that wc and ws stand for")
    return b
def reference(x, u, v, nb, wc, ws):
    qu = [mx_ref.quantize(u[r]) for r in range(N)]
    lay = [pk(wc[r], ws[r]) for r in range(N)]
    now = [x[r] for r in range(N)]
    names = [gentries(nb[r]).astype(np.int64).reshape(8, C, V) for r in range(N)]
    for t in range(R):
        sent = []
        for r in range(N):
            p = mx_ref.matmul(qu[r], mx_ref.quantize(now[r]))
            l = order(p[::16] + np.float32(0.0), names[r])[:, ::-1]
            i = np.argsort(l, axis=1)
            sent.append(mx_ref.quantize(gcols(now[r], l)))
            e = np.take_along_axis(names[r], l[:, :, None], axis=1).reshape(8, -1)
            names[r] = np.take_along_axis(i, e, axis=1).reshape(8, C, V)
        came = decode(join(*sent))
        for r in range(N):
            e = np.concatenate([cut(came, (r + N - 1) % N, 4 * C)[:, 4 * (C - K):], cut(came, r, 4 * C)], axis=1)
            q = mx_ref.quantize(np.ascontiguousarray(((e[:, 4 * K:] + e[:, :4 * C]) * np.float32(0.5)).astype(BF)))
            now[r] = tile([np.maximum(mx_ref.matmul(pick(lay[r], np.arange(128 * b, 128 * b + 128)), q), np.float32(0.0)) * np.float32(0.03125) for b in range(4)])
    y, on = np.zeros((N, 128, C), np.float32), np.zeros((N, 8, V * C), np.float32)
    oc, osc = np.zeros((N, 128, 4 * C), np.uint8), np.zeros((N, 16, C), np.uint8)
    for r in range(N):
        q = mx_ref.quantize(now[r])
        y[r] = mx_ref.matmul(mx_ref.quantize(v[r]), q)
        on[r] = names[r].reshape(8, -1)
        oc[r], osc[r] = emit(q)
    return {"y": y, "on": on, "oc": oc, "osc": osc}

@@ -1,0 +1,496 @@
+from concourse.mybir import dt, AluOpType, AxisListType, ActivationFunctionType
+
+C, K, R = 384, 96, 3
+NSA = 4
+NVA = 24 - NSA
+NVB, NVC = 9, 10
+PIECES = ((0, 160), (160, 288), (288, C))
+C3 = 3 * C
+SH, HUGE, CB = 12.0 * 2 ** 20, 2.0 ** 25, 2048.0
+F32, BF, I32, U16, Q4, U8 = "float32", "bfloat16", "int32", "uint16", "float8_e4m3fn_x4", "uint8"
+
+
+def _sb(n, d=F32):
+    return ("sbuf", [128, n], d)
+
+
+SCRATCH = {
+    "xb": _sb(4 * C, BF), "tb": _sb(512, BF), "zb": _sb(4 * C, BF), "ub": _sb(512, BF), "vb": _sb(512, BF),
+    "dh": _sb(4 * C), "eh": _sb(4 * C),
+    "nbi": _sb(72, I32), "nbo": _sb(72, U16), "nof": _sb(96, U16), "nx": _sb(24, U16), "nf0": _sb(24), "nf1": _sb(24),
+    "nbv": _sb(C3), "vn": _sb(C3), "nsc": _sb(C3),
+    "qx": _sb(C, Q4), "sx": _sb(C, U8), "qz": _sb(C, Q4), "sz": _sb(C, U8),
+    "qu": _sb(128, Q4), "su": _sb(128, U8), "qu2": _sb(128, Q4), "su2": _sb(128, U8), "qv": _sb(128, Q4), "sv": _sb(128, U8),
+    "qw": _sb(512, Q4), "sw": _sb(512, U8), "qe": _sb(512, Q4), "se": _sb(512, U8), "eb": _sb(2048, BF),
+    "one5": _sb(512, BF), "half": _sb(512, BF), "gd": _sb(512, BF), "gd2": _sb(512, BF), "qg": _sb(128, Q4), "sgs": _sb(128, U8),
+    "ct": _sb(3072, BF), "qc": _sb(768, Q4), "scc": _sb(768, U8), "csc": _sb(256),
+    "pmi": _sb(2, I32), "pmj": _sb(2, I32), "pm": _sb(2), "uoi": _sb(8, I32), "uo": _sb(8, U16), "po": _sb(24, U16),
+    "iot": _sb(C), "io3": _sb(C), "io4": _sb(C), "rj": _sb(C), "wz": _sb(2 * C), "tm": _sb(C), "md": _sb(C),
+    "rch": _sb(C, BF), "rdi": _sb(C, BF), "madd": _sb(C), "mmul": _sb(C),
+    "s16": _sb(96), "cc": _sb(8), "cst": _sb(24), "fl": _sb(96), "fl2": _sb(48), "fl3": _sb(24), "fl4": _sb(24),
+    "t1": _sb(C), "t2": _sb(C), "cm": _sb(C), "eq": _sb(C, BF), "cor": _sb(C, BF),
+    "fw": _sb(4 * C, BF), "ce": _sb(7 * C), "wa": _sb(C3 + 8), "wb": _sb(C3 + 8), "gi": _sb(C3), "kc": _sb(C3),
+    "ca": _sb(C3), "cb": _sb(C3), "key": _sb(C), "ksc": _sb(C),
+    "cmp": _sb(10 * C, BF), "scn": _sb(10 * C, BF), "sg": _sb(16 * C, BF), "jk": _sb(C, BF),
+    "col": _sb(16), "acc": _sb(24), "alt": _sb(24), "agt": _sb(24), "rw": _sb(24), "bas": _sb(24), "byw": _sb(24),
+    "o1": _sb(24, U16), "o1b": _sb(24, U16), "o2": _sb(24, U16), "o3": _sb(24, U16), "oc2": _sb(24, U16), "lo": _sb(56, U16),
+    "lb": _sb(C), "lsc": _sb(C), "colb": _sb(C3), "yb": _sb(C),
+    "ps": ("psum", [128, 4096], F32),
+}
+for _r in range(R):
+    SCRATCH["qt%d" % _r] = _sb(K + 128, Q4)
+    SCRATCH["st%d" % _r] = _sb(K + 128, U8)
+
+POOL = {"V": 44, "S": 36, "P": 16, "G": 20, "D": 16}
+SEMAPHORES = [q + str(i) for q in POOL for i in range(POOL[q])] + ["arr%d" % r for r in range(R)] + ["sent"]
+
+
+def rank_program(g, core, T, topo):
+    rank = T.rank_of(core)
+    if rank is None:
+        return
+    nxt = T.cores[(rank + 1) % len(T.cores)]
+    rid, pid = topo.addr(nxt)[0:2]
+    emask = topo.mask(core, nxt)
+    neng = len(topo.engines(core, nxt))
+    alu, act = AluOpType, ActivationFunctionType
+    eng = {"V": g.vector, "S": g.scalar, "P": g.tensor, "G": g, "Y": g.sync}
+    ops = []
+
+    def A(name, a=0, b=None, s=1):
+        if b is None:
+            b = SCRATCH[name][1][1]
+        if name == "ps":
+            return (T[name][:, a:b], [("ps", 1 << (a // 512))])
+        m = ((1 << (b - a)) - 1) << a if s == 1 else sum(1 << c for c in range(a, b, s))
+        return (T[name][:, a:b] if s == 1 else T[name][:, a:b:s], [(name, m)])
+
+    def col(name, c):
+        return A(name, c, c + 1)
+
+    def I(win, off):
+        return (win[0].indirect(off[0]), win[1], off[1])
+
+    def bits(a, d):
+        return (a[0].bitcast(d), a[1])
+
+    def ap(x):
+        return x[0] if isinstance(x, tuple) else x
+
+    def add(q, fn, outs, ins, grp=None, dma=False, pre=None, chain=False):
+        rd, wr = [], []
+        for x in ins:
+            if isinstance(x, tuple):
+                rd += x[1] + (x[2] if len(x) > 2 else [])
+        for x in outs:
+            wr += x[1]
+            rd += x[2] if len(x) > 2 else []
+        ops.append({"q": q, "fn": fn, "rd": rd, "wr": wr, "grp": grp if grp else "#%d" % len(ops), "dma": dma, "pre": pre, "chain": chain})
+
+    def ts(o, i, s1, op0, s2=None, op1=None, grp=None):
+        if op1 is None:
+            add("V", lambda: g.vector.tensor_scalar(o[0], i[0], ap(s1), None, op0), [o], [i, s1], grp)
+        else:
+            add("V", lambda: g.vector.tensor_scalar(o[0], i[0], ap(s1), ap(s2), op0, op1), [o], [i, s1, s2], grp)
+
+    def tt(o, a, b, op, grp=None):
+        add("V", lambda: g.vector.tensor_tensor(o[0], a[0], b[0], op), [o], [a, b], grp)
+
+    def cp(o, i, grp=None):
+        add("V", lambda: g.vector.tensor_copy(o[0], i[0]), [o], [i], grp)
+
+    def scan(o, d0, d1, init, op0, op1, grp=None):
+        add("V", lambda: g.vector.tensor_tensor_scan(o[0], d0[0], d1[0], init, op0, op1), [o], [d0, d1], grp)
+
+    def fill(o, v, grp=None):
+        add("V", lambda: g.vector.memset(o[0], v), [o], [], grp)
+
+    def quant(q, s, i):
+        add("V", lambda: g.vector.quantize_mx(q[0], s[0], i[0]), [q, s], [i])
+
+    def sa(o, i, f, bias=0.0, scale=1.0, acc=None, grp=None):
+        if acc is None:
+            add("S", lambda: g.scalar.activation(o[0], i[0], f, bias=ap(bias), scale=ap(scale)), [o], [i, bias, scale], grp)
+        else:
+            add("S", lambda: g.scalar.activation(o[0], i[0], f, bias=ap(bias), scale=ap(scale), accum_out=acc[0]), [o, acc], [i, bias, scale], grp)
+
+    def sc(o, i, grp=None):
+        add("S", lambda: g.scalar.activation(o[0], i[0], act.Copy), [o], [i], grp)
+
+    def mm(bank, n, wq, ws, c0, xq, xs, x0, start=True, stop=True, grp=None, pre=None):
+        o, a, b = A("ps", 512 * bank, 512 * bank + n), A(wq, c0, c0 + 128), A(ws, c0, c0 + 128)
+        c, d = A(xq, x0, x0 + n), A(xs, x0, x0 + n)
+        add("P", lambda: g.tensor.matmul_mx(o[0], a[0], b[0], c[0], d[0], start, stop), [o], [a, b, c, d], grp, pre=pre, chain=not start)
+
+    def dma(q, o, i, grp=None):
+        add(q, lambda: eng[q].dma_start(ap(o), ap(i)), [o] if isinstance(o, tuple) else [], [i], grp, dma=True)
+
+    def iota(o, pat, base, cm, flag=True):
+        if flag:
+            add("G", lambda: g.iota(o[0], pat, base, cm, allow_small_or_imprecise_dtypes=True), [o], [])
+        else:
+            add("G", lambda: g.iota(o[0], pat, base, cm), [o], [])
+
+    def const(name, a, b, v):
+        iota(A(name, a, b), [[0, b - a]], v, 0)
+
+    def select(o, i, pat, op, base, cm, grp=None):
+        add("G", lambda: g.affine_select(o[0], i[0], pat, op, 0.0, base, cm), [o], [i], grp)
+
+    ones = A("one5", 0, C)
+    dma("Y", A("xb"), T.x[:])
+    dma("S", A("ub"), T.u[:])
+    dma("S", A("nbi"), T.nb[:])
+    dma("Y", bits(A("qw"), dt.uint8), T.wc[:], "w")
+    dma("Y", A("sw"), T.ws[:], "w")
+    dma("Y", A("vb"), T.v[:])
+    iota(A("uoi"), [[16, 8]], 0, 0, False)
+    iota(A("pmi"), [[15, 2]], 0, 1, False)
+    iota(A("tm"), [[0, 24], [1, 16]], 0, 0)
+    fill(A("one5"), 1.0)
+    select(A("gd"), A("one5"), [[-16, 8], [0, 64]], alu.is_ge, 0, 1)
+    select(A("gd2"), A("gd"), [[16, 8], [0, 64]], alu.is_ge, 15, -1)
+    const("fw", 0, 4 * C, 0)
+    const("wa", C3, C3 + 8, -1024)
+    const("wb", C3, C3 + 8, 0)
+    const("ca", 0, C3, 0)
+    const("wa", 0, C3, 0)
+    const("cb", 0, C3, 0)
+    scan(A("iot"), ones, ones, -1.0, alu.add, alu.mult)
+    sa(A("half"), A("one5"), act.Identity, 0.0, 0.5)
+    for b in range(4):
+        select(A("eb", 512 * b, 512 * b + 512), A("half"), [[-1, 512]], alu.is_equal, b, 4, "eb")
+    const("colb", 0, C3, 0)
+    const("tb", 0, 128, 0)
+    sa(A("io3"), A("iot"), act.Identity, 2.0, 3.0)
+    cp(A("uo"), A("uoi"))
+    ts(A("pmj"), A("pmi"), 15, alu.bitwise_and)
+    fill(A("alt"), 0.0)
+    cp(A("pm"), A("pmj"))
+    ts(A("cst"), A("iot", 0, 24), 16.0, alu.mult, 16.0 + C3, alu.add)
+    ts(A("po"), A("iot", 0, 24), 0.0, alu.mult, col("pm", 0), alu.add)
+    ts(col("cc", 7), col("pm", 0), 0.0, alu.is_equal)
+    ts(A("nf1"), A("iot", 0, 24), 16.0, alu.mult, col("pm", 0), alu.add)
+    for t in range(4):
+        ts(col("cc", t), col("cc", 7), 2 * CB, alu.mult, t - CB, alu.add)
+    ts(A("nof", 72, 96), A("nf1"), 3.0, alu.mult, 2.0, alu.add)
+    ts(A("md"), A("tm"), col("pm", 0), alu.is_equal)
+    ts(A("s16", 0, 16), A("tm", 0, 16), col("pm", 1), alu.is_equal, -2 * CB, alu.mult)
+    ts(A("s16", 16, 32), A("tm", 0, 16), col("pm", 0), alu.is_equal, CB, alu.mult)
+    ts(A("cst", 0, 16), A("cst", 0, 16), col("cc", 0), alu.add)
+    tt(A("s16", 64, 80), A("s16", 0, 16), A("s16", 16, 32), alu.add)
+    sa(A("rch"), A("tm"), act.Sign)
+    sa(A("rdi"), A("md"), act.Identity, 1.0, -1.0)
+    cp(A("nbo"), A("nbi"))
+    sc(A("nbv"), I(A("io3"), A("nbo")))
+    sc(A("madd"), I(A("s16", 64, 80), A("po")))
+    quant(A("qu"), A("su"), A("ub"))
+    ts(col("cc", 4), col("cc", 7), -2.0 ** 40, alu.mult, 2.0 ** 40, alu.add)
+    cp(bits(A("qu2"), dt.uint32), I(bits(A("qu"), dt.uint32), A("uo")), "u2")
+    cp(A("su2"), I(A("su"), A("uo")), "u2")
+    quant(A("qx"), A("sx"), A("xb"))
+    ts(col("cc", 4), col("cc", 4), 2.0 ** -40, alu.max)
+    ts(A("s16", 32, 48), A("tm", 0, 16), col("pm", 1), alu.not_equal, 2.0 ** -80, alu.max)
+    ts(A("s16", 48, 64), A("md", 0, 16), 2.0 ** 40, alu.mult, 1.0, alu.max)
+    ts(col("cc", 5), col("cc", 4), -1.0, alu.mult)
+    ts(col("cc", 6), col("cc", 4), -SH, alu.mult)
+    tt(A("s16", 80, 96), A("s16", 32, 48), A("s16", 48, 64), alu.mult)
+
+    def new_names(e):
+        sc(A("nbv", e, C3, 3), I(A("vn", C * e, C * e + C), A("lo", 0, 24)))
+
+    def names_wrapped(e):
+        scan(A("nsc", C * e, C * e + C), A("nbv", e, C3, 3), A("madd"), -1.0, alu.max, alu.add)
+
+    def names_pick(e):
+        ts(A("nof", 24 * e, 24 * e + 24), A("nsc", C * e + 15, C * e + C, 16), col("cc", 0), alu.add)
+
+    def step(win, ctl, out, tag, gap=None):
+        ts(A("gi", 0, C3, 3), I(A(win), A("nx")), SH, alu.add, 0.0, alu.max)
+        for (a, b) in PIECES:
+            for e in (1, 2):
+                sa(A("gi", 3 * a + e, 3 * b, 3), I(A(win), A("nof", 24 * e + a // 16, 24 * e + b // 16)), act.Relu, SH, 1.0, grp=tag + str(a))
+            scan(A(out, 3 * a, 3 * b), A("gi", 3 * a, 3 * b), A(ctl, 3 * a, 3 * b), 0.0, alu.max, alu.add)
+        if gap:
+            gap()
+
+    def rank_keys(key, tag, between, nv):
+        scan(A("ksc"), key, A("mmul"), 0.0, alu.min, alu.mult)
+        for m in range(24 - nv):
+            sa(A("sg", C * m, C * m + C), key, act.Sign, col("ksc", 16 * m + 15), col("cc", 5), col("acc", m), tag + "s")
+        for i in range(nv):
+            ts(A("cmp", C * i, C * i + C), key, col("cc", 4), alu.mult, col("ksc", 16 * (24 - nv + i) + 15), alu.is_gt, tag + "c%d" % (i // 5))
+            for f in between.get(i, []):
+                f()
+        for i in range(nv):
+            scan(A("scn", C * i, C * i + C), ones, A("cmp", C * i, C * i + C), -192.0, alu.mult, alu.add, tag + "n")
+
+    def ranked(o, sign, bs, bv, grp, nv):
+        if sign > 0:
+            ts(A(o, 24 - nv, 24), A("scn", C - 1, C * nv, C), bv, alu.add, grp=grp)
+        else:
+            ts(A(o, 24 - nv, 24), A("scn", C - 1, C * nv, C), -1.0, alu.mult, bv, alu.add, grp)
+        ts(A(o, 0, 24 - nv), A("acc", 0, 24 - nv), -0.5 * sign, alu.mult, bs, alu.add, grp)
+
+    U, NV, TN, BX, BW, ROOT, SG, US, UV, NU, RT3 = (col("col", c) for c in range(11))
+    RECT = ((16, 256, 0), (20, 256, 1024), (8, 128, 2048), (12, 128, 2560))
+
+    for r in range(R):
+        n = "r%d" % r
+        qt, st = "qt%d" % r, "st%d" % r
+        mm(0, C, "qu2", "su2", 0, "qx", "sx", 0)
+        mm(1, C, "qu2", "su2", 0, "qx", "sx", 0)
+        sv = A("ps", 0, C)
+        if r:
+            new_names(2)
+        for (a, b) in ((256, C), (0, 256)):
+            tt(A("t1", a, b), A("ps", a, b), A("md", a, b), alu.mult)
+        for (a, b) in ((256, C), (0, 256)):
+            scan(A("t2", a, b), A("rch", a, b), A("t1", a, b), 0.0, alu.mult, alu.add)
+        scan(A("cm"), sv, ones, -1e29, alu.max, alu.mult)
+
+        def signs(k):
+            m0, w, c0 = RECT[k]
+            for t in range(4):
+                sa(A("sg", c0 + w * t, c0 + w * t + w), A("ps", 512, 512 + w), act.Sign, col("t2", 16 * (m0 + t) + 15), -1.0, grp=n + "p%d" % k)
+
+        def lower(k):
+            m0, w, c0 = RECT[k]
+            for t in range(4):
+                sa(A("ct", c0 + t, c0 + 4 * w, 4), A("sg", c0 + w * t, c0 + w * t + w), act.Relu, 0.0, 1.0, col("alt", m0 + t), n + "q%d" % k)
+
+        def summed(k):
+            m0, w, c0 = RECT[k]
+            quant(A("qc", c0 // 4, c0 // 4 + w), A("scc", c0 // 4, c0 // 4 + w), A("ct", c0, c0 + 4 * w))
+            mm(2, w, "qg", "sgs", 0, "qc", "scc", c0 // 4, k == 0, k == 3, n + "cs")
+
+        signs(0)
+        sa(A("jk"), A("cm"), act.Sign, col("cm", C - 1), -1.0, ROOT)
+        signs(1)
+        lower(0)
+        signs(2)
+        lower(1)
+        signs(3)
+        lower(2)
+        lower(3)
+        for m in range(NSA):
+            sa(A("sg", 3072 + 128 * m, 3200 + 128 * m), A("ps", 512, 640), act.Sign, col("t2", 16 * m + 15), -1.0, grp=n + "a1")
+        for m in range(NSA):
+            a, h = 3072 + 128 * m, 3072 + 144 * m + 16
+            sa(A("sg", a, h), A("sg", a, h), act.Relu, 0.0, 1.0, col("alt", m), n + "a2")
+            sa(A("sg", h, a + 128), A("sg", h, a + 128), act.Relu, 0.0, -1.0, col("agt", m), n + "a2")
+        tt(A("eq"), sv, A("t2"), alu.is_equal)
+        small = {
+            0: [lambda: scan(A("cor"), A("rdi"), A("eq"), 0.0, alu.mult, alu.add)],
+            1: [lambda: tt(A("bas"), A("cst"), A("cor", 15, C, 16), alu.subtract)],
+            2: [lambda e=e: names_wrapped(e) for e in range(2 if r else 0, 3)],
+            3: [lambda e=e: names_pick(e) for e in range(3)] + [lambda: ts(RT3, ROOT, 3.0, alu.mult, 2.0, alu.add)],
+            4: [lambda: ts(A("fl"), A("nof"), RT3, alu.is_equal, float(C3), alu.mult), lambda: cp(A("nf0"), A("nof", 0, 24))],
+            5: [lambda: tt(A("fl2"), A("fl", 0, 48), A("fl", 48, 96), alu.max)],
+            6: [lambda: tt(A("fl3"), A("fl2", 0, 24), A("fl2", 24, 48), alu.max)],
+            7: [lambda: tt(A("bas"), A("bas"), A("fl3"), alu.subtract), lambda: tt(A("nf1"), A("nf0"), A("fl3"), alu.max)],
+            9: [lambda: cp(A("nx"), A("nf1")), lambda: ts(A("fl4"), A("fl3"), 2.0, alu.mult, -float(C3), alu.add)],
+            11: [lambda: summed(0)],
+            17: [lambda: summed(1)],
+        }
+        if r == 0:
+            small[8] = [lambda: quant(A("qg"), A("sgs"), A("gd2"))]
+        for i in range(NVA):
+            m = NSA + i
+            a, h = 128 * (m // 8), 16 * m + 16
+            gp = n + "c%d" % (i // 10)
+            ts(A("cmp", 128 * i, 128 * i + h - a), A("ps", a, h), col("t2", h - 1), alu.is_lt, -1.0, alu.mult, gp)
+            if h < a + 128:
+                ts(A("cmp", 128 * i + h - a, 128 * i + 128), A("ps", h, a + 128), col("t2", h - 1), alu.is_gt, grp=gp)
+            for f in small.get(i, []):
+                f()
+        for i in range(NVA):
+            scan(A("scn", 128 * i, 128 * i + 128), A("one5", 0, 128), A("cmp", 128 * i, 128 * i + 128), 0.0, alu.mult, alu.add, n + "n")
+            if i == 4:
+                summed(2)
+            if i == 11:
+                summed(3)
+                tt(A("bas", 8, 24), A("bas", 8, 24), A("alt", 8, 24), alu.subtract)
+            if i == 16:
+                scan(A("csc"), A("ps", 1024, 1280), A("madd", 0, 256), -1.0, alu.max, alu.add)
+            if i == 18:
+                tt(A("bas", 0, 16), A("bas", 0, 16), A("csc", 15, 256, 16), alu.add)
+        tt(A("rw", 0, NSA), A("agt", 0, NSA), A("alt", 0, NSA), alu.subtract)
+        tt(A("bas", NSA, 24), A("bas", NSA, 24), A("scn", 127, 128 * NVA, 128), alu.add)
+        tt(A("bas", 0, NSA), A("bas", 0, NSA), A("rw", 0, NSA), alu.add)
+        cp(A("o1"), A("bas"))
+        cp(I(A("fw"), A("o1")), ones)
+        if r == 0:
+            for (a, v) in ((1, 0.0), (2, 0.0), (4, 0.0), (5, 0.0), (6, HUGE)):
+                sa(A("ce", C * a, C * a + C), A("iot"), act.Identity, v, 0.0, grp="ce")
+            sc(A("mmul"), I(A("s16", 80, 96), A("po")))
+        tt(A("byw"), A("bas"), A("fl4"), alu.add)
+        scan(A("ce", 0, C), ones, A("fw", 0, C), 0.0, alu.add, alu.subtract)
+        scan(A("ce", C3, C3 + C), A("fw", 0, C), ones, -1.0, alu.add, alu.mult)
+        un = col("ce", C - 1)
+        sa(NU, un, act.Identity, 0.0, -1.0)
+        ts(NV, un, un, alu.mult, -1.0, alu.mult)
+        ts(BW, un, -383.0, alu.mult, -1024.0, alu.add)
+        cp(A("o1b"), A("byw"))
+        sa(A("ca", 2, C3, 3), I(A("ce", 0, 4 * C), A("o1b")), act.Identity, -SH, NU)
+        ts(A("wa", 2, C3, 3), I(A("ce", C3, 7 * C), A("o1")), NV, alu.mult, BW, alu.add)
+        step("wa", "ca", "wb", n + "s2", lambda: sa(A("cb", 2, C3, 3), I(A("ce", 0, 4 * C), A("o1b")), act.Identity, -SH - 512, -1.0))
+        step("wb", "cb", "kc", n + "s3")
+        key = A("kc", 2, C3, 3)
+        sa(A("jk"), key, act.Sign, SH, 1.0, SG)
+        rank_keys(key, n + "B", {
+            0: [lambda: ts(A("fl3"), A("ksc", 15, C, 16), col("cc", 6), alu.is_gt, float(C3), alu.mult)],
+            1: [lambda: ts(U, SG, -0.5, alu.mult, 192.0, alu.add), lambda: ts(NU, SG, 0.5, alu.mult, -192.0, alu.add)],
+            2: [lambda: ts(NV, U, NU, alu.mult), lambda: tt(A("nf1"), A("nf0"), A("fl3"), alu.max)],
+            3: [lambda: ts(TN, NU, 384.0, alu.add, NV, alu.mult), lambda: ts(BX, U, -384.0, alu.mult, -1024.0, alu.add)],
+            4: [lambda: ts(BW, TN, BX, alu.add), lambda: cp(A("nx"), A("nf1"))],
+            5: [lambda: ts(US, U, 191.5, alu.add), lambda: ts(UV, U, 192.0, alu.add)],
+            8: [lambda: quant(A("qe"), A("se"), A("eb"))] if r == 0 else [],
+        }, NVB)
+        if r == 0:
+            sa(A("wz", 0, C), A("iot"), act.Identity, -384.0, 1.0, grp="wz")
+            sa(A("wz", C, 2 * C), A("iot"), act.Identity, HUGE, 0.0, grp="wz")
+        for k in range(4):
+            mm(4 + k, C, "qe", "se", 128 * k, "qx", "sx", 0)
+        ranked("o3", 1, US, UV, n + "o3", NVB)
+        ranked("o2", 1, 191.5, 192.0, n + "o2", NVB)
+        ts(A("wa", 2, C3, 3), I(A("wz"), A("o3")), NV, alu.mult, BW, alu.add)
+        sa(A("ca", 2, C3, 3), I(A("iot"), A("o2")), act.Identity, -SH, NU)
+
+        def unpack(k):
+            sc(A("dh", C * k, C * k + C), A("ps", 512 * (4 + k), 512 * (4 + k) + C))
+
+        step("wa", "ca", "wb", n + "s4", lambda: sa(A("cb", 2, C3, 3), I(A("iot"), A("o2")), act.Identity, -SH - 512, -1.0))
+        if r == 0:
+            sa(A("rj"), A("iot"), act.Identity, 1000.0 - SH, -1.0)
+        step("wb", "cb", "kc", n + "s5")
+        for k in range(3):
+            unpack(k)
+        scan(A("key"), A("rj"), key, 0.0, alu.min, alu.max)
+        rank_keys(A("key"), n + "C", {1: [lambda: quant(A("qv"), A("sv"), A("vb"))]} if r == 0 else {}, NVC)
+        if r == 0:
+            sa(A("io4"), A("iot"), act.Identity, 0.0, 4.0)
+        ranked("oc2", -1, 191.5, 191.0, n + "oc", NVC)
+        cp(I(A("lb"), A("oc2")), A("io4"))
+        sc(A("colb", 2, C3, 3), I(A("io3" if r < R - 1 else "iot"), A("oc2")))
+        unpack(3)
+        for e in range(2):
+            sc(A("vn", C * e, C * e + C), I(A("colb"), A("nof", 24 * e, 24 * e + 24)))
+        scan(A("lsc"), A("lb"), A("madd"), -1.0, alu.max, alu.add)
+        for t in (0, 1, 2, 3):
+            ts(A("lo", 24 + 6 * t, 30 + 6 * t), A("lsc", C - K + 15, C, 16), col("cc", t), alu.add, grp=n + "lt")
+        ts(A("lo", 0, 24), A("lsc", 15, C, 16), col("cc", 0), alu.add, 0.25, alu.mult)
+        for t in range(4):
+            (cp if t < 3 else sc)(A("tb", 128 + t, 512, 4), I(A("xb"), A("lo", 24 + 6 * t, 30 + 6 * t)), n + "tb%d" % (t // 3))
+        quant(A(qt, K, K + 128), A(st, K, K + 128), A("tb"))
+        src_q, src_s = bits(A(qt, 128, K + 128), dt.uint8), A(st, 128, K + 128)
+        dst_q, dst_s = T[qt][:, 0:K].bitcast(dt.uint8), T[st][:, 0:K]
+        arr = T.sem["arr%d" % r]
+        add("G", lambda o=dst_q, i=src_q, s=arr: g.remote_dma(o, i[0], s, T.sem.sent, pid, rid, emask), [], [src_q], "rem")
+        add("G", lambda o=dst_s, i=src_s, s=arr: g.remote_dma(o, i[0], s, T.sem.sent, pid, rid, emask), [], [src_s], "rem")
+        for k in range(4):
+            win = A("dh", C * k, C * k + C)
+            sc(A("eh", C * k, C * k + C - K), I(win, A("lo", 0, (C - K) // 16)))
+            tt(A("zb", 4 * K + k, 4 * C, 4), I(win, A("lo", K // 16, 24)), A("eh", C * k, C * k + C - K), alu.add, n + "zl")
+        new_names(0)
+        for (a, b, bank) in ((128, C, 4), (0, 128, 0)):
+            w = b - a
+            if a == 0:
+                for k in range(4):
+                    mm(k, 128, "qe", "se", 128 * k, qt, st, 0, pre=(arr, 2 * neng) if k == 0 else None)
+                for k in range(4):
+                    tt(A("zb", k, 4 * K, 4), A("ps", 512 * k, 512 * k + K), A("eh", C * k, C * k + K), alu.add, n + "zr")
+            quant(A("qz", a, b), A("sz", a, b), A("zb", 4 * a, 4 * b))
+            if r < R - 1:
+                names_wrapped(0 if a else 1)
+            for k in range(4):
+                mm(bank + k, w, "qw", "sw", 128 * k, "qz", "sz", a)
+            for k in range(4):
+                o, i = A("xb", 4 * a + k, 4 * b, 4), A("ps", 512 * (bank + k), 512 * (bank + k) + w)
+                if k % 2:
+                    ts(o, i, 0.0, alu.max, 0.03125, alu.mult, grp=n + "xv%d" % a)
+                else:
+                    sa(o, i, act.Relu, 0.0, 0.03125, grp=n + "xs%d" % a)
+            quant(A("qx", a, b), A("sx", a, b), A("xb", 4 * a, 4 * b))
+            if a:
+                new_names(1)
+                sc(A("vn", 2 * C, C3), I(A("colb"), A("nof", 48, 72)))
+                if r == R - 1:
+                    dma("Y", T.oc[:, 4 * a:4 * b], bits(A("qx", a, b), dt.uint8), "outy")
+        if r < R - 1:
+            const("fw", 0, C, 0)
+
+    mm(4, C, "qv", "sv", 0, "qx", "sx", 0)
+    new_names(2)
+    dma("Y", T.oc[:, 0:512], bits(A("qx", 0, 128), dt.uint8), "outy")
+    cp(A("yb"), A("ps", 2048, 2048 + C))
+    for k in range(4):
+        dma("Y", T.osc[4 * k:4 * k + 4, :], (T.sx[32 * k:32 * k + 4, :], A("sx")[1]), "outy")
+    dma("S", T.on[:], (T.nbv[0:128:16, :], A("nbv")[1]), "outs")
+    dma("S", T.y[:], A("yb"), "outs")
+
+    groups = {}
+    for k, o in enumerate(ops):
+        groups.setdefault(o["grp"], []).append(k)
+    seen = {}
+    known = {q: 0 for q in eng}
+    snap, waits = [0] * len(ops), [[] for o in ops]
+    wanted = set(["outy", "outs"])
+
+    def need(k, j):
+        q, gp = ops[k]["q"], ops[j]["grp"]
+        if known[q] >> j & 1:
+            return
+        assert gp != ops[k]["grp"] and groups[gp][-1] < k, (k, j, gp)
+        waits[k].append(gp)
+        wanted.add(gp)
+        for i in groups[gp]:
+            known[q] |= snap[i] | 1 << i
+
+    for k, o in enumerate(ops):
+        deps = []
+        for (lst, writing) in ((o["rd"], False), (o["wr"], True)):
+            for (name, m) in lst:
+                for (j, m2, w2) in seen.get(name, []):
+                    if not m & m2:
+                        continue
+                    if writing or w2 or (name == "ps" and ops[j]["q"] != o["q"]):
+                        if not (o["chain"] and name == "ps" and ops[j]["grp"] == o["grp"]):
+                            deps.append(j)
+        for j in sorted(set(deps), reverse=True):
+            need(k, j)
+        snap[k] = known[o["q"]]
+        for (name, m) in o["rd"]:
+            seen.setdefault(name, []).append((k, m, False))
+        for (name, m) in o["wr"]:
+            seen[name] = [s for s in seen.get(name, []) if s[1] & ~m] + [(k, m, True)]
+
+    semof, total, last = {}, {}, {}
+    for k, o in enumerate(ops):
+        gp = o["grp"]
+        if gp not in wanted or gp in semof:
+            continue
+        pool = "D" if o["dma"] else o["q"]
+        pick = None
+        for i in range(POOL[pool]):
+            s = pool + str(i)
+            if s not in last or (not o["dma"] and all(snap[k] >> j & 1 for j in groups[last[s]])):
+                pick = s
+                break
+        assert pick is not None, (pool, k)
+        last[pick] = gp
+        total[pick] = total.get(pick, 0) + (16 if o["dma"] else 1) * len(groups[gp])
+        semof[gp] = (pick, total[pick])
+
+    for k, o in enumerate(ops):
+        e = eng[o["q"]]
+        for gp in waits[k]:
+            e.wait_ge(T.sem[semof[gp][0]], semof[gp][1])
+        if o["pre"]:
+            e.wait_ge(o["pre"][0], o["pre"][1])
+        inst = o["fn"]()
+        if o["grp"] in semof:
+            inst.then_inc(T.sem[semof[o["grp"]][0]], 16 if o["dma"] else 1)
+    g.wait_ge(T.sem.sent, 2 * R * neng)
+    g.sync.wait_ge(T.sem[semof["outy"][0]], semof["outy"][1])
+    g.scalar.wait_ge(T.sem[semof["outs"][0]], semof["outs"][1])

@@ -1,12 +1,21 @@
 from concourse.mybir import dt, AluOpType, AxisListType, ActivationFunctionType
 
 C, K, R = 384, 96, 3
-NSA = 4
-NVA = 24 - NSA
-NVB, NVC = 9, 10
+MS = 14
+NVB, NVC = 9, 8
+TBV = 14
+NM = 5
 PIECES = ((0, 160), (160, 288), (288, C))
 C3 = 3 * C
-SH, HUGE, CB = 12.0 * 2 ** 20, 2.0 ** 25, 2048.0
+R2 = C // 2
+R1 = C * R2
+TOP = float((C + 1) * R1)
+LIFT = 2.0 ** 25
+ZERO = float(R2 * R1 - R2 * R2 - R2 - R2 // 2)
+EVEN = 1.5 * 2 ** 24
+HUGE, CB, BIG = 1e29, 2048.0, 2.0 ** 60
+WID = (384, 320, 256, 192, 128, 128)
+OFF = (0, 384, 704, 960, 1152, 1280)
 F32, BF, I32, U16, Q4, U8 = "float32", "bfloat16", "int32", "uint16", "float8_e4m3fn_x4", "uint8"
 
 
@@ -23,25 +32,26 @@ SCRATCH = {
     "qu": _sb(128, Q4), "su": _sb(128, U8), "qu2": _sb(128, Q4), "su2": _sb(128, U8), "qv": _sb(128, Q4), "sv": _sb(128, U8),
     "qw": _sb(512, Q4), "sw": _sb(512, U8), "qe": _sb(512, Q4), "se": _sb(512, U8), "eb": _sb(2048, BF),
     "one5": _sb(512, BF), "half": _sb(512, BF), "gd": _sb(512, BF), "gd2": _sb(512, BF), "qg": _sb(128, Q4), "sgs": _sb(128, U8),
-    "ct": _sb(3072, BF), "qc": _sb(768, Q4), "scc": _sb(768, U8), "csc": _sb(256),
-    "pmi": _sb(2, I32), "pmj": _sb(2, I32), "pm": _sb(2), "uoi": _sb(8, I32), "uo": _sb(8, U16), "po": _sb(24, U16),
-    "iot": _sb(C), "io3": _sb(C), "io4": _sb(C), "rj": _sb(C), "wz": _sb(2 * C), "tm": _sb(C), "md": _sb(C),
-    "rch": _sb(C, BF), "rdi": _sb(C, BF), "madd": _sb(C), "mmul": _sb(C),
-    "s16": _sb(96), "cc": _sb(8), "cst": _sb(24), "fl": _sb(96), "fl2": _sb(48), "fl3": _sb(24), "fl4": _sb(24),
-    "t1": _sb(C), "t2": _sb(C), "cm": _sb(C), "eq": _sb(C, BF), "cor": _sb(C, BF),
-    "fw": _sb(4 * C, BF), "ce": _sb(7 * C), "wa": _sb(C3 + 8), "wb": _sb(C3 + 8), "gi": _sb(C3), "kc": _sb(C3),
-    "ca": _sb(C3), "cb": _sb(C3), "key": _sb(C), "ksc": _sb(C),
-    "cmp": _sb(10 * C, BF), "scn": _sb(10 * C, BF), "sg": _sb(16 * C, BF), "jk": _sb(C, BF),
-    "col": _sb(16), "acc": _sb(24), "alt": _sb(24), "agt": _sb(24), "rw": _sb(24), "bas": _sb(24), "byw": _sb(24),
-    "o1": _sb(24, U16), "o1b": _sb(24, U16), "o2": _sb(24, U16), "o3": _sb(24, U16), "oc2": _sb(24, U16), "lo": _sb(56, U16),
-    "lb": _sb(C), "lsc": _sb(C), "colb": _sb(C3), "yb": _sb(C),
+    "ct": _sb(4 * 1408, BF), "rs": _sb(4 * 1408, BF), "qc": _sb(1408, Q4), "scc": _sb(1408, U8), "csc": _sb(C), "rst": _sb(640, BF),
+    "pmi": _sb(4, I32), "pmj": _sb(6, I32), "pm": _sb(6), "uoi": _sb(8, I32), "uo": _sb(8, U16), "po": _sb(24, U16),
+    "iot": _sb(C), "io3": _sb(C), "io4": _sb(C), "tm": _sb(C), "md": _sb(C), "hm": _sb(C), "hn": _sb(C), "hd": _sb(C),
+    "rch": _sb(C, BF), "madd": _sb(C), "mmul": _sb(C), "tm4": _sb(K), "ma4": _sb(K), "mb4": _sb(K), "md4": _sb(K),
+    "s16": _sb(96), "cc": _sb(10), "cst": _sb(24), "fl": _sb(96), "fl2": _sb(48), "fl3": _sb(24), "fl4": _sb(24),
+    "t1": _sb(C), "t2": _sb(C), "cm": _sb(C), "hs": _sb(C, BF),
+    "h1": _sb(4 * C), "wa": _sb(C3 + 8), "wb": _sb(C3 + 8), "gi": _sb(C3), "kc": _sb(C3), "cb": _sb(C3),
+    "gj": _sb(4 * C), "kd": _sb(4 * C), "cd": _sb(4 * C), "ksc": _sb(C),
+    "cmp": _sb(10 * C, BF), "scn": _sb(10 * C, BF), "low": _sb(NM * C, BF), "sg": _sb(16 * C, BF), "jk": _sb(C, BF),
+    "col": _sb(4), "acc": _sb(24), "alt": _sb(24), "bas": _sb(24), "pi": _sb(24, I32), "pj": _sb(24, I32),
+    "pc": _sb(24), "pq": _sb(24), "pr": _sb(24), "thr": _sb(24), "tw": _sb(24),
+    "o1": _sb(24, U16), "o2": _sb(24, U16), "oc2": _sb(24, U16), "lo": _sb(24, U16), "lob": _sb(24, U16),
+    "lsc": _sb(C), "lsb": _sb(K), "yb": _sb(C),
     "ps": ("psum", [128, 4096], F32),
 }
 for _r in range(R):
     SCRATCH["qt%d" % _r] = _sb(K + 128, Q4)
     SCRATCH["st%d" % _r] = _sb(K + 128, U8)
 
-POOL = {"V": 44, "S": 36, "P": 16, "G": 20, "D": 16}
+POOL = {"V": 48, "S": 40, "P": 16, "G": 22, "D": 16}
 SEMAPHORES = [q + str(i) for q in POOL for i in range(POOL[q])] + ["arr%d" % r for r in range(R)] + ["sent"]
 
 
@@ -131,109 +141,162 @@ def rank_program(g, core, T, topo):
         else:
             add("G", lambda: g.iota(o[0], pat, base, cm), [o], [])
 
-    def const(name, a, b, v):
-        iota(A(name, a, b), [[0, b - a]], v, 0)
+    def select(o, i, pat, op, base, cm, other=0.0, grp=None):
+        add("G", lambda: g.affine_select(o[0], i[0], pat, op, other, base, cm), [o], [i], grp)
 
-    def select(o, i, pat, op, base, cm, grp=None):
-        add("G", lambda: g.affine_select(o[0], i[0], pat, op, 0.0, base, cm), [o], [i], grp)
+    def run(calls):
+        for f in calls:
+            f()
 
     ones = A("one5", 0, C)
+    CATCH, CAT4, UP, DOWN, PLACED, LANE0, ENDF = (col("cc", c) for c in range(7))
+    RUNS = [[0, 24], [1, 16]]
     dma("Y", A("xb"), T.x[:])
     dma("S", A("ub"), T.u[:])
     dma("S", A("nbi"), T.nb[:])
+    iota(A("pmi", 0, 2), [[15, 2]], 0, 1, False)
+    iota(A("tm"), RUNS, 0, 0)
+    iota(A("uoi"), [[16, 8]], 0, 0, False)
+    iota(A("pmi", 2, 4), [[12, 2]], 0, 1, False)
+    fill(A("one5"), 1.0)
+    fill(A("tb"), 0.0)
+    scan(A("iot"), ones, ones, -1.0, alu.add, alu.mult)
+    for k in range(5):
+        dma("Y", A("ct", 4 * (OFF[k] + WID[k] - 48), 4 * (OFF[k] + WID[k])), A("tb", 0, 192), "ctz")
+    dma("Y", A("ct", 4 * (OFF[5] + 16), 4 * (OFF[5] + 128)), A("tb", 0, 448), "ctz")
     dma("Y", bits(A("qw"), dt.uint8), T.wc[:], "w")
     dma("Y", A("sw"), T.ws[:], "w")
     dma("Y", A("vb"), T.v[:])
-    iota(A("uoi"), [[16, 8]], 0, 0, False)
-    iota(A("pmi"), [[15, 2]], 0, 1, False)
-    iota(A("tm"), [[0, 24], [1, 16]], 0, 0)
-    fill(A("one5"), 1.0)
-    select(A("gd"), A("one5"), [[-16, 8], [0, 64]], alu.is_ge, 0, 1)
-    select(A("gd2"), A("gd"), [[16, 8], [0, 64]], alu.is_ge, 15, -1)
-    const("fw", 0, 4 * C, 0)
-    const("wa", C3, C3 + 8, -1024)
-    const("wb", C3, C3 + 8, 0)
-    const("ca", 0, C3, 0)
-    const("wa", 0, C3, 0)
-    const("cb", 0, C3, 0)
-    scan(A("iot"), ones, ones, -1.0, alu.add, alu.mult)
-    sa(A("half"), A("one5"), act.Identity, 0.0, 0.5)
-    for b in range(4):
-        select(A("eb", 512 * b, 512 * b + 512), A("half"), [[-1, 512]], alu.is_equal, b, 4, "eb")
-    const("colb", 0, C3, 0)
-    const("tb", 0, 128, 0)
+    ts(A("pmj", 0, 2), A("pmi", 0, 2), 15, alu.bitwise_and)
     sa(A("io3"), A("iot"), act.Identity, 2.0, 3.0)
-    cp(A("uo"), A("uoi"))
-    ts(A("pmj"), A("pmi"), 15, alu.bitwise_and)
-    fill(A("alt"), 0.0)
-    cp(A("pm"), A("pmj"))
-    ts(A("cst"), A("iot", 0, 24), 16.0, alu.mult, 16.0 + C3, alu.add)
-    ts(A("po"), A("iot", 0, 24), 0.0, alu.mult, col("pm", 0), alu.add)
-    ts(col("cc", 7), col("pm", 0), 0.0, alu.is_equal)
-    ts(A("nf1"), A("iot", 0, 24), 16.0, alu.mult, col("pm", 0), alu.add)
-    for t in range(4):
-        ts(col("cc", t), col("cc", 7), 2 * CB, alu.mult, t - CB, alu.add)
-    ts(A("nof", 72, 96), A("nf1"), 3.0, alu.mult, 2.0, alu.add)
+    cp(A("pm", 0, 2), A("pmj", 0, 2))
+    cp(A("nbo"), A("nbi"))
     ts(A("md"), A("tm"), col("pm", 0), alu.is_equal)
+    cp(A("uo"), A("uoi"))
+    ts(A("po"), A("iot", 0, 24), 0.0, alu.mult, col("pm", 0), alu.add)
     ts(A("s16", 0, 16), A("tm", 0, 16), col("pm", 1), alu.is_equal, -2 * CB, alu.mult)
     ts(A("s16", 16, 32), A("tm", 0, 16), col("pm", 0), alu.is_equal, CB, alu.mult)
-    ts(A("cst", 0, 16), A("cst", 0, 16), col("cc", 0), alu.add)
-    tt(A("s16", 64, 80), A("s16", 0, 16), A("s16", 16, 32), alu.add)
-    sa(A("rch"), A("tm"), act.Sign)
-    sa(A("rdi"), A("md"), act.Identity, 1.0, -1.0)
-    cp(A("nbo"), A("nbi"))
-    sc(A("nbv"), I(A("io3"), A("nbo")))
-    sc(A("madd"), I(A("s16", 64, 80), A("po")))
+    sa(A("hn"), A("md"), act.Identity, HUGE, -2 * HUGE)
+    sa(A("hm"), A("md"), act.Identity, -HUGE, 2 * HUGE)
+    select(A("hd"), A("hn"), RUNS, alu.is_gt, 0, 0, -HUGE)
+    select(A("gd"), A("one5"), [[-16, 8], [0, 64]], alu.is_ge, 0, 1)
+    select(A("gd2"), A("gd"), [[16, 8], [0, 64]], alu.is_ge, 15, -1)
+    select(A("rch"), ones, RUNS, alu.is_gt, 0, 0)
+    iota(A("rst"), [[0, 640]], 1, 0)
+    for c in (256, 448, 576):
+        iota(col("rst", c), [[0, 1]], 0, 0)
+    iota(A("h1"), [[1, 2 * C], [0, 2]], 0, 0)
+    iota(A("low"), [[0, NM], [1, C]], -R2, 0)
+    fill(A("half"), 0.5)
+    for b in range(4):
+        select(A("eb", 512 * b, 512 * b + 512), A("half"), [[-1, 512]], alu.is_equal, b, 4, 0.0, "eb")
+    iota(A("tm4"), [[0, 24], [1, 4]], 0, 0)
     quant(A("qu"), A("su"), A("ub"))
-    ts(col("cc", 4), col("cc", 7), -2.0 ** 40, alu.mult, 2.0 ** 40, alu.add)
+    ts(LANE0, col("pm", 0), 0.0, alu.is_equal)
+    tt(A("s16", 64, 80), A("s16", 0, 16), A("s16", 16, 32), alu.add)
     cp(bits(A("qu2"), dt.uint32), I(bits(A("qu"), dt.uint32), A("uo")), "u2")
     cp(A("su2"), I(A("su"), A("uo")), "u2")
+    sc(A("nbv"), I(A("io3"), A("nbo")))
+    sc(A("madd"), I(A("s16", 64, 80), A("po")))
+    ts(A("nf1"), A("iot", 0, 24), 16.0, alu.mult, col("pm", 0), alu.add)
+    ts(CATCH, LANE0, 2 * CB, alu.mult, -CB, alu.add)
+    ts(A("cst"), A("iot", 0, 24), 16.0, alu.mult, col("pm", 0), alu.subtract)
     quant(A("qx"), A("sx"), A("xb"))
-    ts(col("cc", 4), col("cc", 4), 2.0 ** -40, alu.max)
-    ts(A("s16", 32, 48), A("tm", 0, 16), col("pm", 1), alu.not_equal, 2.0 ** -80, alu.max)
-    ts(A("s16", 48, 64), A("md", 0, 16), 2.0 ** 40, alu.mult, 1.0, alu.max)
-    ts(col("cc", 5), col("cc", 4), -1.0, alu.mult)
-    ts(col("cc", 6), col("cc", 4), -SH, alu.mult)
-    tt(A("s16", 80, 96), A("s16", 32, 48), A("s16", 48, 64), alu.mult)
+    ts(A("nof", 72, 96), A("nf1"), 3.0, alu.mult, 2.0, alu.add)
+    ts(A("cst"), A("cst"), CATCH, alu.add, 15.0 + C, alu.add)
+
+    key_constants = [
+        lambda: ts(UP, LANE0, -BIG, alu.mult, BIG, alu.add),
+        lambda: ts(ENDF, LANE0, -1.0, alu.mult, 1.0, alu.add),
+        lambda: ts(A("s16", 32, 48), A("tm", 0, 16), col("pm", 0), alu.is_gt),
+        lambda: ts(A("s16", 48, 64), A("md", 0, 16), BIG, alu.mult),
+        lambda: ts(UP, UP, 1 / BIG, alu.max),
+        lambda: ts(ENDF, ENDF, 1 / (BIG * BIG), alu.max),
+        lambda: tt(A("s16", 80, 96), A("s16", 32, 48), A("s16", 48, 64), alu.add),
+        lambda: fill(A("wa", C3, C3 + 8), 0.0),
+        lambda: fill(A("wb", C3, C3 + 8), -LIFT),
+        lambda: ts(col("s16", 95), col("s16", 95), ENDF, alu.mult),
+        lambda: sa(DOWN, UP, act.Identity, 0.0, -1.0),
+        lambda: sa(PLACED, UP, act.Identity, 0.0, -ZERO - 500.0),
+    ]
+    border_constants = [
+        lambda: ts(A("pmj", 2, 4), A("pmi", 2, 4), 15, alu.bitwise_and, 2, alu.logical_shift_right),
+        lambda: ts(A("pmj", 4, 5), A("pmi", 0, 1), 3, alu.bitwise_and),
+        lambda: cp(A("pm", 2, 5), A("pmj", 2, 5)),
+        lambda: ts(A("ma4"), A("tm4"), col("pm", 3), alu.is_equal, -2 * CB, alu.mult),
+        lambda: ts(A("mb4"), A("tm4"), col("pm", 2), alu.is_equal, CB, alu.mult),
+        lambda: ts(CAT4, col("pm", 2), 0.0, alu.is_equal, 2 * CB, alu.mult),
+        lambda: tt(A("md4"), A("ma4"), A("mb4"), alu.add),
+        lambda: ts(CAT4, CAT4, col("pm", 4), alu.add, -CB, alu.add),
+    ]
+
+    def even(o, v):
+        sa(o, A("iot"), act.Identity, v, 0.0)
 
     def new_names(e):
-        sc(A("nbv", e, C3, 3), I(A("vn", C * e, C * e + C), A("lo", 0, 24)))
+        sc(A("nbv", e, C3, 3), I(A("vn", C * e, C * e + C), A("lo")))
 
     def names_wrapped(e):
         scan(A("nsc", C * e, C * e + C), A("nbv", e, C3, 3), A("madd"), -1.0, alu.max, alu.add)
 
     def names_pick(e):
-        ts(A("nof", 24 * e, 24 * e + 24), A("nsc", C * e + 15, C * e + C, 16), col("cc", 0), alu.add)
+        ts(A("nof", 24 * e, 24 * e + 24), A("nsc", C * e + 15, C * e + C, 16), CATCH, alu.add)
 
-    def step(win, ctl, out, tag, gap=None):
-        ts(A("gi", 0, C3, 3), I(A(win), A("nx")), SH, alu.add, 0.0, alu.max)
-        for (a, b) in PIECES:
+    def step(win, first, lifts, scale, got, ctl, out, w, tag, after):
+        ts(A(got, 0, w * C, w), I(A(win), A("nx")), *first)
+        for p, (a, b) in enumerate(PIECES):
             for e in (1, 2):
-                sa(A("gi", 3 * a + e, 3 * b, 3), I(A(win), A("nof", 24 * e + a // 16, 24 * e + b // 16)), act.Relu, SH, 1.0, grp=tag + str(a))
-            scan(A(out, 3 * a, 3 * b), A("gi", 3 * a, 3 * b), A(ctl, 3 * a, 3 * b), 0.0, alu.max, alu.add)
-        if gap:
-            gap()
+                sa(A(got, w * a + e, w * b, w), I(A(win), A("nof", 24 * e + a // 16, 24 * e + b // 16)), act.Identity, lifts[e - 1], scale, grp=tag + str(a))
+            scan(A(out, w * a, w * b), A(got, w * a, w * b), A(ctl, w * a, w * b), -LIFT, alu.max, alu.add)
+            run(after.get(p, []))
+
+    def two_steps(o, got, ctl, out, w, tag, gap_a, gap_b):
+        ts(A("wa", 2, C3 // 2, 3), I(A("h1"), A(o, 0, 12)), -float(R2), alu.mult)
+        sa(A("wa", C3 // 2 + 2, C3, 3), I(A("h1"), A(o, 12, 24)), act.Identity, 0.0, -float(R2))
+        half_digit = lambda: sa(A(ctl, 2, w * C, w), A("wa", 2, C3, 3), act.Identity, -ZERO, 0.4995 / R2)
+        step("wa", (float(C), alu.mult, -TOP, alu.max), (0.0, -LIFT), float(C), "gi", "wa", "wb", 3, tag + "a", {2: [half_digit] + gap_a})
+        key = A(out, w - 1, w * C, w)
+        a = PIECES[0][1]
+        catch = lambda a, b: scan(A("ksc", a, b), A(out, w * a + w - 1, w * b, w), A("mmul", a, b), 0.0, alu.add, alu.mult)
+        step("wb", (-R1 - TOP - LIFT, alu.max, TOP + 2 * LIFT, alu.add), (TOP + LIFT, TOP + LIFT), 1.0, got, ctl, out, w, tag + "b",
+             {1: [lambda: catch(0, a)], 2: gap_b + [lambda: catch(a, C)]})
+        return key
 
     def rank_keys(key, tag, between, nv):
-        scan(A("ksc"), key, A("mmul"), 0.0, alu.min, alu.mult)
-        for m in range(24 - nv):
-            sa(A("sg", C * m, C * m + C), key, act.Sign, col("ksc", 16 * m + 15), col("cc", 5), col("acc", m), tag + "s")
+        ns = 24 - nv
+        for m in range(ns):
+            sa(A("sg", C * m, C * m + C), key, act.Sign, col("ksc", 16 * m + 15), DOWN, col("acc", m), tag + "s%d" % min(m // 8, 1))
+        run(between.get(-2, []))
+        tt(A("thr", ns, 24), A("ksc", 16 * ns + 15, C, 16), A("pc", ns, 24), alu.subtract)
+        run(between.get(-1, []))
         for i in range(nv):
-            ts(A("cmp", C * i, C * i + C), key, col("cc", 4), alu.mult, col("ksc", 16 * (24 - nv + i) + 15), alu.is_gt, tag + "c%d" % (i // 5))
-            for f in between.get(i, []):
-                f()
-        for i in range(nv):
-            scan(A("scn", C * i, C * i + C), ones, A("cmp", C * i, C * i + C), -192.0, alu.mult, alu.add, tag + "n")
+            ts(A("cmp", C * i, C * i + C), key, UP, alu.mult, col("thr", ns + i), alu.is_gt, tag + "c%d" % (i // NM))
+            run(between.get(i, []))
+        for i in range(0, nv, NM):
+            w = C * min(NM, nv - i)
+            scan(A("scn", C * i, C * i + w), A("low", 0, w), A("cmp", C * i, C * i + w), -float(R2), alu.min, alu.add, tag + "n")
 
-    def ranked(o, sign, bs, bv, grp, nv):
+    def ranked_v(sign, p, nv):
+        ends = A("scn", C - 1, C * nv, C)
         if sign > 0:
-            ts(A(o, 24 - nv, 24), A("scn", C - 1, C * nv, C), bv, alu.add, grp=grp)
+            tt(A("tw", 24 - nv, 24), ends, A(p, 24 - nv, 24), alu.add)
         else:
-            ts(A(o, 24 - nv, 24), A("scn", C - 1, C * nv, C), -1.0, alu.mult, bv, alu.add, grp)
-        ts(A(o, 0, 24 - nv), A("acc", 0, 24 - nv), -0.5 * sign, alu.mult, bs, alu.add, grp)
+            tt(A("tw", 24 - nv, 24), A(p, 24 - nv, 24), ends, alu.subtract)
 
-    U, NV, TN, BX, BW, ROOT, SG, US, UV, NU, RT3 = (col("col", c) for c in range(11))
-    RECT = ((16, 256, 0), (20, 256, 1024), (8, 128, 2048), (12, 128, 2560))
+    def ranked_s(sign, p, a, b):
+        tt(A("tw", a, b), A(p, a, b), A("acc", a, b), alu.subtract if sign > 0 else alu.add)
+
+    def offsets_v(o, nv):
+        ts(A(o, 24 - nv, 24), A("tw", 24 - nv, 24), 2.0, alu.mult)
+
+    def offsets_s(o, a, b):
+        ts(A(o, a, b), A("tw", a, b), EVEN, alu.add, EVEN, alu.subtract)
+
+    ROOT, RT3 = col("col", 0), col("col", 1)
+
+    def slot(m):
+        k, t = 5 - (m - 1) // 4, (m - 1) % 4
+        return A("ct", 4 * OFF[k] + t, 4 * (OFF[k] + 16 * m), 4)
 
     for r in range(R):
         n = "r%d" % r
@@ -241,147 +304,172 @@ def rank_program(g, core, T, topo):
         mm(0, C, "qu2", "su2", 0, "qx", "sx", 0)
         mm(1, C, "qu2", "su2", 0, "qx", "sx", 0)
         sv = A("ps", 0, C)
-        if r:
-            new_names(2)
-        for (a, b) in ((256, C), (0, 256)):
-            tt(A("t1", a, b), A("ps", a, b), A("md", a, b), alu.mult)
-        for (a, b) in ((256, C), (0, 256)):
-            scan(A("t2", a, b), A("rch", a, b), A("t1", a, b), 0.0, alu.mult, alu.add)
-        scan(A("cm"), sv, ones, -1e29, alu.max, alu.mult)
-
-        def signs(k):
-            m0, w, c0 = RECT[k]
-            for t in range(4):
-                sa(A("sg", c0 + w * t, c0 + w * t + w), A("ps", 512, 512 + w), act.Sign, col("t2", 16 * (m0 + t) + 15), -1.0, grp=n + "p%d" % k)
-
-        def lower(k):
-            m0, w, c0 = RECT[k]
-            for t in range(4):
-                sa(A("ct", c0 + t, c0 + 4 * w, 4), A("sg", c0 + w * t, c0 + w * t + w), act.Relu, 0.0, 1.0, col("alt", m0 + t), n + "q%d" % k)
-
-        def summed(k):
-            m0, w, c0 = RECT[k]
-            quant(A("qc", c0 // 4, c0 // 4 + w), A("scc", c0 // 4, c0 // 4 + w), A("ct", c0, c0 + 4 * w))
-            mm(2, w, "qg", "sgs", 0, "qc", "scc", c0 // 4, k == 0, k == 3, n + "cs")
-
-        signs(0)
-        sa(A("jk"), A("cm"), act.Sign, col("cm", C - 1), -1.0, ROOT)
-        signs(1)
-        lower(0)
-        signs(2)
-        lower(1)
-        signs(3)
-        lower(2)
-        lower(3)
-        for m in range(NSA):
-            sa(A("sg", 3072 + 128 * m, 3200 + 128 * m), A("ps", 512, 640), act.Sign, col("t2", 16 * m + 15), -1.0, grp=n + "a1")
-        for m in range(NSA):
-            a, h = 3072 + 128 * m, 3072 + 144 * m + 16
-            sa(A("sg", a, h), A("sg", a, h), act.Relu, 0.0, 1.0, col("alt", m), n + "a2")
-            sa(A("sg", h, a + 128), A("sg", h, a + 128), act.Relu, 0.0, -1.0, col("agt", m), n + "a2")
-        tt(A("eq"), sv, A("t2"), alu.is_equal)
-        small = {
-            0: [lambda: scan(A("cor"), A("rdi"), A("eq"), 0.0, alu.mult, alu.add)],
-            1: [lambda: tt(A("bas"), A("cst"), A("cor", 15, C, 16), alu.subtract)],
-            2: [lambda e=e: names_wrapped(e) for e in range(2 if r else 0, 3)],
-            3: [lambda e=e: names_pick(e) for e in range(3)] + [lambda: ts(RT3, ROOT, 3.0, alu.mult, 2.0, alu.add)],
-            4: [lambda: ts(A("fl"), A("nof"), RT3, alu.is_equal, float(C3), alu.mult), lambda: cp(A("nf0"), A("nof", 0, 24))],
-            5: [lambda: tt(A("fl2"), A("fl", 0, 48), A("fl", 48, 96), alu.max)],
-            6: [lambda: tt(A("fl3"), A("fl2", 0, 24), A("fl2", 24, 48), alu.max)],
-            7: [lambda: tt(A("bas"), A("bas"), A("fl3"), alu.subtract), lambda: tt(A("nf1"), A("nf0"), A("fl3"), alu.max)],
-            9: [lambda: cp(A("nx"), A("nf1")), lambda: ts(A("fl4"), A("fl3"), 2.0, alu.mult, -float(C3), alu.add)],
-            11: [lambda: summed(0)],
-            17: [lambda: summed(1)],
-        }
-        if r == 0:
-            small[8] = [lambda: quant(A("qg"), A("sgs"), A("gd2"))]
-        for i in range(NVA):
-            m = NSA + i
-            a, h = 128 * (m // 8), 16 * m + 16
-            gp = n + "c%d" % (i // 10)
-            ts(A("cmp", 128 * i, 128 * i + h - a), A("ps", a, h), col("t2", h - 1), alu.is_lt, -1.0, alu.mult, gp)
-            if h < a + 128:
-                ts(A("cmp", 128 * i + h - a, 128 * i + 128), A("ps", h, a + 128), col("t2", h - 1), alu.is_gt, grp=gp)
-            for f in small.get(i, []):
-                f()
-        for i in range(NVA):
-            scan(A("scn", 128 * i, 128 * i + 128), A("one5", 0, 128), A("cmp", 128 * i, 128 * i + 128), 0.0, alu.mult, alu.add, n + "n")
-            if i == 4:
-                summed(2)
-            if i == 11:
-                summed(3)
-                tt(A("bas", 8, 24), A("bas", 8, 24), A("alt", 8, 24), alu.subtract)
-            if i == 16:
-                scan(A("csc"), A("ps", 1024, 1280), A("madd", 0, 256), -1.0, alu.max, alu.add)
-            if i == 18:
-                tt(A("bas", 0, 16), A("bas", 0, 16), A("csc", 15, 256, 16), alu.add)
-        tt(A("rw", 0, NSA), A("agt", 0, NSA), A("alt", 0, NSA), alu.subtract)
-        tt(A("bas", NSA, 24), A("bas", NSA, 24), A("scn", 127, 128 * NVA, 128), alu.add)
-        tt(A("bas", 0, NSA), A("bas", 0, NSA), A("rw", 0, NSA), alu.add)
-        cp(A("o1"), A("bas"))
-        cp(I(A("fw"), A("o1")), ones)
-        if r == 0:
-            for (a, v) in ((1, 0.0), (2, 0.0), (4, 0.0), (5, 0.0), (6, HUGE)):
-                sa(A("ce", C * a, C * a + C), A("iot"), act.Identity, v, 0.0, grp="ce")
-            sc(A("mmul"), I(A("s16", 80, 96), A("po")))
-        tt(A("byw"), A("bas"), A("fl4"), alu.add)
-        scan(A("ce", 0, C), ones, A("fw", 0, C), 0.0, alu.add, alu.subtract)
-        scan(A("ce", C3, C3 + C), A("fw", 0, C), ones, -1.0, alu.add, alu.mult)
-        un = col("ce", C - 1)
-        sa(NU, un, act.Identity, 0.0, -1.0)
-        ts(NV, un, un, alu.mult, -1.0, alu.mult)
-        ts(BW, un, -383.0, alu.mult, -1024.0, alu.add)
-        cp(A("o1b"), A("byw"))
-        sa(A("ca", 2, C3, 3), I(A("ce", 0, 4 * C), A("o1b")), act.Identity, -SH, NU)
-        ts(A("wa", 2, C3, 3), I(A("ce", C3, 7 * C), A("o1")), NV, alu.mult, BW, alu.add)
-        step("wa", "ca", "wb", n + "s2", lambda: sa(A("cb", 2, C3, 3), I(A("ce", 0, 4 * C), A("o1b")), act.Identity, -SH - 512, -1.0))
-        step("wb", "cb", "kc", n + "s3")
-        key = A("kc", 2, C3, 3)
-        sa(A("jk"), key, act.Sign, SH, 1.0, SG)
-        rank_keys(key, n + "B", {
-            0: [lambda: ts(A("fl3"), A("ksc", 15, C, 16), col("cc", 6), alu.is_gt, float(C3), alu.mult)],
-            1: [lambda: ts(U, SG, -0.5, alu.mult, 192.0, alu.add), lambda: ts(NU, SG, 0.5, alu.mult, -192.0, alu.add)],
-            2: [lambda: ts(NV, U, NU, alu.mult), lambda: tt(A("nf1"), A("nf0"), A("fl3"), alu.max)],
-            3: [lambda: ts(TN, NU, 384.0, alu.add, NV, alu.mult), lambda: ts(BX, U, -384.0, alu.mult, -1024.0, alu.add)],
-            4: [lambda: ts(BW, TN, BX, alu.add), lambda: cp(A("nx"), A("nf1"))],
-            5: [lambda: ts(US, U, 191.5, alu.add), lambda: ts(UV, U, 192.0, alu.add)],
-            8: [lambda: quant(A("qe"), A("se"), A("eb"))] if r == 0 else [],
-        }, NVB)
-        if r == 0:
-            sa(A("wz", 0, C), A("iot"), act.Identity, -384.0, 1.0, grp="wz")
-            sa(A("wz", C, 2 * C), A("iot"), act.Identity, HUGE, 0.0, grp="wz")
-        for k in range(4):
-            mm(4 + k, C, "qe", "se", 128 * k, "qx", "sx", 0)
-        ranked("o3", 1, US, UV, n + "o3", NVB)
-        ranked("o2", 1, 191.5, 192.0, n + "o2", NVB)
-        ts(A("wa", 2, C3, 3), I(A("wz"), A("o3")), NV, alu.mult, BW, alu.add)
-        sa(A("ca", 2, C3, 3), I(A("iot"), A("o2")), act.Identity, -SH, NU)
 
         def unpack(k):
             sc(A("dh", C * k, C * k + C), A("ps", 512 * (4 + k), 512 * (4 + k) + C))
 
-        step("wa", "ca", "wb", n + "s4", lambda: sa(A("cb", 2, C3, 3), I(A("iot"), A("o2")), act.Identity, -SH - 512, -1.0))
+        if r:
+            for k in range(4):
+                mm(4 + k, C, "qe", "se", 128 * k, "qx", "sx", 0)
+            names_wrapped(1)
+            new_names(2)
+        for (a, b) in ((256, C), (0, 256)):
+            tt(A("t1", a, b), A("ps", a, b), A("hm", a, b), alu.min)
+        for (a, b) in ((256, C), (0, 256)):
+            scan(A("t2", a, b), A("hd", a, b), A("t1", a, b), 0.0, alu.min, alu.max)
+        scan(A("cm"), sv, ones, -HUGE, alu.max, alu.mult)
+
+        def runs(k):
+            return range(21 - 4 * k, min(25 - 4 * k, 24))
+
+        def signs(k):
+            for m in runs(k):
+                if m >= MS:
+                    sa(A("sg", C * (m - 8), C * (m - 8) + 16 * m), A("ps", 512, 512 + 16 * m), act.Sign, col("t2", 16 * m + 15), -1.0, grp=n + "p%d" % k)
+
+        def lower(k):
+            for m in runs(k):
+                if m >= MS:
+                    sa(slot(m), A("sg", C * (m - 8), C * (m - 8) + 16 * m), act.Relu, 0.0, 1.0, col("alt", m), n + "q%d" % k)
+
+        def summed(k):
+            w = WID[k] if k < 4 else (256 if r == 0 else 192)
+            quant(A("qc", OFF[k], OFF[k] + w), A("scc", OFF[k], OFF[k] + w), A("ct", 4 * OFF[k], 4 * (OFF[k] + w)))
+
+        signs(0)
+        sa(A("jk"), A("cm"), act.Sign, col("cm", C - 1), -1.0, ROOT)
+        signs(1)
+        sa(RT3, ROOT, act.Identity, 2.0, 3.0)
+        lower(0)
+        signs(2)
+        lower(1)
+        lower(2)
+        tt(slot(24), sv, A("t2"), alu.is_le)
+        small = {
+            12: [lambda e=e: names_wrapped(e) for e in range(2 if r else 0, 3)],
+            11: [lambda e=e: names_pick(e) for e in range(3)],
+            10: [lambda: scan(A("hs"), A("rch"), slot(24), 0.0, alu.mult, alu.add)],
+            9: [lambda: cp(A("nf0"), A("nof", 0, 24))],
+            8: [lambda: tt(A("bas"), A("cst"), A("hs", 15, C, 16), alu.subtract)],
+            6: [lambda: ts(A("fl"), A("nof"), RT3, alu.is_equal, float(C3), alu.mult)],
+            5: [lambda: tt(A("fl2"), A("fl", 0, 48), A("fl", 48, 96), alu.max)],
+            4: [lambda: tt(A("fl3"), A("fl2", 0, 24), A("fl2", 24, 48), alu.max)],
+            3: [lambda: ts(A("fl4"), A("fl3"), 0.0, alu.is_gt, -float(C), alu.mult)],
+            2: [lambda: tt(A("nf1"), A("nf0"), A("fl3"), alu.max)],
+            1: [lambda: tt(A("bas"), A("bas"), A("fl4"), alu.add)],
+        }
         if r == 0:
-            sa(A("rj"), A("iot"), act.Identity, 1000.0 - SH, -1.0)
-        step("wb", "cb", "kc", n + "s5")
-        for k in range(3):
-            unpack(k)
-        scan(A("key"), A("rj"), key, 0.0, alu.min, alu.max)
-        rank_keys(A("key"), n + "C", {1: [lambda: quant(A("qv"), A("sv"), A("vb"))]} if r == 0 else {}, NVC)
+            small[7] = [lambda: quant(A("qg"), A("sgs"), A("gd2"))]
+        for m in range(MS - 1, 0, -1):
+            ts(slot(m), A("ps", 0, 16 * m), col("t2", 16 * m + 15), alu.is_lt, grp=n + "c%d" % ((m - 1) // 4))
+            run(small.get(m, []))
+        summed(3)
+        cp(A("nx"), A("nf1"))
+        summed(4)
+        summed(0)
+        for k in (0, 3, 4, 5):
+            mm(2, WID[k], "qg", "sgs", 0, "qc", "scc", OFF[k], k == 0, False, n + "cs")
+
+        def rows(t):
+            k0 = 2 if 13 + t < MS else 3
+            a, b = OFF[k0], OFF[5] + 64
+            scan(A("rs", 4 * a + t, 4 * b, 4), A("rst", a - OFF[2], 640), A("ct", 4 * a + t, 4 * b, 4), 0.0, alu.mult, alu.add, n + "rs")
+
         if r == 0:
+            run(key_constants)
+        rows(0)
+        rows(1)
+        summed(1)
+        mm(2, WID[1], "qg", "sgs", 0, "qc", "scc", OFF[1], False, False, n + "cs")
+        rows(2)
+        rows(3)
+        summed(2)
+        mm(2, WID[2], "qg", "sgs", 0, "qc", "scc", OFF[2], False, True, n + "cs")
+        for k in (3, 4, 5):
+            e = 4 * (OFF[k] + (WID[k] if k < 5 else 64))
+            tt(A("bas", 21 - 4 * k, 25 - 4 * k), A("bas", 21 - 4 * k, 25 - 4 * k), A("rs", e - 4, e), alu.subtract, n + "bs")
+        if MS > 13:
+            e = 4 * OFF[3] - 4
+            tt(A("bas", 13, MS), A("bas", 13, MS), A("rs", e, e + MS - 13), alu.subtract, n + "bs")
+        tt(A("bas", MS, 24), A("bas", MS, 24), A("alt", MS, 24), alu.subtract, n + "bs")
+        if r == 0:
+            even(A("wa", 0, C3, 3), 0.0)
+            even(A("wa", 1, C3, 3), -LIFT)
+            even(A("cb", 0, C3, 3), -LIFT)
+            even(A("cb", 1, C3, 3), 0.0)
+            sc(A("mmul"), I(A("s16", 80, 96), A("po")))
+        else:
+            for k in range(4):
+                unpack(k)
+        scan(A("csc"), A("ps", 1024, 1024 + C), A("madd"), -1.0, alu.max, alu.add)
+        tt(A("bas"), A("bas"), A("csc", 15, C, 16), alu.add)
+        ts(A("o1"), A("bas"), 2.0, alu.mult)
+        sb_, sc_ = 24 - NVB, 24 - NVC
+        first = [
+            lambda: even(A("cd", 0, 4 * C, 4), -LIFT), lambda: even(A("cd", 1, 4 * C, 4), 0.0),
+        ]
+        key = two_steps("o1", "gi", "cb", "kc", 3, n + "s", [lambda: cp(A("pi"), A("bas"))],
+                        [lambda: ts(A("pj"), A("pi"), 1, alu.bitwise_and)] + (first if r == 0 else []))
+        own = A("ksc", 15, C, 16)
+        rank_keys(key, n + "B", {
+            -2: [lambda: ts(A("pc", sb_, 24), A("pj", sb_, 24), UP, alu.mult), lambda: ts(A("fl3"), own, PLACED, alu.is_gt, float(C3), alu.mult)],
+            -1: [lambda: ts(A("pq", 0, sb_), A("pj", 0, sb_), C - 1.5 + 2 * C, alu.add)],
+            0: [lambda: ts(A("pq", sb_, 24), A("pj", sb_, 24), -1.0, alu.mult, float(R2 + C), alu.add)],
+            1: [lambda: ts(A("fl4", 0, sb_), A("fl3", 0, sb_), 0.0, alu.is_gt, -2.0 * C, alu.mult), lambda: ts(A("fl4", sb_, 24), A("fl3", sb_, 24), 0.0, alu.is_gt, -float(C), alu.mult)],
+            2: [lambda: tt(A("nf1"), A("nf0"), A("fl3"), alu.max)],
+            3: [lambda: tt(A("pr"), A("pq"), A("fl4"), alu.add)],
+            4: [lambda: cp(A("nx"), A("nf1"))],
+            8: [lambda: quant(A("qe"), A("se"), A("eb"))] if r == 0 else [],
+        }, NVB)
+        if r == 0:
+            for k in range(4):
+                mm(4 + k, C, "qe", "se", 128 * k, "qx", "sx", 0)
+        ranked_v(1, "pr", NVB)
+        ranked_s(1, "pr", 0, sb_)
+        offsets_v("o2", NVB)
+        offsets_s("o2", 0, sb_)
+        if r == 0:
+            even(A("cd", 3, 4 * C, 4), 0.0)
+            sa(A("gj", 3, 4 * C, 4), A("iot"), act.Identity, -ZERO - 1000.0, -1.0)
+        key = two_steps("o2", "gj", "cd", "kd", 4, n + "t", [lambda: cp(A("pi"), A("o2"))],
+                        [lambda: ts(A("pj"), A("pi"), 1, alu.logical_shift_right, 1, alu.bitwise_and)] + ([lambda k=k: unpack(k) for k in range(4)] if r == 0 else []))
+        gaps = {
+            -2: [lambda: ts(A("pc", sc_, 24), A("pj", sc_, 24), UP, alu.mult), lambda: ts(A("pq", 0, sc_), A("pj", 0, sc_), -1.0, alu.mult, C - 0.5, alu.add)],
+            -1: [lambda: ts(A("pq", sc_, 24), A("pj", sc_, 24), R2 - 1.0, alu.add)],
+        }
+        if r == 0:
+            gaps[1] = [lambda: quant(A("qv"), A("sv"), A("vb"))]
+            for i in range(4):
+                gaps[2 + i] = border_constants[2 * i:2 * i + 2]
             sa(A("io4"), A("iot"), act.Identity, 0.0, 4.0)
-        ranked("oc2", -1, 191.5, 191.0, n + "oc", NVC)
-        cp(I(A("lb"), A("oc2")), A("io4"))
-        sc(A("colb", 2, C3, 3), I(A("io3" if r < R - 1 else "iot"), A("oc2")))
-        unpack(3)
-        for e in range(2):
-            sc(A("vn", C * e, C * e + C), I(A("colb"), A("nof", 24 * e, 24 * e + 24)))
-        scan(A("lsc"), A("lb"), A("madd"), -1.0, alu.max, alu.add)
-        for t in (0, 1, 2, 3):
-            ts(A("lo", 24 + 6 * t, 30 + 6 * t), A("lsc", C - K + 15, C, 16), col("cc", t), alu.add, grp=n + "lt")
-        ts(A("lo", 0, 24), A("lsc", 15, C, 16), col("cc", 0), alu.add, 0.25, alu.mult)
-        for t in range(4):
-            (cp if t < 3 else sc)(A("tb", 128 + t, 512, 4), I(A("xb"), A("lo", 24 + 6 * t, 30 + 6 * t)), n + "tb%d" % (t // 3))
+        rank_keys(key, n + "C", gaps, NVC)
+
+        def invert(a, b):
+            cp(I(A("gi", 0, 2 * C), A("oc2", a, b)), A("io4", 16 * a, 16 * b))
+
+        ranked_s(-1, "pq", 0, 8)
+        ranked_v(-1, "pq", NVC)
+        offsets_s("oc2", 0, 8)
+        offsets_v("oc2", NVC)
+        invert(0, 8)
+        invert(sc_, 24)
+        ranked_s(-1, "pq", 8, sc_)
+        offsets_s("oc2", 8, sc_)
+        invert(8, sc_)
+        def renamed(e):
+            sc(A("vn", C * e, C * e + C), I(A("wa"), A("nof", 24 * e, 24 * e + 24)))
+
+        if r < R - 1:
+            sa(A("wa", 2, C3, 3), I(A("h1"), A("oc2")), act.Identity, 2.0, 3.0)
+        else:
+            sc(A("wa", 2, C3, 3), I(A("h1"), A("oc2")))
+        renamed(0)
+        scan(A("lsb"), A("gi", 2 * (C - K), 2 * C, 2), A("md4"), -1.0, alu.max, alu.add)
+        scan(A("lsc"), A("gi", 0, 2 * C, 2), A("madd"), -1.0, alu.max, alu.add)
+        ts(A("lob"), A("lsb", 3, K, 4), CAT4, alu.add)
+        ts(A("lo"), A("lsc", 15, C, 16), CATCH, alu.add, 0.25, alu.mult)
+        cp(A("tb", 128, 128 + 16 * TBV), I(A("xb"), A("lob", 0, TBV)))
+        sc(A("tb", 128 + 16 * TBV, 512), I(A("xb"), A("lob", TBV, 24)))
         quant(A(qt, K, K + 128), A(st, K, K + 128), A("tb"))
         src_q, src_s = bits(A(qt, 128, K + 128), dt.uint8), A(st, 128, K + 128)
         dst_q, dst_s = T[qt][:, 0:K].bitcast(dt.uint8), T[st][:, 0:K]
@@ -392,33 +480,40 @@ def rank_program(g, core, T, topo):
             win = A("dh", C * k, C * k + C)
             sc(A("eh", C * k, C * k + C - K), I(win, A("lo", 0, (C - K) // 16)))
             tt(A("zb", 4 * K + k, 4 * C, 4), I(win, A("lo", K // 16, 24)), A("eh", C * k, C * k + C - K), alu.add, n + "zl")
+
+        def layer(a, b, bank, k, on):
+            o, i = A("xb", 4 * a + k, 4 * b, 4), A("ps", 512 * (bank + k), 512 * (bank + k) + b - a)
+            if on == "V":
+                ts(o, i, 0.0, alu.max, 0.03125, alu.mult)
+            else:
+                sa(o, i, act.Relu, 0.0, 0.03125)
+
         new_names(0)
-        for (a, b, bank) in ((128, C, 4), (0, 128, 0)):
-            w = b - a
-            if a == 0:
-                for k in range(4):
-                    mm(k, 128, "qe", "se", 128 * k, qt, st, 0, pre=(arr, 2 * neng) if k == 0 else None)
-                for k in range(4):
-                    tt(A("zb", k, 4 * K, 4), A("ps", 512 * k, 512 * k + K), A("eh", C * k, C * k + K), alu.add, n + "zr")
-            quant(A("qz", a, b), A("sz", a, b), A("zb", 4 * a, 4 * b))
-            if r < R - 1:
-                names_wrapped(0 if a else 1)
-            for k in range(4):
-                mm(bank + k, w, "qw", "sw", 128 * k, "qz", "sz", a)
-            for k in range(4):
-                o, i = A("xb", 4 * a + k, 4 * b, 4), A("ps", 512 * (bank + k), 512 * (bank + k) + w)
-                if k % 2:
-                    ts(o, i, 0.0, alu.max, 0.03125, alu.mult, grp=n + "xv%d" % a)
-                else:
-                    sa(o, i, act.Relu, 0.0, 0.03125, grp=n + "xs%d" % a)
-            quant(A("qx", a, b), A("sx", a, b), A("xb", 4 * a, 4 * b))
-            if a:
-                new_names(1)
-                sc(A("vn", 2 * C, C3), I(A("colb"), A("nof", 48, 72)))
-                if r == R - 1:
-                    dma("Y", T.oc[:, 4 * a:4 * b], bits(A("qx", a, b), dt.uint8), "outy")
+        renamed(1)
+        quant(A("qz", 128, C), A("sz", 128, C), A("zb", 512, 4 * C))
+        for k in range(4):
+            mm(4 + k, C - 128, "qw", "sw", 128 * k, "qz", "sz", 128)
+        for k in range(4):
+            mm(k, 128, "qe", "se", 128 * k, qt, st, 0, pre=(arr, 2 * neng) if k == 0 else None)
         if r < R - 1:
-            const("fw", 0, C, 0)
+            names_wrapped(0)
+        layer(128, C, 4, 0, "V")
+        layer(128, C, 4, 1, "S")
+        layer(128, C, 4, 2, "V")
+        layer(128, C, 4, 3, "S")
+        for k in range(4):
+            tt(A("zb", k, 4 * K, 4), A("ps", 512 * k, 512 * k + K), A("eh", C * k, C * k + K), alu.add, n + "zr")
+        new_names(1)
+        quant(A("qz", 0, 128), A("sz", 0, 128), A("zb", 0, 512))
+        for k in range(4):
+            mm(k, 128, "qw", "sw", 128 * k, "qz", "sz", 0)
+        quant(A("qx", 128, C), A("sx", 128, C), A("xb", 512, 4 * C))
+        if r == R - 1:
+            dma("Y", T.oc[:, 512:4 * C], bits(A("qx", 128, C), dt.uint8), "outy")
+        for k in range(4):
+            layer(0, 128, 0, k, "V" if k % 2 else "S")
+        quant(A("qx", 0, 128), A("sx", 0, 128), A("xb", 0, 512))
+        renamed(2)
 
     mm(4, C, "qv", "sv", 0, "qx", "sx", 0)
     new_names(2)

@@ -9,13 +9,24 @@ PIECES = ((0, 160), (160, 288), (288, C))
 C3 = 3 * C
 R2 = C // 2
 R1 = C * R2
-TOP = float((C + 1) * R1)
-LIFT = 2.0 ** 25
+V1, TURNS, C1 = 10, 1, C + 1
+LATEB = 23
+CUTS = (18,)
+PARTS = ((0, 18), (18, 24))
+LAYER = ("VSVS", "SVSV")
+BASE, LIFT = 2048.0, 2.0 ** 19 + 2.0 ** 15
+FLOOR1 = C * BASE - (C + 1) * C
+PLACE1 = (C + 1) * BASE - LIFT
+FLOOR2 = PLACE1 - (C + 2) * C
+LIFT2 = (FLOOR2 + C) * R2
+HALF = 0.5 - 1 / BASE
 ZERO = float(R2 * R1 - R2 * R2 - R2 - R2 // 2)
 EVEN = 1.5 * 2 ** 24
 HUGE, CB, BIG = 1e29, 2048.0, 2.0 ** 60
 WID = (384, 320, 256, 192, 128, 128)
 OFF = (0, 384, 704, 960, 1152, 1280)
+CYCLE, FIXED, GATHER, SCATTER, PE = 0.00083, 0.02, 1.56, 3.8, 0.0007
+WAKE, SLACK, ISSUE, REMOTE, FIRST = 0.2, 0.1, 0.1, 2.6, 1.0
 F32, BF, I32, U16, Q4, U8 = "float32", "bfloat16", "int32", "uint16", "float8_e4m3fn_x4", "uint8"
 
 
@@ -32,15 +43,15 @@ SCRATCH = {
     "qu": _sb(128, Q4), "su": _sb(128, U8), "qu2": _sb(128, Q4), "su2": _sb(128, U8), "qv": _sb(128, Q4), "sv": _sb(128, U8),
     "qw": _sb(512, Q4), "sw": _sb(512, U8), "qe": _sb(512, Q4), "se": _sb(512, U8), "eb": _sb(2048, BF),
     "one5": _sb(512, BF), "half": _sb(512, BF), "gd": _sb(512, BF), "gd2": _sb(512, BF), "qg": _sb(128, Q4), "sgs": _sb(128, U8),
-    "ct": _sb(4 * 1408, BF), "rs": _sb(4 * 1408, BF), "qc": _sb(1408, Q4), "scc": _sb(1408, U8), "csc": _sb(C), "rst": _sb(640, BF),
+    "ct": _sb(4 * 1408, BF), "rs": _sb(4 * 1408, BF), "qc": _sb(1408, Q4), "scc": _sb(1408, U8), "csc": _sb(C), "rb": _sb(C), "rst": _sb(640, BF),
     "pmi": _sb(4, I32), "pmj": _sb(6, I32), "pm": _sb(6), "uoi": _sb(8, I32), "uo": _sb(8, U16), "po": _sb(24, U16),
     "iot": _sb(C), "io3": _sb(C), "io4": _sb(C), "tm": _sb(C), "md": _sb(C), "hm": _sb(C), "hn": _sb(C), "hd": _sb(C),
     "rch": _sb(C, BF), "madd": _sb(C), "mmul": _sb(C), "tm4": _sb(K), "ma4": _sb(K), "mb4": _sb(K), "md4": _sb(K),
     "s16": _sb(96), "cc": _sb(10), "cst": _sb(24), "fl": _sb(96), "fl2": _sb(48), "fl3": _sb(24), "fl4": _sb(24),
     "t1": _sb(C), "t2": _sb(C), "cm": _sb(C), "hs": _sb(C, BF),
-    "h1": _sb(4 * C), "wa": _sb(C3 + 8), "wb": _sb(C3 + 8), "gi": _sb(C3), "kc": _sb(C3), "cb": _sb(C3),
+    "h1": _sb(4 * C + 8), "wa": _sb(C3 + 8), "wb": _sb(C3 + 8), "gi": _sb(C3), "kc": _sb(C3), "cb": _sb(C3),
     "gj": _sb(4 * C), "kd": _sb(4 * C), "cd": _sb(4 * C), "ksc": _sb(C),
-    "cmp": _sb(10 * C, BF), "scn": _sb(10 * C, BF), "low": _sb(NM * C, BF), "sg": _sb(16 * C, BF), "jk": _sb(C, BF),
+    "cmp": _sb(10 * C1, BF), "scn": _sb(10 * C1, BF), "low": _sb(NM * C1, BF), "pb": _sb(24), "sg": _sb(18 * C, BF), "jk": _sb(C, BF),
     "col": _sb(4), "acc": _sb(24), "alt": _sb(24), "bas": _sb(24), "pi": _sb(24, I32), "pj": _sb(24, I32),
     "pc": _sb(24), "pq": _sb(24), "pr": _sb(24), "thr": _sb(24), "tw": _sb(24),
     "o1": _sb(24, U16), "o2": _sb(24, U16), "oc2": _sb(24, U16), "lo": _sb(24, U16), "lob": _sb(24, U16),
@@ -70,79 +81,90 @@ def rank_program(g, core, T, topo):
     def A(name, a=0, b=None, s=1):
         if b is None:
             b = SCRATCH[name][1][1]
+        n, narrow = len(range(a, b, s)), SCRATCH[name][2] in (BF, U16)
         if name == "ps":
-            return (T[name][:, a:b], [("ps", 1 << (a // 512))])
+            return (T[name][:, a:b], [("ps", 1 << (a // 512))], [], n, narrow)
         m = ((1 << (b - a)) - 1) << a if s == 1 else sum(1 << c for c in range(a, b, s))
-        return (T[name][:, a:b] if s == 1 else T[name][:, a:b:s], [(name, m)])
+        return (T[name][:, a:b] if s == 1 else T[name][:, a:b:s], [(name, m)], [], n, narrow)
 
     def col(name, c):
         return A(name, c, c + 1)
 
     def I(win, off):
-        return (win[0].indirect(off[0]), win[1], off[1])
+        return (win[0].indirect(off[0]), win[1], off[1], 16 * off[3], False)
 
     def bits(a, d):
-        return (a[0].bitcast(d), a[1])
+        return (a[0].bitcast(d),) + a[1:]
 
     def ap(x):
         return x[0] if isinstance(x, tuple) else x
 
-    def add(q, fn, outs, ins, grp=None, dma=False, pre=None, chain=False):
+    def add(q, fn, outs, ins, us, grp=None, dma=False, pre=None, chain=False):
         rd, wr = [], []
         for x in ins:
             if isinstance(x, tuple):
-                rd += x[1] + (x[2] if len(x) > 2 else [])
+                rd += x[1] + x[2]
         for x in outs:
             wr += x[1]
-            rd += x[2] if len(x) > 2 else []
-        ops.append({"q": q, "fn": fn, "rd": rd, "wr": wr, "grp": grp if grp else "#%d" % len(ops), "dma": dma, "pre": pre, "chain": chain})
+            rd += x[2]
+        ops.append({"q": q, "fn": fn, "rd": rd, "wr": wr, "grp": grp if grp else "#%d" % len(ops), "dma": dma, "pre": pre, "chain": chain, "us": us})
+
+    def span(o, ins, per=1.0):
+        if o[2]:
+            return 0.05 + CYCLE * SCATTER * o[3]
+        if ins[0][2]:
+            return 0.06 + CYCLE * GATHER * o[3]
+        return FIXED + CYCLE * max(64, per * o[3])
+
+    def fast(*xs):
+        return 0.5 if all(x[4] for x in xs) else 1.0
 
     def ts(o, i, s1, op0, s2=None, op1=None, grp=None):
         if op1 is None:
-            add("V", lambda: g.vector.tensor_scalar(o[0], i[0], ap(s1), None, op0), [o], [i, s1], grp)
+            add("V", lambda: g.vector.tensor_scalar(o[0], i[0], ap(s1), None, op0), [o], [i, s1], span(o, [i], fast(o, i)), grp)
         else:
-            add("V", lambda: g.vector.tensor_scalar(o[0], i[0], ap(s1), ap(s2), op0, op1), [o], [i, s1, s2], grp)
+            add("V", lambda: g.vector.tensor_scalar(o[0], i[0], ap(s1), ap(s2), op0, op1), [o], [i, s1, s2], span(o, [i], fast(o, i)), grp)
 
     def tt(o, a, b, op, grp=None):
-        add("V", lambda: g.vector.tensor_tensor(o[0], a[0], b[0], op), [o], [a, b], grp)
+        add("V", lambda: g.vector.tensor_tensor(o[0], a[0], b[0], op), [o], [a, b], span(o, [a], 1.0 if "ps" in (a[1][0][0], b[1][0][0]) else 2.0), grp)
 
     def cp(o, i, grp=None):
-        add("V", lambda: g.vector.tensor_copy(o[0], i[0]), [o], [i], grp)
+        add("V", lambda: g.vector.tensor_copy(o[0], i[0]), [o], [i], span(o, [i], fast(o, i)), grp)
 
     def scan(o, d0, d1, init, op0, op1, grp=None):
-        add("V", lambda: g.vector.tensor_tensor_scan(o[0], d0[0], d1[0], init, op0, op1), [o], [d0, d1], grp)
+        add("V", lambda: g.vector.tensor_tensor_scan(o[0], d0[0], d1[0], init, op0, op1), [o], [d0, d1], span(o, [d0], fast(o, d0, d1)), grp)
 
     def fill(o, v, grp=None):
-        add("V", lambda: g.vector.memset(o[0], v), [o], [], grp)
+        add("V", lambda: g.vector.memset(o[0], v), [o], [], span(o, [o], fast(o)), grp)
 
     def quant(q, s, i):
-        add("V", lambda: g.vector.quantize_mx(q[0], s[0], i[0]), [q, s], [i])
+        add("V", lambda: g.vector.quantize_mx(q[0], s[0], i[0]), [q, s], [i], 0.012 + 0.00022 * i[3])
 
     def sa(o, i, f, bias=0.0, scale=1.0, acc=None, grp=None):
         if acc is None:
-            add("S", lambda: g.scalar.activation(o[0], i[0], f, bias=ap(bias), scale=ap(scale)), [o], [i, bias, scale], grp)
+            add("S", lambda: g.scalar.activation(o[0], i[0], f, bias=ap(bias), scale=ap(scale)), [o], [i, bias, scale], span(o, [i]), grp)
         else:
-            add("S", lambda: g.scalar.activation(o[0], i[0], f, bias=ap(bias), scale=ap(scale), accum_out=acc[0]), [o, acc], [i, bias, scale], grp)
+            add("S", lambda: g.scalar.activation(o[0], i[0], f, bias=ap(bias), scale=ap(scale), accum_out=acc[0]), [o, acc], [i, bias, scale], span(o, [i]) + 0.02, grp)
 
     def sc(o, i, grp=None):
-        add("S", lambda: g.scalar.activation(o[0], i[0], act.Copy), [o], [i], grp)
+        add("S", lambda: g.scalar.activation(o[0], i[0], act.Copy), [o], [i], span(o, [i]), grp)
 
     def mm(bank, n, wq, ws, c0, xq, xs, x0, start=True, stop=True, grp=None, pre=None):
         o, a, b = A("ps", 512 * bank, 512 * bank + n), A(wq, c0, c0 + 128), A(ws, c0, c0 + 128)
         c, d = A(xq, x0, x0 + n), A(xs, x0, x0 + n)
-        add("P", lambda: g.tensor.matmul_mx(o[0], a[0], b[0], c[0], d[0], start, stop), [o], [a, b, c, d], grp, pre=pre, chain=not start)
+        add("P", lambda: g.tensor.matmul_mx(o[0], a[0], b[0], c[0], d[0], start, stop), [o], [a, b, c, d], PE * (n + 16), grp, pre=pre, chain=not start)
 
-    def dma(q, o, i, grp=None):
-        add(q, lambda: eng[q].dma_start(ap(o), ap(i)), [o] if isinstance(o, tuple) else [], [i], grp, dma=True)
+    def dma(q, o, i, grp=None, us=1.5, behind=None):
+        add(q, lambda: eng[q].dma_start(ap(o), ap(i)), [o] if isinstance(o, tuple) else [], [i, behind], us, grp, dma=True)
 
     def iota(o, pat, base, cm, flag=True):
         if flag:
-            add("G", lambda: g.iota(o[0], pat, base, cm, allow_small_or_imprecise_dtypes=True), [o], [])
+            add("G", lambda: g.iota(o[0], pat, base, cm, allow_small_or_imprecise_dtypes=True), [o], [], 0.13 + 2 * CYCLE * o[3])
         else:
-            add("G", lambda: g.iota(o[0], pat, base, cm), [o], [])
+            add("G", lambda: g.iota(o[0], pat, base, cm), [o], [], 0.13 + 2 * CYCLE * o[3])
 
     def select(o, i, pat, op, base, cm, other=0.0, grp=None):
-        add("G", lambda: g.affine_select(o[0], i[0], pat, op, other, base, cm), [o], [i], grp)
+        add("G", lambda: g.affine_select(o[0], i[0], pat, op, other, base, cm), [o], [i], 0.17 + 2 * CYCLE * o[3], grp)
 
     def run(calls):
         for f in calls:
@@ -151,7 +173,7 @@ def rank_program(g, core, T, topo):
     ones = A("one5", 0, C)
     CATCH, CAT4, UP, DOWN, PLACED, LANE0, ENDF = (col("cc", c) for c in range(7))
     RUNS = [[0, 24], [1, 16]]
-    dma("Y", A("xb"), T.x[:])
+    dma("Y", A("xb"), T.x[:], us=2.6)
     dma("S", A("ub"), T.u[:])
     dma("S", A("nbi"), T.nb[:])
     iota(A("pmi", 0, 2), [[15, 2]], 0, 1, False)
@@ -164,9 +186,9 @@ def rank_program(g, core, T, topo):
     for k in range(5):
         dma("Y", A("ct", 4 * (OFF[k] + WID[k] - 48), 4 * (OFF[k] + WID[k])), A("tb", 0, 192), "ctz")
     dma("Y", A("ct", 4 * (OFF[5] + 16), 4 * (OFF[5] + 128)), A("tb", 0, 448), "ctz")
-    dma("Y", bits(A("qw"), dt.uint8), T.wc[:], "w")
-    dma("Y", A("sw"), T.ws[:], "w")
-    dma("Y", A("vb"), T.v[:])
+    dma("Y", bits(A("qw"), dt.uint8), T.wc[:], "w", behind=A("xb"))
+    dma("Y", A("sw"), T.ws[:], "w", behind=A("xb"))
+    dma("Y", A("vb"), T.v[:], behind=A("xb"))
     ts(A("pmj", 0, 2), A("pmi", 0, 2), 15, alu.bitwise_and)
     sa(A("io3"), A("iot"), act.Identity, 2.0, 3.0)
     cp(A("pm", 0, 2), A("pmj", 0, 2))
@@ -185,12 +207,7 @@ def rank_program(g, core, T, topo):
     iota(A("rst"), [[0, 640]], 1, 0)
     for c in (256, 448, 576):
         iota(col("rst", c), [[0, 1]], 0, 0)
-    iota(A("h1"), [[1, 2 * C], [0, 2]], 0, 0)
-    iota(A("low"), [[0, NM], [1, C]], -R2, 0)
-    fill(A("half"), 0.5)
-    for b in range(4):
-        select(A("eb", 512 * b, 512 * b + 512), A("half"), [[-1, 512]], alu.is_equal, b, 4, 0.0, "eb")
-    iota(A("tm4"), [[0, 24], [1, 4]], 0, 0)
+    iota(A("h1"), [[1, 2 * C + 4], [0, 2]], 0, 0)
     quant(A("qu"), A("su"), A("ub"))
     ts(LANE0, col("pm", 0), 0.0, alu.is_equal)
     tt(A("s16", 64, 80), A("s16", 0, 16), A("s16", 16, 32), alu.add)
@@ -203,7 +220,7 @@ def rank_program(g, core, T, topo):
     ts(A("cst"), A("iot", 0, 24), 16.0, alu.mult, col("pm", 0), alu.subtract)
     quant(A("qx"), A("sx"), A("xb"))
     ts(A("nof", 72, 96), A("nf1"), 3.0, alu.mult, 2.0, alu.add)
-    ts(A("cst"), A("cst"), CATCH, alu.add, 15.0 + C, alu.add)
+    ts(A("cst"), A("cst"), 17.0 + C, alu.add)
 
     key_constants = [
         lambda: ts(UP, LANE0, -BIG, alu.mult, BIG, alu.add),
@@ -213,8 +230,8 @@ def rank_program(g, core, T, topo):
         lambda: ts(UP, UP, 1 / BIG, alu.max),
         lambda: ts(ENDF, ENDF, 1 / (BIG * BIG), alu.max),
         lambda: tt(A("s16", 80, 96), A("s16", 32, 48), A("s16", 48, 64), alu.add),
-        lambda: fill(A("wa", C3, C3 + 8), 0.0),
-        lambda: fill(A("wb", C3, C3 + 8), -LIFT),
+        lambda: fill(A("wa", C3, C3 + 8), BASE),
+        lambda: fill(A("wb", C3, C3 + 8), PLACE1),
         lambda: ts(col("s16", 95), col("s16", 95), ENDF, alu.mult),
         lambda: sa(DOWN, UP, act.Identity, 0.0, -1.0),
         lambda: sa(PLACED, UP, act.Identity, 0.0, -ZERO - 500.0),
@@ -231,7 +248,7 @@ def rank_program(g, core, T, topo):
     ]
 
     def even(o, v):
-        sa(o, A("iot"), act.Identity, v, 0.0)
+        iota(o, [[0, C]], int(v), 0)
 
     def new_names(e):
         sc(A("nbv", e, C3, 3), I(A("vn", C * e, C * e + C), A("lo")))
@@ -244,88 +261,80 @@ def rank_program(g, core, T, topo):
 
     def step(win, first, lifts, scale, got, ctl, out, w, tag, after):
         ts(A(got, 0, w * C, w), I(A(win), A("nx")), *first)
+        run(after.get(-1, []))
         for p, (a, b) in enumerate(PIECES):
             for e in (1, 2):
                 sa(A(got, w * a + e, w * b, w), I(A(win), A("nof", 24 * e + a // 16, 24 * e + b // 16)), act.Identity, lifts[e - 1], scale, grp=tag + str(a))
-            scan(A(out, w * a, w * b), A(got, w * a, w * b), A(ctl, w * a, w * b), -LIFT, alu.max, alu.add)
+            scan(A(out, w * a, w * b), A(got, w * a, w * b), A(ctl, w * a, w * b), 0.0, alu.max, alu.add)
             run(after.get(p, []))
 
-    def two_steps(o, got, ctl, out, w, tag, gap_a, gap_b):
-        ts(A("wa", 2, C3 // 2, 3), I(A("h1"), A(o, 0, 12)), -float(R2), alu.mult)
-        sa(A("wa", C3 // 2 + 2, C3, 3), I(A("h1"), A(o, 12, 24)), act.Identity, 0.0, -float(R2))
-        half_digit = lambda: sa(A(ctl, 2, w * C, w), A("wa", 2, C3, 3), act.Identity, -ZERO, 0.4995 / R2)
-        step("wa", (float(C), alu.mult, -TOP, alu.max), (0.0, -LIFT), float(C), "gi", "wa", "wb", 3, tag + "a", {2: [half_digit] + gap_a})
-        key = A(out, w - 1, w * C, w)
-        a = PIECES[0][1]
+    def two_steps(got, ctl, out, w, tag, gaps):
+        half_digit = lambda: sa(A(ctl, 2, w * C, w), A("wa", 2, C3, 3), act.Identity, -ZERO - BASE * HALF, HALF)
+        step("wa", (float(C), alu.mult, FLOOR1, alu.max), (0.0, -LIFT), float(C), "gi", "wa", "wb", 3, tag + "a", {-1: gaps[0], 2: [half_digit] + gaps[1]})
         catch = lambda a, b: scan(A("ksc", a, b), A(out, w * a + w - 1, w * b, w), A("mmul", a, b), 0.0, alu.add, alu.mult)
-        step("wb", (-R1 - TOP - LIFT, alu.max, TOP + 2 * LIFT, alu.add), (TOP + LIFT, TOP + LIFT), 1.0, got, ctl, out, w, tag + "b",
-             {1: [lambda: catch(0, a)], 2: gap_b + [lambda: catch(a, C)]})
-        return key
+        step("wb", (FLOOR2, alu.max, float(R2), alu.mult), (-LIFT2, -LIFT2), float(R2), got, ctl, out, w, tag + "b",
+             {-1: gaps[2], 1: [lambda: catch(0, 16 * V1)], 2: gaps[3] + [lambda: catch(16 * V1, C)]})
+        return A(out, w - 1, w * C, w)
 
-    def rank_keys(key, tag, between, nv):
-        ns = 24 - nv
-        for m in range(ns):
-            sa(A("sg", C * m, C * m + C), key, act.Sign, col("ksc", 16 * m + 15), DOWN, col("acc", m), tag + "s%d" % min(m // 8, 1))
-        run(between.get(-2, []))
-        tt(A("thr", ns, 24), A("ksc", 16 * ns + 15, C, 16), A("pc", ns, 24), alu.subtract)
-        run(between.get(-1, []))
+    def rank_keys(key, tag, first, between, nv, cuts):
+        for m in range(nv, 24):
+            sa(A("sg", C * (m - nv), C * (m - nv) + C), key, act.Sign, col("ksc", 16 * m + 15), DOWN, col("acc", m), tag + "s%d" % sum(m >= c for c in cuts))
+        tt(A("thr", 0, nv), A("ksc", 15, 16 * nv, 16), A("pc", 0, nv), alu.subtract)
+        ts(A("cmp", 0, C1 * nv, C1), A("pj", 0, nv), -1.0, alu.mult)
         for i in range(nv):
-            ts(A("cmp", C * i, C * i + C), key, UP, alu.mult, col("thr", ns + i), alu.is_gt, tag + "c%d" % (i // NM))
-            run(between.get(i, []))
+            ts(A("cmp", C1 * i + 1, C1 * i + C1), key, UP, alu.mult, col("thr", i), alu.is_gt, tag + "c%d" % (i // NM))
+            run(first[i:i + 1])
+        run(between)
         for i in range(0, nv, NM):
-            w = C * min(NM, nv - i)
-            scan(A("scn", C * i, C * i + w), A("low", 0, w), A("cmp", C * i, C * i + w), -float(R2), alu.min, alu.add, tag + "n")
-
-    def ranked_v(sign, p, nv):
-        ends = A("scn", C - 1, C * nv, C)
-        if sign > 0:
-            tt(A("tw", 24 - nv, 24), ends, A(p, 24 - nv, 24), alu.add)
-        else:
-            tt(A("tw", 24 - nv, 24), A(p, 24 - nv, 24), ends, alu.subtract)
-
-    def ranked_s(sign, p, a, b):
-        tt(A("tw", a, b), A(p, a, b), A("acc", a, b), alu.subtract if sign > 0 else alu.add)
-
-    def offsets_v(o, nv):
-        ts(A(o, 24 - nv, 24), A("tw", 24 - nv, 24), 2.0, alu.mult)
-
-    def offsets_s(o, a, b):
-        ts(A(o, a, b), A("tw", a, b), EVEN, alu.add, EVEN, alu.subtract)
+            w = C1 * min(NM, nv - i)
+            scan(A("scn", C1 * i, C1 * i + w), A("low", 0, w), A("cmp", C1 * i, C1 * i + w), -float(R2), alu.min, alu.add, tag + "n")
+        return A("scn", C, C1 * nv, C1)
 
     ROOT, RT3 = col("col", 0), col("col", 1)
 
-    def slot(m):
+    def slot(m, a=0, b=None):
         k, t = 5 - (m - 1) // 4, (m - 1) % 4
-        return A("ct", 4 * OFF[k] + t, 4 * (OFF[k] + 16 * m), 4)
+        return A("ct", 4 * (OFF[k] + a) + t, 4 * (OFF[k] + (b or 16 * m)), 4)
 
     for r in range(R):
         n = "r%d" % r
         qt, st = "qt%d" % r, "st%d" % r
-        mm(0, C, "qu2", "su2", 0, "qx", "sx", 0)
-        mm(1, C, "qu2", "su2", 0, "qx", "sx", 0)
+        for (bank, w) in (((1, 128), (0, C)) if r else ((0, C), (1, C))):
+            mm(bank, w, "qu2", "su2", 0, "qx", "sx", 0)
+
+        def parts(b, late, early):
+            return [(128, b, 512 * early - 128), (0, 128, 512 * late)] if r and b > 128 else [(0, b, 512 * late)]
+
         sv = A("ps", 0, C)
 
         def unpack(k):
             sc(A("dh", C * k, C * k + C), A("ps", 512 * (4 + k), 512 * (4 + k) + C))
 
-        if r:
-            for k in range(4):
-                mm(4 + k, C, "qe", "se", 128 * k, "qx", "sx", 0)
-            names_wrapped(1)
-            new_names(2)
-        for (a, b) in ((256, C), (0, 256)):
-            tt(A("t1", a, b), A("ps", a, b), A("hm", a, b), alu.min)
-        for (a, b) in ((256, C), (0, 256)):
+        def masked(a, b, c0):
+            tt(A("t1", a, b), A("ps", c0 + a, c0 + b), A("hm", a, b), alu.min)
+
+        def held(a, b):
             scan(A("t2", a, b), A("hd", a, b), A("t1", a, b), 0.0, alu.min, alu.max)
-        scan(A("cm"), sv, ones, -HUGE, alu.max, alu.mult)
+
+        if r:
+            masked(0, 128, 0)
+            scan(A("cm"), sv, ones, -HUGE, alu.max, alu.mult)
+            held(0, 128)
+        else:
+            masked(256, C, 0)
+            masked(0, 256, 0)
+            held(256, C)
+            held(0, 256)
+            scan(A("cm"), sv, ones, -HUGE, alu.max, alu.mult)
 
         def runs(k):
             return range(21 - 4 * k, min(25 - 4 * k, 24))
 
-        def signs(k):
+        def signs(k, which):
             for m in runs(k):
                 if m >= MS:
-                    sa(A("sg", C * (m - 8), C * (m - 8) + 16 * m), A("ps", 512, 512 + 16 * m), act.Sign, col("t2", 16 * m + 15), -1.0, grp=n + "p%d" % k)
+                    for (a, b, c0) in parts(16 * m, 1, 5)[which]:
+                        sa(A("sg", C * (m - 8) + a, C * (m - 8) + b), A("ps", c0 + a, c0 + b), act.Sign, col("t2", 16 * m + 15), -1.0, grp=n + "p%d%d" % (k, a))
 
         def lower(k):
             for m in runs(k):
@@ -336,19 +345,26 @@ def rank_program(g, core, T, topo):
             w = WID[k] if k < 4 else (256 if r == 0 else 192)
             quant(A("qc", OFF[k], OFF[k] + w), A("scc", OFF[k], OFF[k] + w), A("ct", 4 * OFF[k], 4 * (OFF[k] + w)))
 
-        signs(0)
+        late = slice(-1, None)
+        for k in range(3):
+            signs(k, slice(0, -1))
+        signs(0, late)
         sa(A("jk"), A("cm"), act.Sign, col("cm", C - 1), -1.0, ROOT)
-        signs(1)
+        signs(1, late)
         sa(RT3, ROOT, act.Identity, 2.0, 3.0)
         lower(0)
-        signs(2)
+        signs(2, late)
         lower(1)
         lower(2)
-        tt(slot(24), sv, A("t2"), alu.is_le)
+        for (a, b, c0) in parts(C, 0, 4):
+            tt(slot(24, a, b), A("ps", c0 + a, c0 + b), A("t2", a, b), alu.is_le)
+        if r:
+            for k in range(4):
+                mm(4 + k, C, "qe", "se", 128 * k, "qx", "sx", 0)
         small = {
-            12: [lambda e=e: names_wrapped(e) for e in range(2 if r else 0, 3)],
-            11: [lambda e=e: names_pick(e) for e in range(3)],
-            10: [lambda: scan(A("hs"), A("rch"), slot(24), 0.0, alu.mult, alu.add)],
+            12: [lambda e=e: names_wrapped(e) for e in range(3)],
+            11: [lambda: scan(A("hs"), A("rch"), slot(24), 0.0, alu.mult, alu.add)],
+            10: [lambda: ts(A("nof", 0, 72), A("nsc", 15, C3, 16), CATCH, alu.add)],
             9: [lambda: cp(A("nf0"), A("nof", 0, 24))],
             8: [lambda: tt(A("bas"), A("cst"), A("hs", 15, C, 16), alu.subtract)],
             6: [lambda: ts(A("fl"), A("nof"), RT3, alu.is_equal, float(C3), alu.mult)],
@@ -377,14 +393,10 @@ def rank_program(g, core, T, topo):
 
         if r == 0:
             run(key_constants)
-        rows(0)
-        rows(1)
+        for t in range(4):
+            rows(t)
         summed(1)
         mm(2, WID[1], "qg", "sgs", 0, "qc", "scc", OFF[1], False, False, n + "cs")
-        rows(2)
-        rows(3)
-        summed(2)
-        mm(2, WID[2], "qg", "sgs", 0, "qc", "scc", OFF[2], False, True, n + "cs")
         for k in (3, 4, 5):
             e = 4 * (OFF[k] + (WID[k] if k < 5 else 64))
             tt(A("bas", 21 - 4 * k, 25 - 4 * k), A("bas", 21 - 4 * k, 25 - 4 * k), A("rs", e - 4, e), alu.subtract, n + "bs")
@@ -392,77 +404,88 @@ def rank_program(g, core, T, topo):
             e = 4 * OFF[3] - 4
             tt(A("bas", 13, MS), A("bas", 13, MS), A("rs", e, e + MS - 13), alu.subtract, n + "bs")
         tt(A("bas", MS, 24), A("bas", MS, 24), A("alt", MS, 24), alu.subtract, n + "bs")
+        summed(2)
+        mm(2, WID[2], "qg", "sgs", 0, "qc", "scc", OFF[2], False, True, n + "cs")
+        ts(A("o1"), A("bas"), 2.0, alu.mult)
         if r == 0:
             even(A("wa", 0, C3, 3), 0.0)
             even(A("wa", 1, C3, 3), -LIFT)
-            even(A("cb", 0, C3, 3), -LIFT)
+        ts(A("rb", 0, R2), I(A("h1"), A("o1", 0, 12)), -1.0, alu.mult, BASE + 2, alu.add)
+        sa(A("rb", R2, C), I(A("h1"), A("o1", 12, 24)), act.Identity, BASE + 2, -1.0)
+        tt(A("wa", 2, C3, 3), A("rb"), A("ps", 1024, 1024 + C), alu.subtract)
+        if r == 0:
+            even(A("cb", 0, C3, 3), -LIFT2)
             even(A("cb", 1, C3, 3), 0.0)
             sc(A("mmul"), I(A("s16", 80, 96), A("po")))
-        else:
-            for k in range(4):
-                unpack(k)
-        scan(A("csc"), A("ps", 1024, 1024 + C), A("madd"), -1.0, alu.max, alu.add)
-        tt(A("bas"), A("bas"), A("csc", 15, C, 16), alu.add)
-        ts(A("o1"), A("bas"), 2.0, alu.mult)
-        sb_, sc_ = 24 - NVB, 24 - NVC
-        first = [
-            lambda: even(A("cd", 0, 4 * C, 4), -LIFT), lambda: even(A("cd", 1, 4 * C, 4), 0.0),
-        ]
-        key = two_steps("o1", "gi", "cb", "kc", 3, n + "s", [lambda: cp(A("pi"), A("bas"))],
-                        [lambda: ts(A("pj"), A("pi"), 1, alu.bitwise_and)] + (first if r == 0 else []))
+            iota(A("low"), [[0, NM], [1, C1]], -R2, 0)
+            fill(A("half"), 0.5)
+            for b in range(4):
+                select(A("eb", 512 * b, 512 * b + 512), A("half"), [[-1, 512]], alu.is_equal, b, 4, 0.0, "eb")
+            iota(A("tm4"), [[0, 24], [1, 4]], 0, 0)
+        key = two_steps("gi", "cb", "kc", 3, n + "s", ([], [], [], [
+            lambda: scan(A("csc", 0, R2), A("ps", 1024, 1024 + R2), A("madd", 0, R2), -1.0, alu.max, alu.add),
+            lambda: scan(A("csc", R2, C), A("ps", 1024 + R2, 1024 + C), A("madd", R2, C), -1.0, alu.max, alu.add),
+            lambda: tt(A("pi"), A("csc", 15, C, 16), A("bas"), alu.add),
+            lambda: ts(A("pj"), A("pi"), 1, alu.bitwise_and),
+            lambda: ts(A("pc"), A("pj"), UP, alu.mult)]))
         own = A("ksc", 15, C, 16)
-        rank_keys(key, n + "B", {
-            -2: [lambda: ts(A("pc", sb_, 24), A("pj", sb_, 24), UP, alu.mult), lambda: ts(A("fl3"), own, PLACED, alu.is_gt, float(C3), alu.mult)],
-            -1: [lambda: ts(A("pq", 0, sb_), A("pj", 0, sb_), C - 1.5 + 2 * C, alu.add)],
-            0: [lambda: ts(A("pq", sb_, 24), A("pj", sb_, 24), -1.0, alu.mult, float(R2 + C), alu.add)],
-            1: [lambda: ts(A("fl4", 0, sb_), A("fl3", 0, sb_), 0.0, alu.is_gt, -2.0 * C, alu.mult), lambda: ts(A("fl4", sb_, 24), A("fl3", sb_, 24), 0.0, alu.is_gt, -float(C), alu.mult)],
-            2: [lambda: tt(A("nf1"), A("nf0"), A("fl3"), alu.max)],
-            3: [lambda: tt(A("pr"), A("pq"), A("fl4"), alu.add)],
-            4: [lambda: cp(A("nx"), A("nf1"))],
-            8: [lambda: quant(A("qe"), A("se"), A("eb"))] if r == 0 else [],
-        }, NVB)
+        ends = rank_keys(key, n + "B", [
+            lambda: ts(A("pb", NVB, 24), A("pj", NVB, 24), C - 1.0, alu.add),
+            lambda: ts(A("fl4"), own, PLACED, alu.is_le, 2.0 * C, alu.mult),
+            lambda: ts(A("fl3"), own, PLACED, alu.is_gt, float(C3), alu.mult),
+            lambda: tt(A("pr", NVB, 24), A("pb", NVB, 24), A("fl4", NVB, 24), alu.add),
+            lambda: tt(A("nf1"), A("nf0"), A("fl3"), alu.max),
+            lambda: cp(A("nx"), A("nf1"))], [], NVB, range(LATEB, 24))
+        tt(A("tw", NVB, LATEB), A("pr", NVB, LATEB), A("acc", NVB, LATEB), alu.subtract)
+        cp(A("o2", NVB, LATEB), A("tw", NVB, LATEB))
+        ts(A("pb", 0, NVB), A("ksc", 15, 16 * NVB, 16), PLACED, alu.is_le, float(C), alu.mult)
+        tt(A("tw", 0, NVB), A("pb", 0, NVB), ends, alu.add)
+        ts(A("o2", 0, NVB), A("tw", 0, NVB), 2.0, alu.mult, float(C), alu.add)
+        for m in range(LATEB, 24):
+            ts(col("o2", m), col("acc", m), -1.0, alu.mult, col("pr", m), alu.add, n + "o2")
+        ts(A("wa", 2, C3 // 2, 3), I(A("h1"), A("o2", 0, 12)), -1.0, alu.mult, BASE, alu.add)
+        sa(A("wa", C3 // 2 + 2, C3, 3), I(A("h1"), A("o2", 12, 24)), act.Identity, BASE, -1.0)
         if r == 0:
+            for t, v in ((0, -LIFT2), (1, 0.0), (3, 0.0)):
+                even(A("cd", t, 4 * C, 4), v)
+            iota(A("gj", 3, 4 * C, 4), [[-1, C]], -int(ZERO) - 1000, 0)
+        key = two_steps("gj", "cd", "kd", 4, n + "t", ([], [], [], [
+            lambda: cp(A("pi"), A("o2")),
+            lambda: ts(A("pj"), A("pi"), 1, alu.logical_shift_right, 1, alu.bitwise_and),
+            lambda: ts(A("pc"), A("pj"), UP, alu.mult)]))
+        if r == 0:
+            quant(A("qe"), A("se"), A("eb"))
             for k in range(4):
                 mm(4 + k, C, "qe", "se", 128 * k, "qx", "sx", 0)
-        ranked_v(1, "pr", NVB)
-        ranked_s(1, "pr", 0, sb_)
-        offsets_v("o2", NVB)
-        offsets_s("o2", 0, sb_)
+        for k in range(4):
+            unpack(k)
         if r == 0:
-            even(A("cd", 3, 4 * C, 4), 0.0)
-            sa(A("gj", 3, 4 * C, 4), A("iot"), act.Identity, -ZERO - 1000.0, -1.0)
-        key = two_steps("o2", "gj", "cd", "kd", 4, n + "t", [lambda: cp(A("pi"), A("o2"))],
-                        [lambda: ts(A("pj"), A("pi"), 1, alu.logical_shift_right, 1, alu.bitwise_and)] + ([lambda k=k: unpack(k) for k in range(4)] if r == 0 else []))
-        gaps = {
-            -2: [lambda: ts(A("pc", sc_, 24), A("pj", sc_, 24), UP, alu.mult), lambda: ts(A("pq", 0, sc_), A("pj", 0, sc_), -1.0, alu.mult, C - 0.5, alu.add)],
-            -1: [lambda: ts(A("pq", sc_, 24), A("pj", sc_, 24), R2 - 1.0, alu.add)],
-        }
-        if r == 0:
-            gaps[1] = [lambda: quant(A("qv"), A("sv"), A("vb"))]
-            for i in range(4):
-                gaps[2 + i] = border_constants[2 * i:2 * i + 2]
-            sa(A("io4"), A("iot"), act.Identity, 0.0, 4.0)
-        rank_keys(key, n + "C", gaps, NVC)
+            iota(A("io4"), [[4, C]], 0, 0)
+
+        def rounded(a, b):
+            tt(A("tw", a, b), A("pq", a, b), A("acc", a, b), alu.add)
+            ts(A("oc2", a, b), A("tw", a, b), EVEN, alu.add, EVEN, alu.subtract)
 
         def invert(a, b):
             cp(I(A("gi", 0, 2 * C), A("oc2", a, b)), A("io4", 16 * a, 16 * b))
 
-        ranked_s(-1, "pq", 0, 8)
-        ranked_v(-1, "pq", NVC)
-        offsets_s("oc2", 0, 8)
-        offsets_v("oc2", NVC)
-        invert(0, 8)
-        invert(sc_, 24)
-        ranked_s(-1, "pq", 8, sc_)
-        offsets_s("oc2", 8, sc_)
-        invert(8, sc_)
+        def numbered(a, b):
+            last = r == R - 1
+            sa(A("wa", 48 * a + 2, 48 * b, 3), I(A("h1"), A("oc2", a, b)), act.Identity, 0.0 if last else 2.0, 1.0 if last else 3.0)
+
+        ends = rank_keys(key, n + "C", [lambda: ts(A("pq", NVC, 24), A("pj", NVC, 24), -1.0, alu.mult, C - 0.5, alu.add)], [], NVC, CUTS)
+        ts(A("oc2", 0, NVC), ends, -2.0, alu.mult, C - 2.0, alu.add)
+        for (a, b) in zip((NVC,) + CUTS, CUTS + (24,)):
+            rounded(a, b)
+        for (a, b) in PARTS:
+            invert(a, b)
+        numbered(0, CUTS[-1])
+        numbered(CUTS[-1], 24)
+        if r == 0:
+            run(border_constants)
         def renamed(e):
             sc(A("vn", C * e, C * e + C), I(A("wa"), A("nof", 24 * e, 24 * e + 24)))
 
-        if r < R - 1:
-            sa(A("wa", 2, C3, 3), I(A("h1"), A("oc2")), act.Identity, 2.0, 3.0)
-        else:
-            sc(A("wa", 2, C3, 3), I(A("h1"), A("oc2")))
         renamed(0)
         scan(A("lsb"), A("gi", 2 * (C - K), 2 * C, 2), A("md4"), -1.0, alu.max, alu.add)
         scan(A("lsc"), A("gi", 0, 2 * C, 2), A("madd"), -1.0, alu.max, alu.add)
@@ -474,8 +497,9 @@ def rank_program(g, core, T, topo):
         src_q, src_s = bits(A(qt, 128, K + 128), dt.uint8), A(st, 128, K + 128)
         dst_q, dst_s = T[qt][:, 0:K].bitcast(dt.uint8), T[st][:, 0:K]
         arr = T.sem["arr%d" % r]
-        add("G", lambda o=dst_q, i=src_q, s=arr: g.remote_dma(o, i[0], s, T.sem.sent, pid, rid, emask), [], [src_q], "rem")
-        add("G", lambda o=dst_s, i=src_s, s=arr: g.remote_dma(o, i[0], s, T.sem.sent, pid, rid, emask), [], [src_s], "rem")
+        add("G", lambda o=dst_q, i=src_q, s=arr: g.remote_dma(o, i[0], s, T.sem.sent, pid, rid, emask), [], [src_q], REMOTE, "rem")
+        add("G", lambda o=dst_s, i=src_s, s=arr: g.remote_dma(o, i[0], s, T.sem.sent, pid, rid, emask), [], [src_s], REMOTE + (0 if r else FIRST), "rem")
+        sent = len(ops) - 1
         for k in range(4):
             win = A("dh", C * k, C * k + C)
             sc(A("eh", C * k, C * k + C - K), I(win, A("lo", 0, (C - K) // 16)))
@@ -488,46 +512,108 @@ def rank_program(g, core, T, topo):
             else:
                 sa(o, i, act.Relu, 0.0, 0.03125)
 
-        new_names(0)
-        renamed(1)
         quant(A("qz", 128, C), A("sz", 128, C), A("zb", 512, 4 * C))
         for k in range(4):
             mm(4 + k, C - 128, "qw", "sw", 128 * k, "qz", "sz", 128)
         for k in range(4):
-            mm(k, 128, "qe", "se", 128 * k, qt, st, 0, pre=(arr, 2 * neng) if k == 0 else None)
-        if r < R - 1:
-            names_wrapped(0)
-        layer(128, C, 4, 0, "V")
-        layer(128, C, 4, 1, "S")
-        layer(128, C, 4, 2, "V")
-        layer(128, C, 4, 3, "S")
-        for k in range(4):
-            tt(A("zb", k, 4 * K, 4), A("ps", 512 * k, 512 * k + K), A("eh", C * k, C * k + K), alu.add, n + "zr")
-        new_names(1)
-        quant(A("qz", 0, 128), A("sz", 0, 128), A("zb", 0, 512))
-        for k in range(4):
-            mm(k, 128, "qw", "sw", 128 * k, "qz", "sz", 0)
+            layer(128, C, 4, k, LAYER[0][k])
         quant(A("qx", 128, C), A("sx", 128, C), A("xb", 512, 4 * C))
         if r == R - 1:
             dma("Y", T.oc[:, 512:4 * C], bits(A("qx", 128, C), dt.uint8), "outy")
+            quant(A("qv"), A("sv"), A("vb"))
+            mm(4, C - 128, "qv", "sv", 0, "qx", "sx", 128)
+        else:
+            mm(4, C - 128, "qu2", "su2", 0, "qx", "sx", 128)
+            mm(5, C - 128, "qu2", "su2", 0, "qx", "sx", 128)
+            masked(128, C, 4 * 512 - 128)
+            held(128, C)
         for k in range(4):
-            layer(0, 128, 0, k, "V" if k % 2 else "S")
+            mm(k, 128, "qe", "se", 128 * k, qt, st, 0, pre=(arr, 2 * neng, sent))
+        for k in range(4):
+            tt(A("zb", k, 4 * K, 4), A("ps", 512 * k, 512 * k + K), A("eh", C * k, C * k + K), alu.add, n + "zr")
+        quant(A("qz", 0, 128), A("sz", 0, 128), A("zb", 0, 512))
+        for k in range(4):
+            mm(k, 128, "qw", "sw", 128 * k, "qz", "sz", 0)
+        for k in range(4):
+            layer(0, 128, 0, k, LAYER[1][k])
         quant(A("qx", 0, 128), A("sx", 0, 128), A("xb", 0, 512))
+        renamed(1)
+        new_names(0)
         renamed(2)
+        new_names(1)
+        new_names(2)
 
-    mm(4, C, "qv", "sv", 0, "qx", "sx", 0)
-    new_names(2)
+    mm(5, 128, "qv", "sv", 0, "qx", "sx", 0)
+    cp(A("yb", 0, 128), A("ps", 2560, 2560 + 128))
+    dma("S", T.y[:, 0:128], A("yb", 0, 128), "outs")
+    cp(A("yb", 128, C), A("ps", 2048, 2048 + C - 128))
+    dma("Y", T.y[:, 128:C], A("yb", 128, C), "outy")
     dma("Y", T.oc[:, 0:512], bits(A("qx", 0, 128), dt.uint8), "outy")
-    cp(A("yb"), A("ps", 2048, 2048 + C))
     for k in range(4):
-        dma("Y", T.osc[4 * k:4 * k + 4, :], (T.sx[32 * k:32 * k + 4, :], A("sx")[1]), "outy")
-    dma("S", T.on[:], (T.nbv[0:128:16, :], A("nbv")[1]), "outs")
-    dma("S", T.y[:], A("yb"), "outs")
+        dma("Y", T.osc[4 * k:4 * k + 4, :], (T.sx[32 * k:32 * k + 4, :],) + A("sx")[1:], "outy")
+    dma("S", T.on[:], (T.nbv[0:128:16, :],) + A("nbv")[1:], "outs")
 
-    groups = {}
-    for k, o in enumerate(ops):
-        groups.setdefault(o["grp"], []).append(k)
-    seen = {}
+    def members(calls):
+        groups = {}
+        for k, o in enumerate(calls):
+            groups.setdefault(o["grp"], []).append(k)
+        return groups
+
+    def before(calls):
+        seen, deps, follows = {}, [], []
+        for k, o in enumerate(calls):
+            d, f = set(), set()
+            for (lst, writing) in ((o["rd"], False), (o["wr"], True)):
+                for (name, m) in lst:
+                    for (j, m2, w2) in seen.get(name, []):
+                        if m & m2 and (writing or w2 or (name == "ps" and calls[j]["q"] != o["q"])):
+                            (f if o["chain"] and name == "ps" and calls[j]["grp"] == o["grp"] else d).add(j)
+            deps.append(d)
+            follows.append(f)
+            for (name, m) in o["rd"]:
+                seen.setdefault(name, []).append((k, m, False))
+            for (name, m) in o["wr"]:
+                seen[name] = [s for s in seen.get(name, []) if s[1] & ~m] + [(k, m, True)]
+        return deps, follows
+
+    def ordered(calls):
+        groups = members(calls)
+        deps, follows = before(calls)
+        pred, succ = [], [{} for o in calls]
+        for k, o in enumerate(calls):
+            p = {i: WAKE for j in deps[k] for i in groups[calls[j]["grp"]]}
+            p.update({j: 0.0 for j in follows[k]})
+            if o["pre"]:
+                p[o["pre"][2]] = WAKE
+            pred.append(p)
+            for j in p:
+                succ[j][k] = p[j]
+        hold = [ISSUE if o["dma"] or o["grp"] == "rem" else o["us"] for o in calls]
+
+        def laid(order, back):
+            lines, start = {q: [] for q in eng}, {}
+            for k in order:
+                lag = calls[k]["us"] - hold[k]
+                if back:
+                    t = max([start[j] + hold[j] + w + lag for j, w in succ[k].items()] + [lag])
+                else:
+                    t = max([start[j] + calls[j]["us"] + w for j, w in pred[k].items()] + [0.0])
+                line, at = lines[calls[k]["q"]], 0
+                while at < len(line) and line[at][0] < t + hold[k] - min(SLACK, hold[k] / 2):
+                    t = max(t, line[at][1])
+                    at += 1
+                line.insert(at, (t, t + hold[k]))
+                start[k] = t
+            return start
+
+        start = laid(range(len(calls)), False)
+        for turn in range(TURNS):
+            late = laid(sorted(start, key=lambda k: (-start[k] - hold[k], -k)), True)
+            start = laid(sorted(late, key=lambda k: (-late[k] - hold[k], k)), False)
+        return [calls[k] for k in sorted(start, key=lambda k: (start[k], k))]
+
+    ops = ordered(ops)
+    groups = members(ops)
     known = {q: 0 for q in eng}
     snap, waits = [0] * len(ops), [[] for o in ops]
     wanted = set(["outy", "outs"])
@@ -542,23 +628,10 @@ def rank_program(g, core, T, topo):
         for i in groups[gp]:
             known[q] |= snap[i] | 1 << i
 
-    for k, o in enumerate(ops):
-        deps = []
-        for (lst, writing) in ((o["rd"], False), (o["wr"], True)):
-            for (name, m) in lst:
-                for (j, m2, w2) in seen.get(name, []):
-                    if not m & m2:
-                        continue
-                    if writing or w2 or (name == "ps" and ops[j]["q"] != o["q"]):
-                        if not (o["chain"] and name == "ps" and ops[j]["grp"] == o["grp"]):
-                            deps.append(j)
-        for j in sorted(set(deps), reverse=True):
+    for k, d in enumerate(before(ops)[0]):
+        for j in sorted(d, reverse=True):
             need(k, j)
-        snap[k] = known[o["q"]]
-        for (name, m) in o["rd"]:
-            seen.setdefault(name, []).append((k, m, False))
-        for (name, m) in o["wr"]:
-            seen[name] = [s for s in seen.get(name, []) if s[1] & ~m] + [(k, m, True)]
+        snap[k] = known[ops[k]["q"]]
 
     semof, total, last = {}, {}, {}
     for k, o in enumerate(ops):

@@ -1,16 +1,17 @@
 from concourse.mybir import dt, AluOpType, AxisListType, ActivationFunctionType
 
 C, K, R = 384, 96, 3
-MS = 14
-NVB, NVC = 9, 8
+MSR = (15, 15, 15)
+NVB, NVC = 10, 9
 TBV = 14
 NM = 5
 PIECES = ((0, 160), (160, 288), (288, C))
 C3 = 3 * C
 R2 = C // 2
 R1 = C * R2
-V1, TURNS, C1 = 10, 1, C + 1
-LATEB = 23
+V1, TURNS = 11, 1
+WV = 6
+LATEB = 22
 CUTS = (18,)
 PARTS = ((0, 18), (18, 24))
 LAYER = ("VSVS", "SVSV")
@@ -26,7 +27,7 @@ HUGE, CB, BIG = 1e29, 2048.0, 2.0 ** 60
 WID = (384, 320, 256, 192, 128, 128)
 OFF = (0, 384, 704, 960, 1152, 1280)
 CYCLE, FIXED, GATHER, SCATTER, PE = 0.00083, 0.02, 1.56, 3.8, 0.0007
-WAKE, SLACK, ISSUE, REMOTE, FIRST = 0.2, 0.1, 0.1, 2.6, 1.0
+WAKE, SLACK, ISSUE, REMOTE, FIRST = 0.2, 0.1, 0.1, 2.4, 1.0
 F32, BF, I32, U16, Q4, U8 = "float32", "bfloat16", "int32", "uint16", "float8_e4m3fn_x4", "uint8"
 
 
@@ -37,7 +38,7 @@ def _sb(n, d=F32):
 SCRATCH = {
     "xb": _sb(4 * C, BF), "tb": _sb(512, BF), "zb": _sb(4 * C, BF), "ub": _sb(512, BF), "vb": _sb(512, BF),
     "dh": _sb(4 * C), "eh": _sb(4 * C),
-    "nbi": _sb(72, I32), "nbo": _sb(72, U16), "nof": _sb(96, U16), "nx": _sb(24, U16), "nf0": _sb(24), "nf1": _sb(24),
+    "nbi": _sb(216, I32), "nbd": ("dram", [8, C3], I32), "nof": _sb(96, U16), "nx": _sb(24, U16), "nf0": _sb(24), "nf1": _sb(24),
     "nbv": _sb(C3), "vn": _sb(C3), "nsc": _sb(C3),
     "qx": _sb(C, Q4), "sx": _sb(C, U8), "qz": _sb(C, Q4), "sz": _sb(C, U8),
     "qu": _sb(128, Q4), "su": _sb(128, U8), "qu2": _sb(128, Q4), "su2": _sb(128, U8), "qv": _sb(128, Q4), "sv": _sb(128, U8),
@@ -45,13 +46,13 @@ SCRATCH = {
     "one5": _sb(512, BF), "half": _sb(512, BF), "gd": _sb(512, BF), "gd2": _sb(512, BF), "qg": _sb(128, Q4), "sgs": _sb(128, U8),
     "ct": _sb(4 * 1408, BF), "rs": _sb(4 * 1408, BF), "qc": _sb(1408, Q4), "scc": _sb(1408, U8), "csc": _sb(C), "rb": _sb(C), "rst": _sb(640, BF),
     "pmi": _sb(4, I32), "pmj": _sb(6, I32), "pm": _sb(6), "uoi": _sb(8, I32), "uo": _sb(8, U16), "po": _sb(24, U16),
-    "iot": _sb(C), "io3": _sb(C), "io4": _sb(C), "tm": _sb(C), "md": _sb(C), "hm": _sb(C), "hn": _sb(C), "hd": _sb(C),
+    "iot": _sb(24), "io4": _sb(C), "tm": _sb(C), "md": _sb(C), "hm": _sb(C), "hn": _sb(C), "hd": _sb(C),
     "rch": _sb(C, BF), "madd": _sb(C), "mmul": _sb(C), "tm4": _sb(K), "ma4": _sb(K), "mb4": _sb(K), "md4": _sb(K),
     "s16": _sb(96), "cc": _sb(10), "cst": _sb(24), "fl": _sb(96), "fl2": _sb(48), "fl3": _sb(24), "fl4": _sb(24),
     "t1": _sb(C), "t2": _sb(C), "cm": _sb(C), "hs": _sb(C, BF),
     "h1": _sb(4 * C + 8), "wa": _sb(C3 + 8), "wb": _sb(C3 + 8), "gi": _sb(C3), "kc": _sb(C3), "cb": _sb(C3),
     "gj": _sb(4 * C), "kd": _sb(4 * C), "cd": _sb(4 * C), "ksc": _sb(C),
-    "cmp": _sb(10 * C1, BF), "scn": _sb(10 * C1, BF), "low": _sb(NM * C1, BF), "pb": _sb(24), "sg": _sb(18 * C, BF), "jk": _sb(C, BF),
+    "cmp": _sb(10 * C, BF), "scn": _sb(10 * R2, BF), "pb": _sb(24), "rd": _sb(24), "ini": _sb(24, BF), "sg": _sb(18 * C, BF), "jk": _sb(C, BF),
     "col": _sb(4), "acc": _sb(24), "alt": _sb(24), "bas": _sb(24), "pi": _sb(24, I32), "pj": _sb(24, I32),
     "pc": _sb(24), "pq": _sb(24), "pr": _sb(24), "thr": _sb(24), "tw": _sb(24),
     "o1": _sb(24, U16), "o2": _sb(24, U16), "oc2": _sb(24, U16), "lo": _sb(24, U16), "lob": _sb(24, U16),
@@ -62,7 +63,7 @@ for _r in range(R):
     SCRATCH["qt%d" % _r] = _sb(K + 128, Q4)
     SCRATCH["st%d" % _r] = _sb(K + 128, U8)
 
-POOL = {"V": 48, "S": 40, "P": 16, "G": 22, "D": 16}
+POOL = {"V": 48, "S": 40, "P": 16, "G": 26, "D": 16}
 SEMAPHORES = [q + str(i) for q in POOL for i in range(POOL[q])] + ["arr%d" % r for r in range(R)] + ["sent"]
 
 
@@ -132,7 +133,7 @@ def rank_program(g, core, T, topo):
         add("V", lambda: g.vector.tensor_copy(o[0], i[0]), [o], [i], span(o, [i], fast(o, i)), grp)
 
     def scan(o, d0, d1, init, op0, op1, grp=None):
-        add("V", lambda: g.vector.tensor_tensor_scan(o[0], d0[0], d1[0], init, op0, op1), [o], [d0, d1], span(o, [d0], fast(o, d0, d1)), grp)
+        add("V", lambda: g.vector.tensor_tensor_scan(o[0], d0[0], d1[0], ap(init), op0, op1), [o], [d0, d1, init], span(o, [d0], fast(o, d0, d1)), grp)
 
     def fill(o, v, grp=None):
         add("V", lambda: g.vector.memset(o[0], v), [o], [], span(o, [o], fast(o)), grp)
@@ -170,19 +171,37 @@ def rank_program(g, core, T, topo):
         for f in calls:
             f()
 
+    def own_scores(a, b, c0):
+        tt(A("t1", a, b), A("ps", c0 + a, c0 + b), A("hm", a, b), alu.min)
+        scan(A("t2", a, b), A("hd", a, b), A("t1", a, b), 0.0, alu.min, alu.max)
+
+    def early_scores():
+        mm(4, C - 128, "qu2", "su2", 0, "qx", "sx", 128)
+        mm(5, C - 128, "qu2", "su2", 0, "qx", "sx", 128)
+        own_scores(128, C, 4 * 512 - 128)
+
     ones = A("one5", 0, C)
-    CATCH, CAT4, UP, DOWN, PLACED, LANE0, ENDF = (col("cc", c) for c in range(7))
+    CATCH, CAT4, UP, DOWN, PLACED, LANE0, ENDF, BACK = (col("cc", c) for c in range(8))
     RUNS = [[0, 24], [1, 16]]
-    dma("Y", A("xb"), T.x[:], us=2.6)
+    dma("Y", A("xb", 512, 4 * C), T.x[:, 512:4 * C], us=2.0)
+    dma("Y", A("xb", 0, 512), T.x[:, 0:512], us=2.6)
     dma("S", A("ub"), T.u[:])
-    dma("S", A("nbi"), T.nb[:])
+    flat = (T.nbd[:], [("nbd", 1)], [], 72, False)
+    dma("S", flat, T.nb[:])
+    for i in range(16):
+        cut = min(3, 16 - 3 * i % 16)
+        for (e, b) in ((0, cut), (cut, 3)):
+            if b > e:
+                c, p = divmod(3 * i + e, 16)
+                a, w = 72 * e + 2 - c, 72 * (b - e) - 2 + c
+                dma("YS"[i % 2], (T.nbi[i:128:16, a:a + w], [("nbi%d" % i, ((1 << w) - 1) << a)], [], w, False), (T.nbd[:, 72 * p:72 * p + w],) + flat[1:], "nb")
     iota(A("pmi", 0, 2), [[15, 2]], 0, 1, False)
     iota(A("tm"), RUNS, 0, 0)
     iota(A("uoi"), [[16, 8]], 0, 0, False)
     iota(A("pmi", 2, 4), [[12, 2]], 0, 1, False)
     fill(A("one5"), 1.0)
-    fill(A("tb"), 0.0)
-    scan(A("iot"), ones, ones, -1.0, alu.add, alu.mult)
+    sa(A("tb"), A("one5"), act.Identity, 0.0, 0.0)
+    iota(A("iot"), [[1, 24]], 0, 0)
     for k in range(5):
         dma("Y", A("ct", 4 * (OFF[k] + WID[k] - 48), 4 * (OFF[k] + WID[k])), A("tb", 0, 192), "ctz")
     dma("Y", A("ct", 4 * (OFF[5] + 16), 4 * (OFF[5] + 128)), A("tb", 0, 448), "ctz")
@@ -190,9 +209,7 @@ def rank_program(g, core, T, topo):
     dma("Y", A("sw"), T.ws[:], "w", behind=A("xb"))
     dma("Y", A("vb"), T.v[:], behind=A("xb"))
     ts(A("pmj", 0, 2), A("pmi", 0, 2), 15, alu.bitwise_and)
-    sa(A("io3"), A("iot"), act.Identity, 2.0, 3.0)
     cp(A("pm", 0, 2), A("pmj", 0, 2))
-    cp(A("nbo"), A("nbi"))
     ts(A("md"), A("tm"), col("pm", 0), alu.is_equal)
     cp(A("uo"), A("uoi"))
     ts(A("po"), A("iot", 0, 24), 0.0, alu.mult, col("pm", 0), alu.add)
@@ -203,22 +220,21 @@ def rank_program(g, core, T, topo):
     select(A("hd"), A("hn"), RUNS, alu.is_gt, 0, 0, -HUGE)
     select(A("gd"), A("one5"), [[-16, 8], [0, 64]], alu.is_ge, 0, 1)
     select(A("gd2"), A("gd"), [[16, 8], [0, 64]], alu.is_ge, 15, -1)
-    select(A("rch"), ones, RUNS, alu.is_gt, 0, 0)
-    iota(A("rst"), [[0, 640]], 1, 0)
-    for c in (256, 448, 576):
-        iota(col("rst", c), [[0, 1]], 0, 0)
+    sa(A("rch"), A("tm"), act.Sign)
+    iota(A("rs", 2 * OFF[3] - 8, 2 * OFF[3]), [[0, 8]], -256, 0)
     iota(A("h1"), [[1, 2 * C + 4], [0, 2]], 0, 0)
     quant(A("qu"), A("su"), A("ub"))
     ts(LANE0, col("pm", 0), 0.0, alu.is_equal)
     tt(A("s16", 64, 80), A("s16", 0, 16), A("s16", 16, 32), alu.add)
     cp(bits(A("qu2"), dt.uint32), I(bits(A("qu"), dt.uint32), A("uo")), "u2")
     cp(A("su2"), I(A("su"), A("uo")), "u2")
-    sc(A("nbv"), I(A("io3"), A("nbo")))
     sc(A("madd"), I(A("s16", 64, 80), A("po")))
     ts(A("nf1"), A("iot", 0, 24), 16.0, alu.mult, col("pm", 0), alu.add)
     ts(CATCH, LANE0, 2 * CB, alu.mult, -CB, alu.add)
     ts(A("cst"), A("iot", 0, 24), 16.0, alu.mult, col("pm", 0), alu.subtract)
-    quant(A("qx"), A("sx"), A("xb"))
+    quant(A("qx", 128, C), A("sx", 128, C), A("xb", 512, 4 * C))
+    early_scores()
+    quant(A("qx", 0, 128), A("sx", 0, 128), A("xb", 0, 512))
     ts(A("nof", 72, 96), A("nf1"), 3.0, alu.mult, 2.0, alu.add)
     ts(A("cst"), A("cst"), 17.0 + C, alu.add)
 
@@ -233,6 +249,7 @@ def rank_program(g, core, T, topo):
         lambda: fill(A("wa", C3, C3 + 8), BASE),
         lambda: fill(A("wb", C3, C3 + 8), PLACE1),
         lambda: ts(col("s16", 95), col("s16", 95), ENDF, alu.mult),
+        lambda: ts(BACK, LANE0, BIG, alu.mult, 1 / BIG, alu.max),
         lambda: sa(DOWN, UP, act.Identity, 0.0, -1.0),
         lambda: sa(PLACED, UP, act.Identity, 0.0, -ZERO - 500.0),
     ]
@@ -256,8 +273,9 @@ def rank_program(g, core, T, topo):
     def names_wrapped(e):
         scan(A("nsc", C * e, C * e + C), A("nbv", e, C3, 3), A("madd"), -1.0, alu.max, alu.add)
 
-    def names_pick(e):
-        ts(A("nof", 24 * e, 24 * e + 24), A("nsc", C * e + 15, C * e + C, 16), CATCH, alu.add)
+    def first_names():
+        i = A("nbi", 2, 216, 3)
+        ts(A("nof", 0, 72), (i[0], [("nbi%d" % p, i[1][0][1]) for p in range(16)]) + i[2:], 3.0, alu.mult, 2.0, alu.add)
 
     def step(win, first, lifts, scale, got, ctl, out, w, tag, after):
         ts(A(got, 0, w * C, w), I(A(win), A("nx")), *first)
@@ -273,22 +291,22 @@ def rank_program(g, core, T, topo):
         step("wa", (float(C), alu.mult, FLOOR1, alu.max), (0.0, -LIFT), float(C), "gi", "wa", "wb", 3, tag + "a", {-1: gaps[0], 2: [half_digit] + gaps[1]})
         catch = lambda a, b: scan(A("ksc", a, b), A(out, w * a + w - 1, w * b, w), A("mmul", a, b), 0.0, alu.add, alu.mult)
         step("wb", (FLOOR2, alu.max, float(R2), alu.mult), (-LIFT2, -LIFT2), float(R2), got, ctl, out, w, tag + "b",
-             {-1: gaps[2], 1: [lambda: catch(0, 16 * V1)], 2: gaps[3] + [lambda: catch(16 * V1, C)]})
+             {-1: gaps[2], 1: [lambda: catch(0, 160)], 2: [lambda: catch(160, 192)] + gaps[3] + [lambda: catch(192, C)]})
         return A(out, w - 1, w * C, w)
 
     def rank_keys(key, tag, first, between, nv, cuts):
         for m in range(nv, 24):
             sa(A("sg", C * (m - nv), C * (m - nv) + C), key, act.Sign, col("ksc", 16 * m + 15), DOWN, col("acc", m), tag + "s%d" % sum(m >= c for c in cuts))
-        tt(A("thr", 0, nv), A("ksc", 15, 16 * nv, 16), A("pc", 0, nv), alu.subtract)
-        ts(A("cmp", 0, C1 * nv, C1), A("pj", 0, nv), -1.0, alu.mult)
+        cp(A("pc"), A("pj"))
+        ts(A("thr", 0, nv), A("ksc", 15, 16 * nv, 16), BACK, alu.mult)
+        sa(A("ini", 0, nv), A("pc", 0, nv), act.Identity, -float(R2), -1.0)
         for i in range(nv):
-            ts(A("cmp", C1 * i + 1, C1 * i + C1), key, UP, alu.mult, col("thr", i), alu.is_gt, tag + "c%d" % (i // NM))
+            ts(A("cmp", C * i, C * i + C), key, col("pc", i), alu.add, col("thr", i), alu.is_gt, tag + "c%d" % (i // NM))
             run(first[i:i + 1])
         run(between)
-        for i in range(0, nv, NM):
-            w = C1 * min(NM, nv - i)
-            scan(A("scn", C1 * i, C1 * i + w), A("low", 0, w), A("cmp", C1 * i, C1 * i + w), -float(R2), alu.min, alu.add, tag + "n")
-        return A("scn", C, C1 * nv, C1)
+        for i in range(nv):
+            scan(A("scn", R2 * i, R2 * i + R2), A("cmp", C * i, C * i + R2), A("cmp", C * i + R2, C * i + C), col("ini", i), alu.add, alu.add, tag + "n")
+        return A("scn", R2 - 1, R2 * nv, R2)
 
     ROOT, RT3 = col("col", 0), col("col", 1)
 
@@ -297,35 +315,19 @@ def rank_program(g, core, T, topo):
         return A("ct", 4 * (OFF[k] + a) + t, 4 * (OFF[k] + (b or 16 * m)), 4)
 
     for r in range(R):
-        n = "r%d" % r
+        n, MS = "r%d" % r, MSR[r]
         qt, st = "qt%d" % r, "st%d" % r
-        for (bank, w) in (((1, 128), (0, C)) if r else ((0, C), (1, C))):
-            mm(bank, w, "qu2", "su2", 0, "qx", "sx", 0)
+        mm(1, 128, "qu2", "su2", 0, "qx", "sx", 0)
+        mm(0, C, "qu2", "su2", 0, "qx", "sx", 0)
 
         def parts(b, late, early):
-            return [(128, b, 512 * early - 128), (0, 128, 512 * late)] if r and b > 128 else [(0, b, 512 * late)]
-
-        sv = A("ps", 0, C)
+            return [(128, b, 512 * early - 128), (0, 128, 512 * late)]
 
         def unpack(k):
             sc(A("dh", C * k, C * k + C), A("ps", 512 * (4 + k), 512 * (4 + k) + C))
 
-        def masked(a, b, c0):
-            tt(A("t1", a, b), A("ps", c0 + a, c0 + b), A("hm", a, b), alu.min)
-
-        def held(a, b):
-            scan(A("t2", a, b), A("hd", a, b), A("t1", a, b), 0.0, alu.min, alu.max)
-
-        if r:
-            masked(0, 128, 0)
-            scan(A("cm"), sv, ones, -HUGE, alu.max, alu.mult)
-            held(0, 128)
-        else:
-            masked(256, C, 0)
-            masked(0, 256, 0)
-            held(256, C)
-            held(0, 256)
-            scan(A("cm"), sv, ones, -HUGE, alu.max, alu.mult)
+        own_scores(0, 128, 0)
+        scan(A("cm"), A("ps", 0, C), ones, -HUGE, alu.max, alu.mult)
 
         def runs(k):
             return range(21 - 4 * k, min(25 - 4 * k, 24))
@@ -362,17 +364,16 @@ def rank_program(g, core, T, topo):
             for k in range(4):
                 mm(4 + k, C, "qe", "se", 128 * k, "qx", "sx", 0)
         small = {
-            12: [lambda e=e: names_wrapped(e) for e in range(3)],
+            12: [lambda e=e: names_wrapped(e) for e in range(3 if r else 0)],
             11: [lambda: scan(A("hs"), A("rch"), slot(24), 0.0, alu.mult, alu.add)],
-            10: [lambda: ts(A("nof", 0, 72), A("nsc", 15, C3, 16), CATCH, alu.add)],
-            9: [lambda: cp(A("nf0"), A("nof", 0, 24))],
+            10: [lambda: ts(A("nof", 0, 72), A("nsc", 15, C3, 16), CATCH, alu.add)] if r else [first_names],
+            9: [lambda: ts(A("nf0"), A("nof", 0, 24), -2.0, alu.add, 1 / 3, alu.mult)],
             8: [lambda: tt(A("bas"), A("cst"), A("hs", 15, C, 16), alu.subtract)],
-            6: [lambda: ts(A("fl"), A("nof"), RT3, alu.is_equal, float(C3), alu.mult)],
+            6: [lambda: ts(A("fl"), A("nof"), RT3, alu.is_equal, float(C), alu.mult)],
             5: [lambda: tt(A("fl2"), A("fl", 0, 48), A("fl", 48, 96), alu.max)],
             4: [lambda: tt(A("fl3"), A("fl2", 0, 24), A("fl2", 24, 48), alu.max)],
-            3: [lambda: ts(A("fl4"), A("fl3"), 0.0, alu.is_gt, -float(C), alu.mult)],
-            2: [lambda: tt(A("nf1"), A("nf0"), A("fl3"), alu.max)],
-            1: [lambda: tt(A("bas"), A("bas"), A("fl4"), alu.add)],
+            2: [lambda: tt(A("nf1"), A("nf0"), A("fl", 72, 96), alu.max)],
+            1: [lambda: tt(A("bas"), A("bas"), A("fl3"), alu.subtract)],
         }
         if r == 0:
             small[7] = [lambda: quant(A("qg"), A("sgs"), A("gd2"))]
@@ -380,7 +381,7 @@ def rank_program(g, core, T, topo):
             ts(slot(m), A("ps", 0, 16 * m), col("t2", 16 * m + 15), alu.is_lt, grp=n + "c%d" % ((m - 1) // 4))
             run(small.get(m, []))
         summed(3)
-        cp(A("nx"), A("nf1"))
+        ts(A("nx"), A("nf1"), 3.0, alu.mult, 2.0, alu.add)
         summed(4)
         summed(0)
         for k in (0, 3, 4, 5):
@@ -389,7 +390,7 @@ def rank_program(g, core, T, topo):
         def rows(t):
             k0 = 2 if 13 + t < MS else 3
             a, b = OFF[k0], OFF[5] + 64
-            scan(A("rs", 4 * a + t, 4 * b, 4), A("rst", a - OFF[2], 640), A("ct", 4 * a + t, 4 * b, 4), 0.0, alu.mult, alu.add, n + "rs")
+            scan(A("rs", 2 * a + t, 2 * b, 4), A("ct", 4 * a + t, 4 * b, 8), A("ct", 4 * a + 4 + t, 4 * b, 8), -256.0, alu.add, alu.add, n + "rs")
 
         if r == 0:
             run(key_constants)
@@ -398,11 +399,10 @@ def rank_program(g, core, T, topo):
         summed(1)
         mm(2, WID[1], "qg", "sgs", 0, "qc", "scc", OFF[1], False, False, n + "cs")
         for k in (3, 4, 5):
-            e = 4 * (OFF[k] + (WID[k] if k < 5 else 64))
-            tt(A("bas", 21 - 4 * k, 25 - 4 * k), A("bas", 21 - 4 * k, 25 - 4 * k), A("rs", e - 4, e), alu.subtract, n + "bs")
-        if MS > 13:
-            e = 4 * OFF[3] - 4
-            tt(A("bas", 13, MS), A("bas", 13, MS), A("rs", e, e + MS - 13), alu.subtract, n + "bs")
+            e = 2 * (OFF[k] + (WID[k] if k < 5 else 64))
+            tt(A("rd", 21 - 4 * k, 25 - 4 * k), A("rs", e - 4, e), A("rs", 2 * OFF[k] - 4, 2 * OFF[k]), alu.subtract, n + "rd")
+        ts(A("rd", 13, MS), A("rs", 2 * OFF[3] - 4, 2 * OFF[3] - 4 + MS - 13), 256.0, alu.add, grp=n + "rd")
+        tt(A("bas", 1, MS), A("bas", 1, MS), A("rd", 1, MS), alu.subtract, n + "bs")
         tt(A("bas", MS, 24), A("bas", MS, 24), A("alt", MS, 24), alu.subtract, n + "bs")
         summed(2)
         mm(2, WID[2], "qg", "sgs", 0, "qc", "scc", OFF[2], False, True, n + "cs")
@@ -417,45 +417,40 @@ def rank_program(g, core, T, topo):
             even(A("cb", 0, C3, 3), -LIFT2)
             even(A("cb", 1, C3, 3), 0.0)
             sc(A("mmul"), I(A("s16", 80, 96), A("po")))
-            iota(A("low"), [[0, NM], [1, C1]], -R2, 0)
             fill(A("half"), 0.5)
             for b in range(4):
-                select(A("eb", 512 * b, 512 * b + 512), A("half"), [[-1, 512]], alu.is_equal, b, 4, 0.0, "eb")
+                select(A("eb", 512 * b, 512 * b + 512), A("half"), [[-1, 512]], alu.is_equal, b, 4)
             iota(A("tm4"), [[0, 24], [1, 4]], 0, 0)
         key = two_steps("gi", "cb", "kc", 3, n + "s", ([], [], [], [
             lambda: scan(A("csc", 0, R2), A("ps", 1024, 1024 + R2), A("madd", 0, R2), -1.0, alu.max, alu.add),
             lambda: scan(A("csc", R2, C), A("ps", 1024 + R2, 1024 + C), A("madd", R2, C), -1.0, alu.max, alu.add),
             lambda: tt(A("pi"), A("csc", 15, C, 16), A("bas"), alu.add),
-            lambda: ts(A("pj"), A("pi"), 1, alu.bitwise_and),
-            lambda: ts(A("pc"), A("pj"), UP, alu.mult)]))
+            lambda: ts(A("pj"), A("pi"), 1, alu.bitwise_and)]))
         own = A("ksc", 15, C, 16)
         ends = rank_keys(key, n + "B", [
-            lambda: ts(A("pb", NVB, 24), A("pj", NVB, 24), C - 1.0, alu.add),
+            lambda: sa(A("pb", NVB, 24), A("pc", NVB, 24), act.Identity, C - 1.0),
             lambda: ts(A("fl4"), own, PLACED, alu.is_le, 2.0 * C, alu.mult),
-            lambda: ts(A("fl3"), own, PLACED, alu.is_gt, float(C3), alu.mult),
-            lambda: tt(A("pr", NVB, 24), A("pb", NVB, 24), A("fl4", NVB, 24), alu.add),
-            lambda: tt(A("nf1"), A("nf0"), A("fl3"), alu.max),
-            lambda: cp(A("nx"), A("nf1"))], [], NVB, range(LATEB, 24))
+            lambda: tt(A("pr", NVB, 24), A("pb", NVB, 24), A("fl4", NVB, 24), alu.add)], [], NVB, range(LATEB, 24))
         tt(A("tw", NVB, LATEB), A("pr", NVB, LATEB), A("acc", NVB, LATEB), alu.subtract)
         cp(A("o2", NVB, LATEB), A("tw", NVB, LATEB))
         ts(A("pb", 0, NVB), A("ksc", 15, 16 * NVB, 16), PLACED, alu.is_le, float(C), alu.mult)
         tt(A("tw", 0, NVB), A("pb", 0, NVB), ends, alu.add)
         ts(A("o2", 0, NVB), A("tw", 0, NVB), 2.0, alu.mult, float(C), alu.add)
+        ts(A("wa", 2, 48 * WV, 3), I(A("h1"), A("o2", 0, WV)), -1.0, alu.mult, BASE, alu.add)
         for m in range(LATEB, 24):
-            ts(col("o2", m), col("acc", m), -1.0, alu.mult, col("pr", m), alu.add, n + "o2")
-        ts(A("wa", 2, C3 // 2, 3), I(A("h1"), A("o2", 0, 12)), -1.0, alu.mult, BASE, alu.add)
-        sa(A("wa", C3 // 2 + 2, C3, 3), I(A("h1"), A("o2", 12, 24)), act.Identity, BASE, -1.0)
+            ts(col("o2", m), col("acc", m), -1.0, alu.mult, col("pr", m), alu.add)
+        ts(A("wa", 48 * LATEB + 2, C3, 3), I(A("h1"), A("o2", LATEB, 24)), -1.0, alu.mult, BASE, alu.add)
+        sa(A("wa", 48 * WV + 2, 48 * LATEB, 3), I(A("h1"), A("o2", WV, LATEB)), act.Identity, BASE, -1.0)
         if r == 0:
             for t, v in ((0, -LIFT2), (1, 0.0), (3, 0.0)):
                 even(A("cd", t, 4 * C, 4), v)
             iota(A("gj", 3, 4 * C, 4), [[-1, C]], -int(ZERO) - 1000, 0)
         key = two_steps("gj", "cd", "kd", 4, n + "t", ([], [], [], [
             lambda: cp(A("pi"), A("o2")),
-            lambda: ts(A("pj"), A("pi"), 1, alu.logical_shift_right, 1, alu.bitwise_and),
-            lambda: ts(A("pc"), A("pj"), UP, alu.mult)]))
+            lambda: ts(A("pj"), A("pi"), 1, alu.logical_shift_right, 1, alu.bitwise_and)]))
         if r == 0:
-            quant(A("qe"), A("se"), A("eb"))
             for k in range(4):
+                quant(A("qe", 128 * k, 128 * k + 128), A("se", 128 * k, 128 * k + 128), A("eb", 512 * k, 512 * k + 512))
                 mm(4 + k, C, "qe", "se", 128 * k, "qx", "sx", 0)
         for k in range(4):
             unpack(k)
@@ -473,7 +468,7 @@ def rank_program(g, core, T, topo):
             last = r == R - 1
             sa(A("wa", 48 * a + 2, 48 * b, 3), I(A("h1"), A("oc2", a, b)), act.Identity, 0.0 if last else 2.0, 1.0 if last else 3.0)
 
-        ends = rank_keys(key, n + "C", [lambda: ts(A("pq", NVC, 24), A("pj", NVC, 24), -1.0, alu.mult, C - 0.5, alu.add)], [], NVC, CUTS)
+        ends = rank_keys(key, n + "C", [lambda: sa(A("pq", NVC, 24), A("pc", NVC, 24), act.Identity, C - 0.5, -1.0)], [], NVC, CUTS)
         ts(A("oc2", 0, NVC), ends, -2.0, alu.mult, C - 2.0, alu.add)
         for (a, b) in zip((NVC,) + CUTS, CUTS + (24,)):
             rounded(a, b)
@@ -487,19 +482,22 @@ def rank_program(g, core, T, topo):
             sc(A("vn", C * e, C * e + C), I(A("wa"), A("nof", 24 * e, 24 * e + 24)))
 
         renamed(0)
-        scan(A("lsb"), A("gi", 2 * (C - K), 2 * C, 2), A("md4"), -1.0, alu.max, alu.add)
-        scan(A("lsc"), A("gi", 0, 2 * C, 2), A("madd"), -1.0, alu.max, alu.add)
-        ts(A("lob"), A("lsb", 3, K, 4), CAT4, alu.add)
-        ts(A("lo"), A("lsc", 15, C, 16), CATCH, alu.add, 0.25, alu.mult)
+        for (a, b) in ((0, C - K), (C - K, C)):
+            scan(A("lsc", a, b), A("gi", 2 * a, 2 * b, 2), A("madd", a, b), -1.0, alu.max, alu.add)
+            if a == 0:
+                scan(A("lsb"), A("gi", 2 * (C - K), 2 * C, 2), A("md4"), -1.0, alu.max, alu.add)
+            ts(A("lo", a // 16, b // 16), A("lsc", a + 15, b, 16), CATCH, alu.add, 0.25, alu.mult)
+            if a == 0:
+                ts(A("lob"), A("lsb", 3, K, 4), CAT4, alu.add)
         cp(A("tb", 128, 128 + 16 * TBV), I(A("xb"), A("lob", 0, TBV)))
         sc(A("tb", 128 + 16 * TBV, 512), I(A("xb"), A("lob", TBV, 24)))
         quant(A(qt, K, K + 128), A(st, K, K + 128), A("tb"))
         src_q, src_s = bits(A(qt, 128, K + 128), dt.uint8), A(st, 128, K + 128)
         dst_q, dst_s = T[qt][:, 0:K].bitcast(dt.uint8), T[st][:, 0:K]
         arr = T.sem["arr%d" % r]
-        add("G", lambda o=dst_q, i=src_q, s=arr: g.remote_dma(o, i[0], s, T.sem.sent, pid, rid, emask), [], [src_q], REMOTE, "rem")
+        add("G", lambda o=dst_q, i=src_q, s=arr: g.remote_dma(o, i[0], s, T.sem.sent, pid, rid, emask), [], [src_q], REMOTE + 2 * ISSUE + (0 if r else FIRST), "rem")
         add("G", lambda o=dst_s, i=src_s, s=arr: g.remote_dma(o, i[0], s, T.sem.sent, pid, rid, emask), [], [src_s], REMOTE + (0 if r else FIRST), "rem")
-        sent = len(ops) - 1
+        sent = (len(ops) - 2, len(ops) - 1)
         for k in range(4):
             win = A("dh", C * k, C * k + C)
             sc(A("eh", C * k, C * k + C - K), I(win, A("lo", 0, (C - K) // 16)))
@@ -523,10 +521,7 @@ def rank_program(g, core, T, topo):
             quant(A("qv"), A("sv"), A("vb"))
             mm(4, C - 128, "qv", "sv", 0, "qx", "sx", 128)
         else:
-            mm(4, C - 128, "qu2", "su2", 0, "qx", "sx", 128)
-            mm(5, C - 128, "qu2", "su2", 0, "qx", "sx", 128)
-            masked(128, C, 4 * 512 - 128)
-            held(128, C)
+            early_scores()
         for k in range(4):
             mm(k, 128, "qe", "se", 128 * k, qt, st, 0, pre=(arr, 2 * neng, sent))
         for k in range(4):
@@ -550,7 +545,7 @@ def rank_program(g, core, T, topo):
     dma("Y", T.y[:, 128:C], A("yb", 128, C), "outy")
     dma("Y", T.oc[:, 0:512], bits(A("qx", 0, 128), dt.uint8), "outy")
     for k in range(4):
-        dma("Y", T.osc[4 * k:4 * k + 4, :], (T.sx[32 * k:32 * k + 4, :],) + A("sx")[1:], "outy")
+        dma("YS"[k % 2], T.osc[4 * k:4 * k + 4, :], (T.sx[32 * k:32 * k + 4, :],) + A("sx")[1:], ("outy", "outs")[k % 2])
     dma("S", T.on[:], (T.nbv[0:128:16, :],) + A("nbv")[1:], "outs")
 
     def members(calls):
@@ -584,7 +579,7 @@ def rank_program(g, core, T, topo):
             p = {i: WAKE for j in deps[k] for i in groups[calls[j]["grp"]]}
             p.update({j: 0.0 for j in follows[k]})
             if o["pre"]:
-                p[o["pre"][2]] = WAKE
+                p.update({j: WAKE for j in o["pre"][2]})
             pred.append(p)
             for j in p:
                 succ[j][k] = p[j]

from concourse.mybir import dt, AluOpType, AxisListType, ActivationFunctionType

C, K, R = 384, 96, 3
MSR = (15, 15, 15)
NVB, NVC = 10, 9
TBV = 14
NM = 5
PIECES = ((0, 160), (160, 288), (288, C))
C3 = 3 * C
R2 = C // 2
R1 = C * R2
V1, TURNS = 11, 1
WV = 6
LATEB = 22
CUTS = (18,)
PARTS = ((0, 18), (18, 24))
LAYER = ("VSVS", "SVSV")
BASE, LIFT = 2048.0, 2.0 ** 19 + 2.0 ** 15
FLOOR1 = C * BASE - (C + 1) * C
PLACE1 = (C + 1) * BASE - LIFT
FLOOR2 = PLACE1 - (C + 2) * C
LIFT2 = (FLOOR2 + C) * R2
HALF = 0.5 - 1 / BASE
ZERO = float(R2 * R1 - R2 * R2 - R2 - R2 // 2)
EVEN = 1.5 * 2 ** 24
HUGE, CB, BIG = 1e29, 2048.0, 2.0 ** 60
WID = (384, 320, 256, 192, 128, 128)
OFF = (0, 384, 704, 960, 1152, 1280)
CYCLE, FIXED, GATHER, SCATTER, PE = 0.00083, 0.02, 1.56, 3.8, 0.0007
WAKE, SLACK, ISSUE, REMOTE, FIRST = 0.2, 0.1, 0.1, 2.4, 1.0
F32, BF, I32, U16, Q4, U8 = "float32", "bfloat16", "int32", "uint16", "float8_e4m3fn_x4", "uint8"


def _sb(n, d=F32):
    return ("sbuf", [128, n], d)


SCRATCH = {
    "xb": _sb(4 * C, BF), "tb": _sb(512, BF), "zb": _sb(4 * C, BF), "ub": _sb(512, BF), "vb": _sb(512, BF),
    "dh": _sb(4 * C), "eh": _sb(4 * C),
    "nbi": _sb(216, I32), "nbd": ("dram", [8, C3], I32), "nof": _sb(96, U16), "nx": _sb(24, U16), "nf0": _sb(24), "nf1": _sb(24),
    "nbv": _sb(C3), "vn": _sb(C3), "nsc": _sb(C3),
    "qx": _sb(C, Q4), "sx": _sb(C, U8), "qz": _sb(C, Q4), "sz": _sb(C, U8),
    "qu": _sb(128, Q4), "su": _sb(128, U8), "qu2": _sb(128, Q4), "su2": _sb(128, U8), "qv": _sb(128, Q4), "sv": _sb(128, U8),
    "qw": _sb(512, Q4), "sw": _sb(512, U8), "qe": _sb(512, Q4), "se": _sb(512, U8), "eb": _sb(2048, BF),
    "one5": _sb(512, BF), "half": _sb(512, BF), "gd": _sb(512, BF), "gd2": _sb(512, BF), "qg": _sb(128, Q4), "sgs": _sb(128, U8),
    "ct": _sb(4 * 1408, BF), "rs": _sb(4 * 1408, BF), "qc": _sb(1408, Q4), "scc": _sb(1408, U8), "csc": _sb(C), "rb": _sb(C), "rst": _sb(640, BF),
    "pmi": _sb(4, I32), "pmj": _sb(6, I32), "pm": _sb(6), "uoi": _sb(8, I32), "uo": _sb(8, U16), "po": _sb(24, U16),
    "iot": _sb(24), "io4": _sb(C), "tm": _sb(C), "md": _sb(C), "hm": _sb(C), "hn": _sb(C), "hd": _sb(C),
    "rch": _sb(C, BF), "madd": _sb(C), "mmul": _sb(C), "tm4": _sb(K), "ma4": _sb(K), "mb4": _sb(K), "md4": _sb(K),
    "s16": _sb(96), "cc": _sb(10), "cst": _sb(24), "fl": _sb(96), "fl2": _sb(48), "fl3": _sb(24), "fl4": _sb(24),
    "t1": _sb(C), "t2": _sb(C), "cm": _sb(C), "hs": _sb(C, BF),
    "h1": _sb(4 * C + 8), "wa": _sb(C3 + 8), "wb": _sb(C3 + 8), "gi": _sb(C3), "kc": _sb(C3), "cb": _sb(C3),
    "gj": _sb(4 * C), "kd": _sb(4 * C), "cd": _sb(4 * C), "ksc": _sb(C),
    "cmp": _sb(10 * C, BF), "scn": _sb(10 * R2, BF), "pb": _sb(24), "rd": _sb(24), "ini": _sb(24, BF), "sg": _sb(18 * C, BF), "jk": _sb(C, BF),
    "col": _sb(4), "acc": _sb(24), "alt": _sb(24), "bas": _sb(24), "pi": _sb(24, I32), "pj": _sb(24, I32),
    "pc": _sb(24), "pq": _sb(24), "pr": _sb(24), "thr": _sb(24), "tw": _sb(24),
    "o1": _sb(24, U16), "o2": _sb(24, U16), "oc2": _sb(24, U16), "lo": _sb(24, U16), "lob": _sb(24, U16),
    "lsc": _sb(C), "lsb": _sb(K), "yb": _sb(C),
    "ps": ("psum", [128, 4096], F32),
}
for _r in range(R):
    SCRATCH["qt%d" % _r] = _sb(K + 128, Q4)
    SCRATCH["st%d" % _r] = _sb(K + 128, U8)

POOL = {"V": 48, "S": 40, "P": 16, "G": 26, "D": 16}
SEMAPHORES = [q + str(i) for q in POOL for i in range(POOL[q])] + ["arr%d" % r for r in range(R)] + ["sent"]


def rank_program(g, core, T, topo):
    rank = T.rank_of(core)
    if rank is None:
        return
    nxt = T.cores[(rank + 1) % len(T.cores)]
    rid, pid = topo.addr(nxt)[0:2]
    emask = topo.mask(core, nxt)
    neng = len(topo.engines(core, nxt))
    alu, act = AluOpType, ActivationFunctionType
    eng = {"V": g.vector, "S": g.scalar, "P": g.tensor, "G": g, "Y": g.sync}
    ops = []

    def A(name, a=0, b=None, s=1):
        if b is None:
            b = SCRATCH[name][1][1]
        n, narrow = len(range(a, b, s)), SCRATCH[name][2] in (BF, U16)
        if name == "ps":
            return (T[name][:, a:b], [("ps", 1 << (a // 512))], [], n, narrow)
        m = ((1 << (b - a)) - 1) << a if s == 1 else sum(1 << c for c in range(a, b, s))
        return (T[name][:, a:b] if s == 1 else T[name][:, a:b:s], [(name, m)], [], n, narrow)

    def col(name, c):
        return A(name, c, c + 1)

    def I(win, off):
        return (win[0].indirect(off[0]), win[1], off[1], 16 * off[3], False)

    def bits(a, d):
        return (a[0].bitcast(d),) + a[1:]

    def ap(x):
        return x[0] if isinstance(x, tuple) else x

    def add(q, fn, outs, ins, us, grp=None, dma=False, pre=None, chain=False):
        rd, wr = [], []
        for x in ins:
            if isinstance(x, tuple):
                rd += x[1] + x[2]
        for x in outs:
            wr += x[1]
            rd += x[2]
        ops.append({"q": q, "fn": fn, "rd": rd, "wr": wr, "grp": grp if grp else "#%d" % len(ops), "dma": dma, "pre": pre, "chain": chain, "us": us})

    def span(o, ins, per=1.0):
        if o[2]:
            return 0.05 + CYCLE * SCATTER * o[3]
        if ins[0][2]:
            return 0.06 + CYCLE * GATHER * o[3]
        return FIXED + CYCLE * max(64, per * o[3])

    def fast(*xs):
        return 0.5 if all(x[4] for x in xs) else 1.0

    def ts(o, i, s1, op0, s2=None, op1=None, grp=None):
        if op1 is None:
            add("V", lambda: g.vector.tensor_scalar(o[0], i[0], ap(s1), None, op0), [o], [i, s1], span(o, [i], fast(o, i)), grp)
        else:
            add("V", lambda: g.vector.tensor_scalar(o[0], i[0], ap(s1), ap(s2), op0, op1), [o], [i, s1, s2], span(o, [i], fast(o, i)), grp)

    def tt(o, a, b, op, grp=None):
        add("V", lambda: g.vector.tensor_tensor(o[0], a[0], b[0], op), [o], [a, b], span(o, [a], 1.0 if "ps" in (a[1][0][0], b[1][0][0]) else 2.0), grp)

    def cp(o, i, grp=None):
        add("V", lambda: g.vector.tensor_copy(o[0], i[0]), [o], [i], span(o, [i], fast(o, i)), grp)

    def scan(o, d0, d1, init, op0, op1, grp=None):
        add("V", lambda: g.vector.tensor_tensor_scan(o[0], d0[0], d1[0], ap(init), op0, op1), [o], [d0, d1, init], span(o, [d0], fast(o, d0, d1)), grp)

    def fill(o, v, grp=None):
        add("V", lambda: g.vector.memset(o[0], v), [o], [], span(o, [o], fast(o)), grp)

    def quant(q, s, i):
        add("V", lambda: g.vector.quantize_mx(q[0], s[0], i[0]), [q, s], [i], 0.012 + 0.00022 * i[3])

    def sa(o, i, f, bias=0.0, scale=1.0, acc=None, grp=None):
        if acc is None:
            add("S", lambda: g.scalar.activation(o[0], i[0], f, bias=ap(bias), scale=ap(scale)), [o], [i, bias, scale], span(o, [i]), grp)
        else:
            add("S", lambda: g.scalar.activation(o[0], i[0], f, bias=ap(bias), scale=ap(scale), accum_out=acc[0]), [o, acc], [i, bias, scale], span(o, [i]) + 0.02, grp)

    def sc(o, i, grp=None):
        add("S", lambda: g.scalar.activation(o[0], i[0], act.Copy), [o], [i], span(o, [i]), grp)

    def mm(bank, n, wq, ws, c0, xq, xs, x0, start=True, stop=True, grp=None, pre=None):
        o, a, b = A("ps", 512 * bank, 512 * bank + n), A(wq, c0, c0 + 128), A(ws, c0, c0 + 128)
        c, d = A(xq, x0, x0 + n), A(xs, x0, x0 + n)
        add("P", lambda: g.tensor.matmul_mx(o[0], a[0], b[0], c[0], d[0], start, stop), [o], [a, b, c, d], PE * (n + 16), grp, pre=pre, chain=not start)

    def dma(q, o, i, grp=None, us=1.5, behind=None):
        add(q, lambda: eng[q].dma_start(ap(o), ap(i)), [o] if isinstance(o, tuple) else [], [i, behind], us, grp, dma=True)

    def iota(o, pat, base, cm, flag=True):
        if flag:
            add("G", lambda: g.iota(o[0], pat, base, cm, allow_small_or_imprecise_dtypes=True), [o], [], 0.13 + 2 * CYCLE * o[3])
        else:
            add("G", lambda: g.iota(o[0], pat, base, cm), [o], [], 0.13 + 2 * CYCLE * o[3])

    def select(o, i, pat, op, base, cm, other=0.0, grp=None):
        add("G", lambda: g.affine_select(o[0], i[0], pat, op, other, base, cm), [o], [i], 0.17 + 2 * CYCLE * o[3], grp)

    def run(calls):
        for f in calls:
            f()

    def own_scores(a, b, c0):
        tt(A("t1", a, b), A("ps", c0 + a, c0 + b), A("hm", a, b), alu.min)
        scan(A("t2", a, b), A("hd", a, b), A("t1", a, b), 0.0, alu.min, alu.max)

    def early_scores():
        mm(4, C - 128, "qu2", "su2", 0, "qx", "sx", 128)
        mm(5, C - 128, "qu2", "su2", 0, "qx", "sx", 128)
        own_scores(128, C, 4 * 512 - 128)

    ones = A("one5", 0, C)
    CATCH, CAT4, UP, DOWN, PLACED, LANE0, ENDF, BACK = (col("cc", c) for c in range(8))
    RUNS = [[0, 24], [1, 16]]
    dma("Y", A("xb", 512, 4 * C), T.x[:, 512:4 * C], us=2.0)
    dma("Y", A("xb", 0, 512), T.x[:, 0:512], us=2.6)
    dma("S", A("ub"), T.u[:])
    flat = (T.nbd[:], [("nbd", 1)], [], 72, False)
    dma("S", flat, T.nb[:])
    for i in range(16):
        cut = min(3, 16 - 3 * i % 16)
        for (e, b) in ((0, cut), (cut, 3)):
            if b > e:
                c, p = divmod(3 * i + e, 16)
                a, w = 72 * e + 2 - c, 72 * (b - e) - 2 + c
                dma("YS"[i % 2], (T.nbi[i:128:16, a:a + w], [("nbi%d" % i, ((1 << w) - 1) << a)], [], w, False), (T.nbd[:, 72 * p:72 * p + w],) + flat[1:], "nb")
    iota(A("pmi", 0, 2), [[15, 2]], 0, 1, False)
    iota(A("tm"), RUNS, 0, 0)
    iota(A("uoi"), [[16, 8]], 0, 0, False)
    iota(A("pmi", 2, 4), [[12, 2]], 0, 1, False)
    fill(A("one5"), 1.0)
    sa(A("tb"), A("one5"), act.Identity, 0.0, 0.0)
    iota(A("iot"), [[1, 24]], 0, 0)
    for k in range(5):
        dma("Y", A("ct", 4 * (OFF[k] + WID[k] - 48), 4 * (OFF[k] + WID[k])), A("tb", 0, 192), "ctz")
    dma("Y", A("ct", 4 * (OFF[5] + 16), 4 * (OFF[5] + 128)), A("tb", 0, 448), "ctz")
    dma("Y", bits(A("qw"), dt.uint8), T.wc[:], "w", behind=A("xb"))
    dma("Y", A("sw"), T.ws[:], "w", behind=A("xb"))
    dma("Y", A("vb"), T.v[:], behind=A("xb"))
    ts(A("pmj", 0, 2), A("pmi", 0, 2), 15, alu.bitwise_and)
    cp(A("pm", 0, 2), A("pmj", 0, 2))
    ts(A("md"), A("tm"), col("pm", 0), alu.is_equal)
    cp(A("uo"), A("uoi"))
    ts(A("po"), A("iot", 0, 24), 0.0, alu.mult, col("pm", 0), alu.add)
    ts(A("s16", 0, 16), A("tm", 0, 16), col("pm", 1), alu.is_equal, -2 * CB, alu.mult)
    ts(A("s16", 16, 32), A("tm", 0, 16), col("pm", 0), alu.is_equal, CB, alu.mult)
    sa(A("hn"), A("md"), act.Identity, HUGE, -2 * HUGE)
    sa(A("hm"), A("md"), act.Identity, -HUGE, 2 * HUGE)
    select(A("hd"), A("hn"), RUNS, alu.is_gt, 0, 0, -HUGE)
    select(A("gd"), A("one5"), [[-16, 8], [0, 64]], alu.is_ge, 0, 1)
    select(A("gd2"), A("gd"), [[16, 8], [0, 64]], alu.is_ge, 15, -1)
    sa(A("rch"), A("tm"), act.Sign)
    iota(A("rs", 2 * OFF[3] - 8, 2 * OFF[3]), [[0, 8]], -256, 0)
    iota(A("h1"), [[1, 2 * C + 4], [0, 2]], 0, 0)
    quant(A("qu"), A("su"), A("ub"))
    ts(LANE0, col("pm", 0), 0.0, alu.is_equal)
    tt(A("s16", 64, 80), A("s16", 0, 16), A("s16", 16, 32), alu.add)
    cp(bits(A("qu2"), dt.uint32), I(bits(A("qu"), dt.uint32), A("uo")), "u2")
    cp(A("su2"), I(A("su"), A("uo")), "u2")
    sc(A("madd"), I(A("s16", 64, 80), A("po")))
    ts(A("nf1"), A("iot", 0, 24), 16.0, alu.mult, col("pm", 0), alu.add)
    ts(CATCH, LANE0, 2 * CB, alu.mult, -CB, alu.add)
    ts(A("cst"), A("iot", 0, 24), 16.0, alu.mult, col("pm", 0), alu.subtract)
    quant(A("qx", 128, C), A("sx", 128, C), A("xb", 512, 4 * C))
    early_scores()
    quant(A("qx", 0, 128), A("sx", 0, 128), A("xb", 0, 512))
    ts(A("nof", 72, 96), A("nf1"), 3.0, alu.mult, 2.0, alu.add)
    ts(A("cst"), A("cst"), 17.0 + C, alu.add)

    key_constants = [
        lambda: ts(UP, LANE0, -BIG, alu.mult, BIG, alu.add),
        lambda: ts(ENDF, LANE0, -1.0, alu.mult, 1.0, alu.add),
        lambda: ts(A("s16", 32, 48), A("tm", 0, 16), col("pm", 0), alu.is_gt),
        lambda: ts(A("s16", 48, 64), A("md", 0, 16), BIG, alu.mult),
        lambda: ts(UP, UP, 1 / BIG, alu.max),
        lambda: ts(ENDF, ENDF, 1 / (BIG * BIG), alu.max),
        lambda: tt(A("s16", 80, 96), A("s16", 32, 48), A("s16", 48, 64), alu.add),
        lambda: fill(A("wa", C3, C3 + 8), BASE),
        lambda: fill(A("wb", C3, C3 + 8), PLACE1),
        lambda: ts(col("s16", 95), col("s16", 95), ENDF, alu.mult),
        lambda: ts(BACK, LANE0, BIG, alu.mult, 1 / BIG, alu.max),
        lambda: sa(DOWN, UP, act.Identity, 0.0, -1.0),
        lambda: sa(PLACED, UP, act.Identity, 0.0, -ZERO - 500.0),
    ]
    border_constants = [
        lambda: ts(A("pmj", 2, 4), A("pmi", 2, 4), 15, alu.bitwise_and, 2, alu.logical_shift_right),
        lambda: ts(A("pmj", 4, 5), A("pmi", 0, 1), 3, alu.bitwise_and),
        lambda: cp(A("pm", 2, 5), A("pmj", 2, 5)),
        lambda: ts(A("ma4"), A("tm4"), col("pm", 3), alu.is_equal, -2 * CB, alu.mult),
        lambda: ts(A("mb4"), A("tm4"), col("pm", 2), alu.is_equal, CB, alu.mult),
        lambda: ts(CAT4, col("pm", 2), 0.0, alu.is_equal, 2 * CB, alu.mult),
        lambda: tt(A("md4"), A("ma4"), A("mb4"), alu.add),
        lambda: ts(CAT4, CAT4, col("pm", 4), alu.add, -CB, alu.add),
    ]

    def even(o, v):
        iota(o, [[0, C]], int(v), 0)

    def new_names(e):
        sc(A("nbv", e, C3, 3), I(A("vn", C * e, C * e + C), A("lo")))

    def names_wrapped(e):
        scan(A("nsc", C * e, C * e + C), A("nbv", e, C3, 3), A("madd"), -1.0, alu.max, alu.add)

    def first_names():
        i = A("nbi", 2, 216, 3)
        ts(A("nof", 0, 72), (i[0], [("nbi%d" % p, i[1][0][1]) for p in range(16)]) + i[2:], 3.0, alu.mult, 2.0, alu.add)

    def step(win, first, lifts, scale, got, ctl, out, w, tag, after):
        ts(A(got, 0, w * C, w), I(A(win), A("nx")), *first)
        run(after.get(-1, []))
        for p, (a, b) in enumerate(PIECES):
            for e in (1, 2):
                sa(A(got, w * a + e, w * b, w), I(A(win), A("nof", 24 * e + a // 16, 24 * e + b // 16)), act.Identity, lifts[e - 1], scale, grp=tag + str(a))
            scan(A(out, w * a, w * b), A(got, w * a, w * b), A(ctl, w * a, w * b), 0.0, alu.max, alu.add)
            run(after.get(p, []))

    def two_steps(got, ctl, out, w, tag, gaps):
        half_digit = lambda: sa(A(ctl, 2, w * C, w), A("wa", 2, C3, 3), act.Identity, -ZERO - BASE * HALF, HALF)
        step("wa", (float(C), alu.mult, FLOOR1, alu.max), (0.0, -LIFT), float(C), "gi", "wa", "wb", 3, tag + "a", {-1: gaps[0], 2: [half_digit] + gaps[1]})
        catch = lambda a, b: scan(A("ksc", a, b), A(out, w * a + w - 1, w * b, w), A("mmul", a, b), 0.0, alu.add, alu.mult)
        step("wb", (FLOOR2, alu.max, float(R2), alu.mult), (-LIFT2, -LIFT2), float(R2), got, ctl, out, w, tag + "b",
             {-1: gaps[2], 1: [lambda: catch(0, 160)], 2: [lambda: catch(160, 192)] + gaps[3] + [lambda: catch(192, C)]})
        return A(out, w - 1, w * C, w)

    def rank_keys(key, tag, first, between, nv, cuts):
        for m in range(nv, 24):
            sa(A("sg", C * (m - nv), C * (m - nv) + C), key, act.Sign, col("ksc", 16 * m + 15), DOWN, col("acc", m), tag + "s%d" % sum(m >= c for c in cuts))
        cp(A("pc"), A("pj"))
        ts(A("thr", 0, nv), A("ksc", 15, 16 * nv, 16), BACK, alu.mult)
        sa(A("ini", 0, nv), A("pc", 0, nv), act.Identity, -float(R2), -1.0)
        for i in range(nv):
            ts(A("cmp", C * i, C * i + C), key, col("pc", i), alu.add, col("thr", i), alu.is_gt, tag + "c%d" % (i // NM))
            run(first[i:i + 1])
        run(between)
        for i in range(nv):
            scan(A("scn", R2 * i, R2 * i + R2), A("cmp", C * i, C * i + R2), A("cmp", C * i + R2, C * i + C), col("ini", i), alu.add, alu.add, tag + "n")
        return A("scn", R2 - 1, R2 * nv, R2)

    ROOT, RT3 = col("col", 0), col("col", 1)

    def slot(m, a=0, b=None):
        k, t = 5 - (m - 1) // 4, (m - 1) % 4
        return A("ct", 4 * (OFF[k] + a) + t, 4 * (OFF[k] + (b or 16 * m)), 4)

    for r in range(R):
        n, MS = "r%d" % r, MSR[r]
        qt, st = "qt%d" % r, "st%d" % r
        mm(1, 128, "qu2", "su2", 0, "qx", "sx", 0)
        mm(0, C, "qu2", "su2", 0, "qx", "sx", 0)

        def parts(b, late, early):
            return [(128, b, 512 * early - 128), (0, 128, 512 * late)]

        def unpack(k):
            sc(A("dh", C * k, C * k + C), A("ps", 512 * (4 + k), 512 * (4 + k) + C))

        own_scores(0, 128, 0)
        scan(A("cm"), A("ps", 0, C), ones, -HUGE, alu.max, alu.mult)

        def runs(k):
            return range(21 - 4 * k, min(25 - 4 * k, 24))

        def signs(k, which):
            for m in runs(k):
                if m >= MS:
                    for (a, b, c0) in parts(16 * m, 1, 5)[which]:
                        sa(A("sg", C * (m - 8) + a, C * (m - 8) + b), A("ps", c0 + a, c0 + b), act.Sign, col("t2", 16 * m + 15), -1.0, grp=n + "p%d%d" % (k, a))

        def lower(k):
            for m in runs(k):
                if m >= MS:
                    sa(slot(m), A("sg", C * (m - 8), C * (m - 8) + 16 * m), act.Relu, 0.0, 1.0, col("alt", m), n + "q%d" % k)

        def summed(k):
            w = WID[k] if k < 4 else (256 if r == 0 else 192)
            quant(A("qc", OFF[k], OFF[k] + w), A("scc", OFF[k], OFF[k] + w), A("ct", 4 * OFF[k], 4 * (OFF[k] + w)))

        late = slice(-1, None)
        for k in range(3):
            signs(k, slice(0, -1))
        signs(0, late)
        sa(A("jk"), A("cm"), act.Sign, col("cm", C - 1), -1.0, ROOT)
        signs(1, late)
        sa(RT3, ROOT, act.Identity, 2.0, 3.0)
        lower(0)
        signs(2, late)
        lower(1)
        lower(2)
        for (a, b, c0) in parts(C, 0, 4):
            tt(slot(24, a, b), A("ps", c0 + a, c0 + b), A("t2", a, b), alu.is_le)
        if r:
            for k in range(4):
                mm(4 + k, C, "qe", "se", 128 * k, "qx", "sx", 0)
        small = {
            12: [lambda e=e: names_wrapped(e) for e in range(3 if r else 0)],
            11: [lambda: scan(A("hs"), A("rch"), slot(24), 0.0, alu.mult, alu.add)],
            10: [lambda: ts(A("nof", 0, 72), A("nsc", 15, C3, 16), CATCH, alu.add)] if r else [first_names],
            9: [lambda: ts(A("nf0"), A("nof", 0, 24), -2.0, alu.add, 1 / 3, alu.mult)],
            8: [lambda: tt(A("bas"), A("cst"), A("hs", 15, C, 16), alu.subtract)],
            6: [lambda: ts(A("fl"), A("nof"), RT3, alu.is_equal, float(C), alu.mult)],
            5: [lambda: tt(A("fl2"), A("fl", 0, 48), A("fl", 48, 96), alu.max)],
            4: [lambda: tt(A("fl3"), A("fl2", 0, 24), A("fl2", 24, 48), alu.max)],
            2: [lambda: tt(A("nf1"), A("nf0"), A("fl", 72, 96), alu.max)],
            1: [lambda: tt(A("bas"), A("bas"), A("fl3"), alu.subtract)],
        }
        if r == 0:
            small[7] = [lambda: quant(A("qg"), A("sgs"), A("gd2"))]
        for m in range(MS - 1, 0, -1):
            ts(slot(m), A("ps", 0, 16 * m), col("t2", 16 * m + 15), alu.is_lt, grp=n + "c%d" % ((m - 1) // 4))
            run(small.get(m, []))
        summed(3)
        ts(A("nx"), A("nf1"), 3.0, alu.mult, 2.0, alu.add)
        summed(4)
        summed(0)
        for k in (0, 3, 4, 5):
            mm(2, WID[k], "qg", "sgs", 0, "qc", "scc", OFF[k], k == 0, False, n + "cs")

        def rows(t):
            k0 = 2 if 13 + t < MS else 3
            a, b = OFF[k0], OFF[5] + 64
            scan(A("rs", 2 * a + t, 2 * b, 4), A("ct", 4 * a + t, 4 * b, 8), A("ct", 4 * a + 4 + t, 4 * b, 8), -256.0, alu.add, alu.add, n + "rs")

        if r == 0:
            run(key_constants)
        for t in range(4):
            rows(t)
        summed(1)
        mm(2, WID[1], "qg", "sgs", 0, "qc", "scc", OFF[1], False, False, n + "cs")
        for k in (3, 4, 5):
            e = 2 * (OFF[k] + (WID[k] if k < 5 else 64))
            tt(A("rd", 21 - 4 * k, 25 - 4 * k), A("rs", e - 4, e), A("rs", 2 * OFF[k] - 4, 2 * OFF[k]), alu.subtract, n + "rd")
        ts(A("rd", 13, MS), A("rs", 2 * OFF[3] - 4, 2 * OFF[3] - 4 + MS - 13), 256.0, alu.add, grp=n + "rd")
        tt(A("bas", 1, MS), A("bas", 1, MS), A("rd", 1, MS), alu.subtract, n + "bs")
        tt(A("bas", MS, 24), A("bas", MS, 24), A("alt", MS, 24), alu.subtract, n + "bs")
        summed(2)
        mm(2, WID[2], "qg", "sgs", 0, "qc", "scc", OFF[2], False, True, n + "cs")
        ts(A("o1"), A("bas"), 2.0, alu.mult)
        if r == 0:
            even(A("wa", 0, C3, 3), 0.0)
            even(A("wa", 1, C3, 3), -LIFT)
        ts(A("rb", 0, R2), I(A("h1"), A("o1", 0, 12)), -1.0, alu.mult, BASE + 2, alu.add)
        sa(A("rb", R2, C), I(A("h1"), A("o1", 12, 24)), act.Identity, BASE + 2, -1.0)
        tt(A("wa", 2, C3, 3), A("rb"), A("ps", 1024, 1024 + C), alu.subtract)
        if r == 0:
            even(A("cb", 0, C3, 3), -LIFT2)
            even(A("cb", 1, C3, 3), 0.0)
            sc(A("mmul"), I(A("s16", 80, 96), A("po")))
            fill(A("half"), 0.5)
            for b in range(4):
                select(A("eb", 512 * b, 512 * b + 512), A("half"), [[-1, 512]], alu.is_equal, b, 4)
            iota(A("tm4"), [[0, 24], [1, 4]], 0, 0)
        key = two_steps("gi", "cb", "kc", 3, n + "s", ([], [], [], [
            lambda: scan(A("csc", 0, R2), A("ps", 1024, 1024 + R2), A("madd", 0, R2), -1.0, alu.max, alu.add),
            lambda: scan(A("csc", R2, C), A("ps", 1024 + R2, 1024 + C), A("madd", R2, C), -1.0, alu.max, alu.add),
            lambda: tt(A("pi"), A("csc", 15, C, 16), A("bas"), alu.add),
            lambda: ts(A("pj"), A("pi"), 1, alu.bitwise_and)]))
        own = A("ksc", 15, C, 16)
        ends = rank_keys(key, n + "B", [
            lambda: sa(A("pb", NVB, 24), A("pc", NVB, 24), act.Identity, C - 1.0),
            lambda: ts(A("fl4"), own, PLACED, alu.is_le, 2.0 * C, alu.mult),
            lambda: tt(A("pr", NVB, 24), A("pb", NVB, 24), A("fl4", NVB, 24), alu.add)], [], NVB, range(LATEB, 24))
        tt(A("tw", NVB, LATEB), A("pr", NVB, LATEB), A("acc", NVB, LATEB), alu.subtract)
        cp(A("o2", NVB, LATEB), A("tw", NVB, LATEB))
        ts(A("pb", 0, NVB), A("ksc", 15, 16 * NVB, 16), PLACED, alu.is_le, float(C), alu.mult)
        tt(A("tw", 0, NVB), A("pb", 0, NVB), ends, alu.add)
        ts(A("o2", 0, NVB), A("tw", 0, NVB), 2.0, alu.mult, float(C), alu.add)
        ts(A("wa", 2, 48 * WV, 3), I(A("h1"), A("o2", 0, WV)), -1.0, alu.mult, BASE, alu.add)
        for m in range(LATEB, 24):
            ts(col("o2", m), col("acc", m), -1.0, alu.mult, col("pr", m), alu.add)
        ts(A("wa", 48 * LATEB + 2, C3, 3), I(A("h1"), A("o2", LATEB, 24)), -1.0, alu.mult, BASE, alu.add)
        sa(A("wa", 48 * WV + 2, 48 * LATEB, 3), I(A("h1"), A("o2", WV, LATEB)), act.Identity, BASE, -1.0)
        if r == 0:
            for t, v in ((0, -LIFT2), (1, 0.0), (3, 0.0)):
                even(A("cd", t, 4 * C, 4), v)
            iota(A("gj", 3, 4 * C, 4), [[-1, C]], -int(ZERO) - 1000, 0)
        key = two_steps("gj", "cd", "kd", 4, n + "t", ([], [], [], [
            lambda: cp(A("pi"), A("o2")),
            lambda: ts(A("pj"), A("pi"), 1, alu.logical_shift_right, 1, alu.bitwise_and)]))
        if r == 0:
            for k in range(4):
                quant(A("qe", 128 * k, 128 * k + 128), A("se", 128 * k, 128 * k + 128), A("eb", 512 * k, 512 * k + 512))
                mm(4 + k, C, "qe", "se", 128 * k, "qx", "sx", 0)
        for k in range(4):
            unpack(k)
        if r == 0:
            iota(A("io4"), [[4, C]], 0, 0)

        def rounded(a, b):
            tt(A("tw", a, b), A("pq", a, b), A("acc", a, b), alu.add)
            ts(A("oc2", a, b), A("tw", a, b), EVEN, alu.add, EVEN, alu.subtract)

        def invert(a, b):
            cp(I(A("gi", 0, 2 * C), A("oc2", a, b)), A("io4", 16 * a, 16 * b))

        def numbered(a, b):
            last = r == R - 1
            sa(A("wa", 48 * a + 2, 48 * b, 3), I(A("h1"), A("oc2", a, b)), act.Identity, 0.0 if last else 2.0, 1.0 if last else 3.0)

        ends = rank_keys(key, n + "C", [lambda: sa(A("pq", NVC, 24), A("pc", NVC, 24), act.Identity, C - 0.5, -1.0)], [], NVC, CUTS)
        ts(A("oc2", 0, NVC), ends, -2.0, alu.mult, C - 2.0, alu.add)
        for (a, b) in zip((NVC,) + CUTS, CUTS + (24,)):
            rounded(a, b)
        for (a, b) in PARTS:
            invert(a, b)
        numbered(0, CUTS[-1])
        numbered(CUTS[-1], 24)
        if r == 0:
            run(border_constants)
        def renamed(e):
            sc(A("vn", C * e, C * e + C), I(A("wa"), A("nof", 24 * e, 24 * e + 24)))

        renamed(0)
        for (a, b) in ((0, C - K), (C - K, C)):
            scan(A("lsc", a, b), A("gi", 2 * a, 2 * b, 2), A("madd", a, b), -1.0, alu.max, alu.add)
            if a == 0:
                scan(A("lsb"), A("gi", 2 * (C - K), 2 * C, 2), A("md4"), -1.0, alu.max, alu.add)
            ts(A("lo", a // 16, b // 16), A("lsc", a + 15, b, 16), CATCH, alu.add, 0.25, alu.mult)
            if a == 0:
                ts(A("lob"), A("lsb", 3, K, 4), CAT4, alu.add)
        cp(A("tb", 128, 128 + 16 * TBV), I(A("xb"), A("lob", 0, TBV)))
        sc(A("tb", 128 + 16 * TBV, 512), I(A("xb"), A("lob", TBV, 24)))
        quant(A(qt, K, K + 128), A(st, K, K + 128), A("tb"))
        src_q, src_s = bits(A(qt, 128, K + 128), dt.uint8), A(st, 128, K + 128)
        dst_q, dst_s = T[qt][:, 0:K].bitcast(dt.uint8), T[st][:, 0:K]
        arr = T.sem["arr%d" % r]
        add("G", lambda o=dst_q, i=src_q, s=arr: g.remote_dma(o, i[0], s, T.sem.sent, pid, rid, emask), [], [src_q], REMOTE + 2 * ISSUE + (0 if r else FIRST), "rem")
        add("G", lambda o=dst_s, i=src_s, s=arr: g.remote_dma(o, i[0], s, T.sem.sent, pid, rid, emask), [], [src_s], REMOTE + (0 if r else FIRST), "rem")
        sent = (len(ops) - 2, len(ops) - 1)
        for k in range(4):
            win = A("dh", C * k, C * k + C)
            sc(A("eh", C * k, C * k + C - K), I(win, A("lo", 0, (C - K) // 16)))
            tt(A("zb", 4 * K + k, 4 * C, 4), I(win, A("lo", K // 16, 24)), A("eh", C * k, C * k + C - K), alu.add, n + "zl")

        def layer(a, b, bank, k, on):
            o, i = A("xb", 4 * a + k, 4 * b, 4), A("ps", 512 * (bank + k), 512 * (bank + k) + b - a)
            if on == "V":
                ts(o, i, 0.0, alu.max, 0.03125, alu.mult)
            else:
                sa(o, i, act.Relu, 0.0, 0.03125)

        quant(A("qz", 128, C), A("sz", 128, C), A("zb", 512, 4 * C))
        for k in range(4):
            mm(4 + k, C - 128, "qw", "sw", 128 * k, "qz", "sz", 128)
        for k in range(4):
            layer(128, C, 4, k, LAYER[0][k])
        quant(A("qx", 128, C), A("sx", 128, C), A("xb", 512, 4 * C))
        if r == R - 1:
            dma("Y", T.oc[:, 512:4 * C], bits(A("qx", 128, C), dt.uint8), "outy")
            quant(A("qv"), A("sv"), A("vb"))
            mm(4, C - 128, "qv", "sv", 0, "qx", "sx", 128)
        else:
            early_scores()
        for k in range(4):
            mm(k, 128, "qe", "se", 128 * k, qt, st, 0, pre=(arr, 2 * neng, sent))
        for k in range(4):
            tt(A("zb", k, 4 * K, 4), A("ps", 512 * k, 512 * k + K), A("eh", C * k, C * k + K), alu.add, n + "zr")
        quant(A("qz", 0, 128), A("sz", 0, 128), A("zb", 0, 512))
        for k in range(4):
            mm(k, 128, "qw", "sw", 128 * k, "qz", "sz", 0)
        for k in range(4):
            layer(0, 128, 0, k, LAYER[1][k])
        quant(A("qx", 0, 128), A("sx", 0, 128), A("xb", 0, 512))
        renamed(1)
        new_names(0)
        renamed(2)
        new_names(1)
        new_names(2)

    mm(5, 128, "qv", "sv", 0, "qx", "sx", 0)
    cp(A("yb", 0, 128), A("ps", 2560, 2560 + 128))
    dma("S", T.y[:, 0:128], A("yb", 0, 128), "outs")
    cp(A("yb", 128, C), A("ps", 2048, 2048 + C - 128))
    dma("Y", T.y[:, 128:C], A("yb", 128, C), "outy")
    dma("Y", T.oc[:, 0:512], bits(A("qx", 0, 128), dt.uint8), "outy")
    for k in range(4):
        dma("YS"[k % 2], T.osc[4 * k:4 * k + 4, :], (T.sx[32 * k:32 * k + 4, :],) + A("sx")[1:], ("outy", "outs")[k % 2])
    dma("S", T.on[:], (T.nbv[0:128:16, :],) + A("nbv")[1:], "outs")

    def members(calls):
        groups = {}
        for k, o in enumerate(calls):
            groups.setdefault(o["grp"], []).append(k)
        return groups

    def before(calls):
        seen, deps, follows = {}, [], []
        for k, o in enumerate(calls):
            d, f = set(), set()
            for (lst, writing) in ((o["rd"], False), (o["wr"], True)):
                for (name, m) in lst:
                    for (j, m2, w2) in seen.get(name, []):
                        if m & m2 and (writing or w2 or (name == "ps" and calls[j]["q"] != o["q"])):
                            (f if o["chain"] and name == "ps" and calls[j]["grp"] == o["grp"] else d).add(j)
            deps.append(d)
            follows.append(f)
            for (name, m) in o["rd"]:
                seen.setdefault(name, []).append((k, m, False))
            for (name, m) in o["wr"]:
                seen[name] = [s for s in seen.get(name, []) if s[1] & ~m] + [(k, m, True)]
        return deps, follows

    def ordered(calls):
        groups = members(calls)
        deps, follows = before(calls)
        pred, succ = [], [{} for o in calls]
        for k, o in enumerate(calls):
            p = {i: WAKE for j in deps[k] for i in groups[calls[j]["grp"]]}
            p.update({j: 0.0 for j in follows[k]})
            if o["pre"]:
                p.update({j: WAKE for j in o["pre"][2]})
            pred.append(p)
            for j in p:
                succ[j][k] = p[j]
        hold = [ISSUE if o["dma"] or o["grp"] == "rem" else o["us"] for o in calls]

        def laid(order, back):
            lines, start = {q: [] for q in eng}, {}
            for k in order:
                lag = calls[k]["us"] - hold[k]
                if back:
                    t = max([start[j] + hold[j] + w + lag for j, w in succ[k].items()] + [lag])
                else:
                    t = max([start[j] + calls[j]["us"] + w for j, w in pred[k].items()] + [0.0])
                line, at = lines[calls[k]["q"]], 0
                while at < len(line) and line[at][0] < t + hold[k] - min(SLACK, hold[k] / 2):
                    t = max(t, line[at][1])
                    at += 1
                line.insert(at, (t, t + hold[k]))
                start[k] = t
            return start

        start = laid(range(len(calls)), False)
        for turn in range(TURNS):
            late = laid(sorted(start, key=lambda k: (-start[k] - hold[k], -k)), True)
            start = laid(sorted(late, key=lambda k: (-late[k] - hold[k], k)), False)
        return [calls[k] for k in sorted(start, key=lambda k: (start[k], k))]

    ops = ordered(ops)
    groups = members(ops)
    known = {q: 0 for q in eng}
    snap, waits = [0] * len(ops), [[] for o in ops]
    wanted = set(["outy", "outs"])

    def need(k, j):
        q, gp = ops[k]["q"], ops[j]["grp"]
        if known[q] >> j & 1:
            return
        assert gp != ops[k]["grp"] and groups[gp][-1] < k, (k, j, gp)
        waits[k].append(gp)
        wanted.add(gp)
        for i in groups[gp]:
            known[q] |= snap[i] | 1 << i

    for k, d in enumerate(before(ops)[0]):
        for j in sorted(d, reverse=True):
            need(k, j)
        snap[k] = known[ops[k]["q"]]

    semof, total, last = {}, {}, {}
    for k, o in enumerate(ops):
        gp = o["grp"]
        if gp not in wanted or gp in semof:
            continue
        pool = "D" if o["dma"] else o["q"]
        pick = None
        for i in range(POOL[pool]):
            s = pool + str(i)
            if s not in last or (not o["dma"] and all(snap[k] >> j & 1 for j in groups[last[s]])):
                pick = s
                break
        assert pick is not None, (pool, k)
        last[pick] = gp
        total[pick] = total.get(pick, 0) + (16 if o["dma"] else 1) * len(groups[gp])
        semof[gp] = (pick, total[pick])

    for k, o in enumerate(ops):
        e = eng[o["q"]]
        for gp in waits[k]:
            e.wait_ge(T.sem[semof[gp][0]], semof[gp][1])
        if o["pre"]:
            e.wait_ge(o["pre"][0], o["pre"][1])
        inst = o["fn"]()
        if o["grp"] in semof:
            inst.then_inc(T.sem[semof[o["grp"]][0]], 16 if o["dma"] else 1)
    g.wait_ge(T.sem.sent, 2 * R * neng)
    g.sync.wait_ge(T.sem[semof["outy"][0]], semof["outy"][1])
    g.scalar.wait_ge(T.sem[semof["outs"][0]], semof["outs"][1])
